import numpy as np
import ml_dtypes


def mxq(x, axis, fmt="e4m3"):
    dtype, down = {"e4m3": (ml_dtypes.float8_e4m3fn, 7), "e5m2": (ml_dtypes.float8_e5m2, 14)}[fmt]
    v = np.moveaxis(np.asarray(x, np.float32).astype(ml_dtypes.bfloat16).astype(np.float64), axis, -1)
    blocks = v.reshape(v.shape[:-1] + (-1, 32))
    amax = np.abs(blocks).max(-1, keepdims=True)
    byte = np.maximum(np.where(amax > 0, np.frexp(amax)[1] - 1 + 127, 0) - down, 1)
    scale = np.exp2(byte - 127.0)
    codes = (blocks / scale).astype(np.float32).astype(dtype).astype(np.float64)
    return np.moveaxis((codes * scale).reshape(v.shape), -1, axis)


WIDE = False


def mx_kscale(k):
    if not WIDE:
        return np.ones(k)
    levels = np.array([10, -10, 5, -5, 0])
    if k % 512:
        return np.exp2(np.random.permutation(np.resize(levels, k // 32))).repeat(32)
    a = np.empty((k // 512, 16))
    for p in range(k // 512):
        a[p, :8] = np.random.permutation(np.resize(levels, 8))
        for g in range(8):
            far = levels[np.abs(levels - a[p, g]) >= 10]
            a[p, g + 8] = far[np.random.randint(len(far))]
    return np.exp2(a.ravel()).repeat(32)


def f64(x):
    return np.asarray(x).astype(np.float64)


def striped(idx):
    return np.tile(idx.reshape(-1, 16).T, (8, 1)).astype(np.uint16)


def unstriped(offs):
    return offs[:16].T.reshape(-1).astype(np.int64)


def striped8(idx):
    return np.concatenate([x.reshape(-1, 16).T for x in idx]).astype(np.uint16)


def runs(offs, k):
    lists = np.stack([offs[16 * r : 16 * r + 16].T.reshape(-1) for r in range(8)]).astype(np.int64)
    return lists[np.arange(k) % 512 // 64]


def pack_weight(w):
    k, n = w.shape
    w = f64(np.asarray(w, np.float32).astype(ml_dtypes.bfloat16)).reshape(k // 32, 32, n)
    amax = np.abs(w).max(1)
    byte = np.clip(np.where(amax > 0, np.frexp(amax)[1] - 1 + 127 - 7, 1), 1, 254)
    scaled = (w * np.exp2(127.0 - byte)[:, None, :]).reshape(k, n).astype(np.float32)
    words = np.ascontiguousarray(scaled.reshape(k // 512, 128, 4, n).transpose(0, 1, 3, 2)).astype(ml_dtypes.float8_e4m3fn).view(np.uint8)
    return words, np.ascontiguousarray(byte.astype(np.uint8).reshape(k // 512, 16, n))


def unpack_weight(words, scales):
    g, p, n, _ = words.shape
    vals = np.ascontiguousarray(words).view(ml_dtypes.float8_e4m3fn).astype(np.float64) * np.repeat(np.exp2(scales.astype(np.float64) - 127.0), 8, axis=1)[..., None]
    return vals.transpose(0, 1, 3, 2).reshape(g * 512, n)


def relu(v):
    return np.maximum(v, 0.0)


K, T, S, N, U, H = 512, 2048, 512, 512, 1024, 512


def setup_inputs():
    n = np.random.standard_normal
    s = mx_kscale(K)[:, None]
    u = mx_kscale(H)
    packed_xT = pack_weight(n((K, T)) * s)
    return {
        "x_words": packed_xT[0],
        "x_scales": packed_xT[1],
        "w1": (n((K, H)) / np.sqrt(K) / s * u).astype(np.float32),
        "b1": (0.5 * n((H, 1)) * u[:, None]).astype(np.float32),
        "w2": (n((H, N)) / np.sqrt(H) / u[:, None]).astype(np.float32),
        "b2": (0.5 * n((N, 1))).astype(np.float32),
        "offs": striped(np.random.permutation(T)[:S]),
        "held": striped8(np.stack([np.random.permutation(U)[:S] for _ in range(8)])),
    }


def reference(x_words, x_scales, w1, b1, w2, b2, offs, held):
    xq = unpack_weight(x_words, x_scales)[:, unstriped(offs)]
    y = relu((mxq(f64(w1), 0, "e4m3").T @ xq) + f64(b1))
    z = np.zeros((H, U))
    z[np.arange(H)[:, None], runs(held, H)] = y
    return (mxq(f64(w2), 0, "e4m3").T @ mxq(z, 0, "e4m3")) + f64(b2)

@@ -1,0 +1,158 @@
+from contextlib import ExitStack
+
+import concourse.mybir as mybir
+
+K, T, S, N, U, H = 512, 2048, 512, 512, 1024, 512
+FLOPS = 2 * K * H * S + 2 * H * N * U
+
+F32 = mybir.dt.float32
+BF16 = mybir.dt.bfloat16
+I32 = mybir.dt.int32
+U32 = mybir.dt.uint32
+U16 = mybir.dt.uint16
+U8 = mybir.dt.uint8
+FP8X4 = mybir.dt.float8_e4m3fn_x4
+ACT = mybir.ActivationFunctionType
+
+P = 128
+PACK = 4
+HALF = S // 2
+CHUNKS = (128, 128, 256, 256, 256)
+SHARED_CHUNKS = 2
+
+
+def dealt(grouped):
+    return grouped.rearrange("p (t m j) -> p m j t", t=PACK, j=PACK)
+
+
+def by_column(raw):
+    return raw.rearrange("p j (m t) -> p m j t", t=PACK)
+
+
+def tile_picked_sae8_relu_p_kernel(
+    tc, x_words, x_scales, w1, b1, w2, b2, offs, held, out
+):
+    nc = tc.nc
+    with ExitStack() as ctx:
+        lists = ctx.enter_context(tc.tile_pool(name="lists", bufs=1))
+        sb = ctx.enter_context(tc.tile_pool(name="sb", bufs=1))
+        psum = ctx.enter_context(tc.psum_pool(name="psum", bufs=8))
+
+        offs_t = lists.tile([P, S // 16], U16, name="offs_t")
+        held_t = lists.tile([P, S // 16], U16, name="held_t")
+
+        xs = sb.tile([P, T], U8, name="xs", align_bytes=64)
+        nc.vector.memset(xs[:].bitcast(I32), 0)
+
+        w1_rows = w1.rearrange("(p j) c -> p j c", j=PACK)
+        w1_raw = [sb.tile([P, PACK, H // 2], F32, name="w1_raw%d" % h) for h in range(2)]
+        xw = sb.tile([P, T], I32, name="xw", align_bytes=64)
+        w2_raw = sb.tile([P, PACK, N], F32, name="w2_raw")
+        b1_t = sb.tile([P, PACK], F32, name="b1_t")
+        b2_t = sb.tile([P, PACK], F32, name="b2_t")
+
+        nc.sync.dma_start(offs_t[:], offs)
+        nc.sync.dma_start(w1_raw[0][:], w1_rows[:, :, 0 : H // 2])
+        for q in range(4):
+            nc.scalar.dma_start(
+                xs[32 * q : 32 * q + 4, :].bitcast(I32), x_scales[0, 4 * q : 4 * q + 4, :].bitcast(I32)
+            )
+        nc.sync.dma_start(w1_raw[1][:], w1_rows[:, :, H // 2 : H])
+        nc.sync.dma_start(xw[:], x_words[0].rearrange("p n r -> p (n r)").bitcast(I32))
+        nc.sync.dma_start(held_t[:], held)
+        nc.scalar.dma_start(b1_t[:], b1.rearrange("(p t) o -> p (t o)", t=PACK))
+        nc.sync.dma_start(w2_raw[:], w2.rearrange("(p j) c -> p j c", j=PACK))
+        nc.sync.dma_start(b2_t[:], b2.rearrange("(p t) o -> p (t o)", t=PACK))
+
+        early = [sb.tile([P, U], F32, name="early%d" % h) for h in range(2)]
+        late = [sb.tile([P, 2 * U], F32, name="late%d" % h) for h in range(2)]
+        for h in range(2):
+            nc.vector.memset(early[h][:], 0.0)
+        for h in range(2):
+            nc.vector.memset(late[h][:, 0:U], 0.0)
+
+        w1_bf = sb.tile([P, PACK * H], BF16, name="w1_bf", align_bytes=64)
+        nc.scalar.activation(dealt(w1_bf[:])[:, 0:64], by_column(w1_raw[0][:]), ACT.Copy)
+        xs_g = sb.tile([P, S], U8, name="xs_g", align_bytes=64)
+        nc.vector.tensor_copy(xs_g[:], xs[:].indirect(offs_t[:]))
+        nc.vector.tensor_copy(dealt(w1_bf[:])[:, 64:128], by_column(w1_raw[1][:]))
+        w1_q = sb.tile([P, H], U32, name="w1_q", align_bytes=64)
+        w1_s = sb.tile([P, H], U8, name="w1_s", align_bytes=64)
+        nc.vector.quantize_mx(out=w1_q[:].bitcast(FP8X4), scales=w1_s[:], in_=w1_bf[:])
+
+        xw_g = sb.tile([P, S], U32, name="xw_g", align_bytes=64)
+        for h in range(2):
+            nc.vector.tensor_copy(
+                xw_g[:, h * HALF : (h + 1) * HALF],
+                xw[:].bitcast(U32).indirect(offs_t[:, h * 16 : (h + 1) * 16]),
+            )
+
+        def encode(t, lo, hi):
+            acc = psum.tile([P, 512], F32, name="acc")
+            cols = slice(t * P, (t + 1) * P)
+            nc.tensor.matmul_mx(
+                out=acc[:, 0 : hi - lo],
+                lhsT=w1_q[:, cols].bitcast(FP8X4),
+                lhsT_scale=w1_s[:, cols],
+                rhs=xw_g[:, lo:hi].bitcast(FP8X4),
+                rhs_scale=xs_g[:, lo:hi],
+                start=True,
+                stop=True,
+            )
+            y = sb.tile([P, hi - lo], F32, name="y%d_%d" % (t, lo))
+            nc.scalar.activation(y[:], acc[:, 0 : hi - lo], ACT.Relu, bias=b1_t[:, t : t + 1])
+            return y
+
+        for lo in (0, HALF):
+            for h in range(2):
+                y = encode(2 * h + 1, lo, lo + HALF)
+                nc.vector.tensor_copy(early[h][:].indirect(held_t[:, lo // 16 : (lo + HALF) // 16]), y[:])
+        y_late = [encode(2 * h, 0, S) for h in range(2)]
+
+        w2_bf = sb.tile([P, PACK * N], BF16, name="w2_bf", align_bytes=64)
+        nc.scalar.activation(dealt(w2_bf[:]), by_column(w2_raw[:]), ACT.Copy)
+        w2_q = sb.tile([P, N], U32, name="w2_q", align_bytes=64)
+        w2_s = sb.tile([P, N], U8, name="w2_s", align_bytes=64)
+        nc.vector.quantize_mx(out=w2_q[:].bitcast(FP8X4), scales=w2_s[:], in_=w2_bf[:])
+
+        for h in range(2):
+            nc.scalar.copy(late[h][:, U : 2 * U], early[h][:])
+        for h in range(2):
+            nc.vector.tensor_copy(late[h][:].indirect(held_t[:]), y_late[h][:])
+
+        starts = [sum(CHUNKS[:c]) for c in range(len(CHUNKS))]
+        pairs = [late[h][:].rearrange("p (e w) -> p w e", e=2) for h in range(2)]
+        z_bf = []
+        for c, width in enumerate(CHUNKS):
+            zb = sb.tile([P, width, PACK], BF16, name="z_bf%d" % c, align_bytes=64)
+            nc.scalar.activation(zb[:, :, 0:2], pairs[0][:, starts[c] : starts[c] + width, :], ACT.Copy)
+            z_bf.append(zb)
+
+        out_rows = out.rearrange("(p t) w -> p t w", t=PACK)
+        for c, width in enumerate(CHUNKS):
+            nc.vector.tensor_copy(z_bf[c][:, :, 2:4], pairs[1][:, starts[c] : starts[c] + width, :])
+            z_q = sb.tile([P, width], U32, name="z_q%d" % c, align_bytes=64)
+            z_s = sb.tile([P, width], U8, name="z_s%d" % c, align_bytes=64)
+            nc.vector.quantize_mx(
+                out=z_q[:].bitcast(FP8X4), scales=z_s[:], in_=z_bf[c][:].rearrange("p w t -> p (w t)")
+            )
+            for g in range(2):
+                res = sb.tile([P, 2, width], F32, name="res%d_%d" % (c, g))
+                for e in range(2):
+                    t = 2 * g + e
+                    acc = psum.tile([P, 512], F32, name="acc")
+                    cols = slice(t * P, (t + 1) * P)
+                    nc.tensor.matmul_mx(
+                        out=acc[:, 0:width],
+                        lhsT=w2_q[:, cols].bitcast(FP8X4),
+                        lhsT_scale=w2_s[:, cols],
+                        rhs=z_q[:].bitcast(FP8X4),
+                        rhs_scale=z_s[:],
+                        start=True,
+                        stop=True,
+                    )
+                    if e == 1 and c >= len(CHUNKS) - SHARED_CHUNKS:
+                        nc.vector.tensor_scalar_add(res[:, e, :], acc[:, 0:width], b2_t[:, t : t + 1])
+                    else:
+                        nc.scalar.activation(res[:, e, :], acc[:, 0:width], ACT.Identity, bias=b2_t[:, t : t + 1])
+                nc.sync.dma_start(out_rows[:, 2 * g : 2 * g + 2, starts[c] : starts[c] + width], res[:])

@@ -17,8 +17,11 @@ ACT = mybir.ActivationFunctionType
 P = 128
 PACK = 4
 HALF = S // 2
-CHUNKS = (128, 128, 256, 256, 256)
-SHARED_CHUNKS = 2
+CHUNKS = (128, 128, 256, 512)
+STORE_ROWS = (2, 2, 2, 1)
+VECTOR_ROWS = ((), (), (), (0, 2))
+W1_SCALAR = 64
+CAST_COLS = 256
 
 
 def dealt(grouped):
@@ -42,25 +45,24 @@ def tile_picked_sae8_relu_p_kernel(
         held_t = lists.tile([P, S // 16], U16, name="held_t")
 
         xs = sb.tile([P, T], U8, name="xs", align_bytes=64)
-        nc.vector.memset(xs[:].bitcast(I32), 0)
+        nc.gpsimd.memset(xs[:].bitcast(I32), 0)
 
         w1_rows = w1.rearrange("(p j) c -> p j c", j=PACK)
-        w1_raw = [sb.tile([P, PACK, H // 2], F32, name="w1_raw%d" % h) for h in range(2)]
+        w1_raw = sb.tile([P, PACK, H], F32, name="w1_raw")
         xw = sb.tile([P, T], I32, name="xw", align_bytes=64)
         w2_raw = sb.tile([P, PACK, N], F32, name="w2_raw")
         b1_t = sb.tile([P, PACK], F32, name="b1_t")
         b2_t = sb.tile([P, PACK], F32, name="b2_t")
 
         nc.sync.dma_start(offs_t[:], offs)
-        nc.sync.dma_start(w1_raw[0][:], w1_rows[:, :, 0 : H // 2])
+        nc.sync.dma_start(w1_raw[:], w1_rows)
         for q in range(4):
-            nc.scalar.dma_start(
+            nc.sync.dma_start(
                 xs[32 * q : 32 * q + 4, :].bitcast(I32), x_scales[0, 4 * q : 4 * q + 4, :].bitcast(I32)
             )
-        nc.sync.dma_start(w1_raw[1][:], w1_rows[:, :, H // 2 : H])
+        nc.sync.dma_start(b1_t[:], b1.rearrange("(p t) o -> p (t o)", t=PACK))
         nc.sync.dma_start(xw[:], x_words[0].rearrange("p n r -> p (n r)").bitcast(I32))
         nc.sync.dma_start(held_t[:], held)
-        nc.scalar.dma_start(b1_t[:], b1.rearrange("(p t) o -> p (t o)", t=PACK))
         nc.sync.dma_start(w2_raw[:], w2.rearrange("(p j) c -> p j c", j=PACK))
         nc.sync.dma_start(b2_t[:], b2.rearrange("(p t) o -> p (t o)", t=PACK))
 
@@ -69,23 +71,24 @@ def tile_picked_sae8_relu_p_kernel(
         for h in range(2):
             nc.vector.memset(early[h][:], 0.0)
         for h in range(2):
-            nc.vector.memset(late[h][:, 0:U], 0.0)
+            nc.gpsimd.memset(late[h][:, 0:U], 0.0)
 
-        w1_bf = sb.tile([P, PACK * H], BF16, name="w1_bf", align_bytes=64)
-        nc.scalar.activation(dealt(w1_bf[:])[:, 0:64], by_column(w1_raw[0][:]), ACT.Copy)
+        w1_bf = sb.tile([P, PACK * H], BF16, name="w1_bf", tag="w1_bf", align_bytes=64)
+        nc.scalar.activation(dealt(w1_bf[:])[:, 0:W1_SCALAR], by_column(w1_raw[:])[:, 0:W1_SCALAR], ACT.Copy)
         xs_g = sb.tile([P, S], U8, name="xs_g", align_bytes=64)
-        nc.vector.tensor_copy(xs_g[:], xs[:].indirect(offs_t[:]))
-        nc.vector.tensor_copy(dealt(w1_bf[:])[:, 64:128], by_column(w1_raw[1][:]))
+        nc.vector.tensor_copy(dealt(w1_bf[:])[:, W1_SCALAR:P], by_column(w1_raw[:])[:, W1_SCALAR:P])
+        nc.vector.tensor_copy(xs_g[:, 0:HALF], xs[:].indirect(offs_t[:, 0:16]))
         w1_q = sb.tile([P, H], U32, name="w1_q", align_bytes=64)
         w1_s = sb.tile([P, H], U8, name="w1_s", align_bytes=64)
         nc.vector.quantize_mx(out=w1_q[:].bitcast(FP8X4), scales=w1_s[:], in_=w1_bf[:])
 
-        xw_g = sb.tile([P, S], U32, name="xw_g", align_bytes=64)
+        xw_g = sb.tile([P, S], U32, name="xw_g", tag="w1_bf", align_bytes=64)
         for h in range(2):
             nc.vector.tensor_copy(
                 xw_g[:, h * HALF : (h + 1) * HALF],
                 xw[:].bitcast(U32).indirect(offs_t[:, h * 16 : (h + 1) * 16]),
             )
+        nc.vector.tensor_copy(xs_g[:, HALF:S], xs[:].indirect(offs_t[:, 16:32]))
 
         def encode(t, lo, hi):
             acc = psum.tile([P, 512], F32, name="acc")
@@ -128,18 +131,31 @@ def tile_picked_sae8_relu_p_kernel(
             nc.scalar.activation(zb[:, :, 0:2], pairs[0][:, starts[c] : starts[c] + width, :], ACT.Copy)
             z_bf.append(zb)
 
-        out_rows = out.rearrange("(p t) w -> p t w", t=PACK)
-        for c, width in enumerate(CHUNKS):
-            nc.vector.tensor_copy(z_bf[c][:, :, 2:4], pairs[1][:, starts[c] : starts[c] + width, :])
-            z_q = sb.tile([P, width], U32, name="z_q%d" % c, align_bytes=64)
-            z_s = sb.tile([P, width], U8, name="z_s%d" % c, align_bytes=64)
+        def cast(c, lo, hi):
+            nc.vector.tensor_copy(z_bf[c][:, lo:hi, 2:4], pairs[1][:, starts[c] + lo : starts[c] + hi, :])
+
+        def quantise(c):
+            z_q = sb.tile([P, CHUNKS[c]], U32, name="z_q%d" % c, align_bytes=64)
+            z_s = sb.tile([P, CHUNKS[c]], U8, name="z_s%d" % c, align_bytes=64)
             nc.vector.quantize_mx(
                 out=z_q[:].bitcast(FP8X4), scales=z_s[:], in_=z_bf[c][:].rearrange("p w t -> p (w t)")
             )
-            for g in range(2):
-                res = sb.tile([P, 2, width], F32, name="res%d_%d" % (c, g))
-                for e in range(2):
-                    t = 2 * g + e
+            return z_q, z_s
+
+        z_mx = []
+        for c, width in enumerate(CHUNKS):
+            for lo in range(0, width, CAST_COLS):
+                cast(c, lo, min(width, lo + CAST_COLS))
+            z_mx.append(quantise(c))
+
+        out_rows = out.rearrange("(p t) w -> p t w", t=PACK)
+        for c, width in enumerate(CHUNKS):
+            z_q, z_s = z_mx[c]
+            rows = STORE_ROWS[c]
+            for g in range(PACK // rows):
+                res = sb.tile([P, rows, width], F32, name="res%d_%d" % (c, g))
+                for e in range(rows):
+                    t = rows * g + e
                     acc = psum.tile([P, 512], F32, name="acc")
                     cols = slice(t * P, (t + 1) * P)
                     nc.tensor.matmul_mx(
@@ -151,8 +167,8 @@ def tile_picked_sae8_relu_p_kernel(
                         start=True,
                         stop=True,
                     )
-                    if e == 1 and c >= len(CHUNKS) - SHARED_CHUNKS:
+                    if t in VECTOR_ROWS[c]:
                         nc.vector.tensor_scalar_add(res[:, e, :], acc[:, 0:width], b2_t[:, t : t + 1])
                     else:
                         nc.scalar.activation(res[:, e, :], acc[:, 0:width], ACT.Identity, bias=b2_t[:, t : t + 1])
-                nc.sync.dma_start(out_rows[:, 2 * g : 2 * g + 2, starts[c] : starts[c] + width], res[:])
+                nc.sync.dma_start(out_rows[:, rows * g : rows * (g + 1), starts[c] : starts[c] + width], res[:])

@@ -20,16 +20,8 @@ HALF = S // 2
 CHUNKS = (128, 128, 256, 512)
 STORE_ROWS = (2, 2, 2, 1)
 VECTOR_ROWS = ((), (), (), (0, 2))
-W1_SCALAR = 64
 CAST_COLS = 256
-
-
-def dealt(grouped):
-    return grouped.rearrange("p (t m j) -> p m j t", t=PACK, j=PACK)
-
-
-def by_column(raw):
-    return raw.rearrange("p j (m t) -> p m j t", t=PACK)
+FIRST = 128
 
 
 def tile_picked_sae8_relu_p_kernel(
@@ -45,7 +37,7 @@ def tile_picked_sae8_relu_p_kernel(
         held_t = lists.tile([P, S // 16], U16, name="held_t")
 
         xs = sb.tile([P, T], U8, name="xs", align_bytes=64)
-        nc.gpsimd.memset(xs[:].bitcast(I32), 0)
+        nc.vector.memset(xs[:].bitcast(I32), 0)
 
         w1_rows = w1.rearrange("(p j) c -> p j c", j=PACK)
         w1_raw = sb.tile([P, PACK, H], F32, name="w1_raw")
@@ -54,14 +46,14 @@ def tile_picked_sae8_relu_p_kernel(
         b1_t = sb.tile([P, PACK], F32, name="b1_t")
         b2_t = sb.tile([P, PACK], F32, name="b2_t")
 
-        nc.sync.dma_start(offs_t[:], offs)
         nc.sync.dma_start(w1_raw[:], w1_rows)
+        nc.sync.dma_start(offs_t[:], offs)
         for q in range(4):
             nc.sync.dma_start(
                 xs[32 * q : 32 * q + 4, :].bitcast(I32), x_scales[0, 4 * q : 4 * q + 4, :].bitcast(I32)
             )
-        nc.sync.dma_start(b1_t[:], b1.rearrange("(p t) o -> p (t o)", t=PACK))
         nc.sync.dma_start(xw[:], x_words[0].rearrange("p n r -> p (n r)").bitcast(I32))
+        nc.sync.dma_start(b1_t[:], b1.rearrange("(p t) o -> p (t o)", t=PACK))
         nc.sync.dma_start(held_t[:], held)
         nc.sync.dma_start(w2_raw[:], w2.rearrange("(p j) c -> p j c", j=PACK))
         nc.sync.dma_start(b2_t[:], b2.rearrange("(p t) o -> p (t o)", t=PACK))
@@ -71,57 +63,70 @@ def tile_picked_sae8_relu_p_kernel(
         for h in range(2):
             nc.vector.memset(early[h][:], 0.0)
         for h in range(2):
-            nc.gpsimd.memset(late[h][:, 0:U], 0.0)
+            nc.scalar.copy(late[h][:, 0:U], early[0][:])
 
-        w1_bf = sb.tile([P, PACK * H], BF16, name="w1_bf", tag="w1_bf", align_bytes=64)
-        nc.scalar.activation(dealt(w1_bf[:])[:, 0:W1_SCALAR], by_column(w1_raw[:])[:, 0:W1_SCALAR], ACT.Copy)
+        w1_by_parity = w1_raw[:].rearrange("p j (m u v) -> p v m j u", u=2, v=2)
+        w1_bf = [sb.tile([P, 2 * H], BF16, name="w1_bf%d" % v, align_bytes=64) for v in range(2)]
+        w1_dealt = [w1_bf[v][:].rearrange("p (u m j) -> p m j u", u=2, j=PACK) for v in range(2)]
+        nc.vector.tensor_copy(w1_dealt[1], w1_by_parity[:, 1])
+        nc.scalar.activation(w1_dealt[0], w1_by_parity[:, 0], ACT.Copy)
         xs_g = sb.tile([P, S], U8, name="xs_g", align_bytes=64)
-        nc.vector.tensor_copy(dealt(w1_bf[:])[:, W1_SCALAR:P], by_column(w1_raw[:])[:, W1_SCALAR:P])
-        nc.vector.tensor_copy(xs_g[:, 0:HALF], xs[:].indirect(offs_t[:, 0:16]))
-        w1_q = sb.tile([P, H], U32, name="w1_q", align_bytes=64)
-        w1_s = sb.tile([P, H], U8, name="w1_s", align_bytes=64)
-        nc.vector.quantize_mx(out=w1_q[:].bitcast(FP8X4), scales=w1_s[:], in_=w1_bf[:])
+        nc.vector.tensor_copy(xs_g[:], xs[:].indirect(offs_t[:]))
+        w1_q = [sb.tile([P, H // 2], U32, name="w1_q%d" % v, align_bytes=64) for v in range(2)]
+        w1_s = [sb.tile([P, H // 2], U8, name="w1_s%d" % v, align_bytes=64) for v in range(2)]
+        for v in (1, 0):
+            nc.vector.quantize_mx(out=w1_q[v][:].bitcast(FP8X4), scales=w1_s[v][:], in_=w1_bf[v][:])
 
-        xw_g = sb.tile([P, S], U32, name="xw_g", tag="w1_bf", align_bytes=64)
+        xw_g = sb.tile([P, S], U32, name="xw_g", tag="w1_bf1", align_bytes=64)
         for h in range(2):
             nc.vector.tensor_copy(
                 xw_g[:, h * HALF : (h + 1) * HALF],
                 xw[:].bitcast(U32).indirect(offs_t[:, h * 16 : (h + 1) * 16]),
             )
-        nc.vector.tensor_copy(xs_g[:, HALF:S], xs[:].indirect(offs_t[:, 16:32]))
 
         def encode(t, lo, hi):
             acc = psum.tile([P, 512], F32, name="acc")
-            cols = slice(t * P, (t + 1) * P)
-            nc.tensor.matmul_mx(
-                out=acc[:, 0 : hi - lo],
-                lhsT=w1_q[:, cols].bitcast(FP8X4),
-                lhsT_scale=w1_s[:, cols],
-                rhs=xw_g[:, lo:hi].bitcast(FP8X4),
-                rhs_scale=xs_g[:, lo:hi],
-                start=True,
-                stop=True,
-            )
+            cols = slice(t // 2 * P, (t // 2 + 1) * P)
+            cuts = [lo, hi] if lo % HALF == 0 else [lo, HALF, hi]
+            for a, b in zip(cuts[:-1], cuts[1:]):
+                nc.tensor.matmul_mx(
+                    out=acc[:, a - lo : b - lo],
+                    lhsT=w1_q[t % 2][:, cols].bitcast(FP8X4),
+                    lhsT_scale=w1_s[t % 2][:, cols],
+                    rhs=xw_g[:, a:b].bitcast(FP8X4),
+                    rhs_scale=xs_g[:, a:b],
+                    start=True,
+                    stop=True,
+                )
             y = sb.tile([P, hi - lo], F32, name="y%d_%d" % (t, lo))
             nc.scalar.activation(y[:], acc[:, 0 : hi - lo], ACT.Relu, bias=b1_t[:, t : t + 1])
             return y
 
-        for lo in (0, HALF):
-            for h in range(2):
-                y = encode(2 * h + 1, lo, lo + HALF)
-                nc.vector.tensor_copy(early[h][:].indirect(held_t[:, lo // 16 : (lo + HALF) // 16]), y[:])
-        y_late = [encode(2 * h, 0, S) for h in range(2)]
+        def scatter(window, y, lo, hi):
+            nc.vector.tensor_copy(window[:].indirect(held_t[:, lo // 16 : hi // 16]), y[:])
 
-        w2_bf = sb.tile([P, PACK * N], BF16, name="w2_bf", align_bytes=64)
-        nc.scalar.activation(dealt(w2_bf[:]), by_column(w2_raw[:]), ACT.Copy)
-        w2_q = sb.tile([P, N], U32, name="w2_q", align_bytes=64)
-        w2_s = sb.tile([P, N], U8, name="w2_s", align_bytes=64)
-        nc.vector.quantize_mx(out=w2_q[:].bitcast(FP8X4), scales=w2_s[:], in_=w2_bf[:])
+        for h, lo, hi in ((0, 0, FIRST), (1, 0, HALF), (0, FIRST, S), (1, HALF, S)):
+            scatter(early[h], encode(2 * h + 1, lo, hi), lo, hi)
+        y_0 = encode(0, 0, S)
+        y_2 = encode(2, 0, S)
 
+        w2_by_pair = w2_raw[:].rearrange("p j (m g e) -> p g m j e", g=2, e=2)
+        w2_bf = [sb.tile([P, 2 * N], BF16, name="w2_bf%d" % g, align_bytes=64) for g in range(2)]
+        w2_q = [sb.tile([P, N // 2], U32, name="w2_q%d" % g, align_bytes=64) for g in range(2)]
+        w2_s = [sb.tile([P, N // 2], U8, name="w2_s%d" % g, align_bytes=64) for g in range(2)]
+
+        def quantise_w2(g):
+            nc.scalar.activation(
+                w2_bf[g][:].rearrange("p (e m j) -> p m j e", e=2, j=PACK), w2_by_pair[:, g], ACT.Copy
+            )
+            nc.vector.quantize_mx(out=w2_q[g][:].bitcast(FP8X4), scales=w2_s[g][:], in_=w2_bf[g][:])
+
+        quantise_w2(0)
         for h in range(2):
             nc.scalar.copy(late[h][:, U : 2 * U], early[h][:])
-        for h in range(2):
-            nc.vector.tensor_copy(late[h][:].indirect(held_t[:]), y_late[h][:])
+        scatter(late[0], y_0, 0, S)
+        scatter(late[1], y_2, 0, S)
+        quantise_w2(1)
 
         starts = [sum(CHUNKS[:c]) for c in range(len(CHUNKS))]
         pairs = [late[h][:].rearrange("p (e w) -> p w e", e=2) for h in range(2)]
@@ -157,11 +162,11 @@ def tile_picked_sae8_relu_p_kernel(
                 for e in range(rows):
                     t = rows * g + e
                     acc = psum.tile([P, 512], F32, name="acc")
-                    cols = slice(t * P, (t + 1) * P)
+                    cols = slice(t % 2 * P, (t % 2 + 1) * P)
                     nc.tensor.matmul_mx(
                         out=acc[:, 0:width],
-                        lhsT=w2_q[:, cols].bitcast(FP8X4),
-                        lhsT_scale=w2_s[:, cols],
+                        lhsT=w2_q[t // 2][:, cols].bitcast(FP8X4),
+                        lhsT_scale=w2_s[t // 2][:, cols],
                         rhs=z_q[:].bitcast(FP8X4),
                         rhs_scale=z_s[:],
                         start=True,

@@ -18,10 +18,11 @@ P = 128
 PACK = 4
 HALF = S // 2
 CHUNKS = (128, 128, 256, 512)
-STORE_ROWS = (2, 2, 2, 1)
+STORE_ROWS = ((1, 1, 2), (2, 2), (2, 2), (1, 1, 1, 1))
 VECTOR_ROWS = ((), (), (), (0, 2))
 CAST_COLS = 256
 FIRST = 128
+WARM = 6
 
 
 def tile_picked_sae8_relu_p_kernel(
@@ -108,7 +109,7 @@ def tile_picked_sae8_relu_p_kernel(
         for h, lo, hi in ((0, 0, FIRST), (1, 0, HALF), (0, FIRST, S), (1, HALF, S)):
             scatter(early[h], encode(2 * h + 1, lo, hi), lo, hi)
         y_0 = encode(0, 0, S)
-        y_2 = encode(2, 0, S)
+        y_2 = encode(2, 0, HALF)
 
         w2_by_pair = w2_raw[:].rearrange("p j (m g e) -> p g m j e", g=2, e=2)
         w2_bf = [sb.tile([P, 2 * N], BF16, name="w2_bf%d" % g, align_bytes=64) for g in range(2)]
@@ -125,8 +126,21 @@ def tile_picked_sae8_relu_p_kernel(
         for h in range(2):
             nc.scalar.copy(late[h][:, U : 2 * U], early[h][:])
         scatter(late[0], y_0, 0, S)
-        scatter(late[1], y_2, 0, S)
+        scatter(late[1], y_2, 0, HALF)
         quantise_w2(1)
+        scatter(late[1], encode(2, HALF, S), HALF, S)
+
+        warm = psum.tile([P, 512], F32, name="acc")
+        for i in range(WARM):
+            nc.tensor.matmul_mx(
+                out=warm[:, 0:HALF],
+                lhsT=w2_q[1][:, 0:P].bitcast(FP8X4),
+                lhsT_scale=w2_s[1][:, 0:P],
+                rhs=w2_q[1][:].bitcast(FP8X4),
+                rhs_scale=w2_s[1][:],
+                start=(i == 0),
+                stop=(i == WARM - 1),
+            )
 
         starts = [sum(CHUNKS[:c]) for c in range(len(CHUNKS))]
         pairs = [late[h][:].rearrange("p (e w) -> p w e", e=2) for h in range(2)]
@@ -135,6 +149,8 @@ def tile_picked_sae8_relu_p_kernel(
             zb = sb.tile([P, width, PACK], BF16, name="z_bf%d" % c, align_bytes=64)
             nc.scalar.activation(zb[:, :, 0:2], pairs[0][:, starts[c] : starts[c] + width, :], ACT.Copy)
             z_bf.append(zb)
+
+        nc.scalar.activation(z_bf[-1][:, CAST_COLS:, 2:4], pairs[1][:, U - CAST_COLS : U, :], ACT.Copy)
 
         def cast(c, lo, hi):
             nc.vector.tensor_copy(z_bf[c][:, lo:hi, 2:4], pairs[1][:, starts[c] + lo : starts[c] + hi, :])
@@ -149,18 +165,17 @@ def tile_picked_sae8_relu_p_kernel(
 
         z_mx = []
         for c, width in enumerate(CHUNKS):
-            for lo in range(0, width, CAST_COLS):
-                cast(c, lo, min(width, lo + CAST_COLS))
+            cast(c, 0, min(width, CAST_COLS))
             z_mx.append(quantise(c))
 
         out_rows = out.rearrange("(p t) w -> p t w", t=PACK)
         for c, width in enumerate(CHUNKS):
             z_q, z_s = z_mx[c]
-            rows = STORE_ROWS[c]
-            for g in range(PACK // rows):
+            for g, rows in enumerate(STORE_ROWS[c]):
+                t0 = sum(STORE_ROWS[c][:g])
                 res = sb.tile([P, rows, width], F32, name="res%d_%d" % (c, g))
                 for e in range(rows):
-                    t = rows * g + e
+                    t = t0 + e
                     acc = psum.tile([P, 512], F32, name="acc")
                     cols = slice(t % 2 * P, (t % 2 + 1) * P)
                     nc.tensor.matmul_mx(
@@ -176,4 +191,4 @@ def tile_picked_sae8_relu_p_kernel(
                         nc.vector.tensor_scalar_add(res[:, e, :], acc[:, 0:width], b2_t[:, t : t + 1])
                     else:
                         nc.scalar.activation(res[:, e, :], acc[:, 0:width], ACT.Identity, bias=b2_t[:, t : t + 1])
-                nc.sync.dma_start(out_rows[:, rows * g : rows * (g + 1), starts[c] : starts[c] + width], res[:])
+                nc.sync.dma_start(out_rows[:, t0 : t0 + rows, starts[c] : starts[c] + width], res[:])

@@ -17,12 +17,11 @@ ACT = mybir.ActivationFunctionType
 P = 128
 PACK = 4
 HALF = S // 2
-CHUNKS = (128, 128, 256, 512)
-STORE_ROWS = ((1, 1, 2), (2, 2), (2, 2), (1, 1, 1, 1))
-VECTOR_ROWS = ((), (), (), (0, 2))
-CAST_COLS = 256
+CHUNKS = (128, 128, 128, 128, 256, 256)
+STORE_ROWS = ((2, 2), (4,), (4,), (4,), (4,), (4,))
+VECTOR_ROWS = ((), (), (), (1, 3), (1, 3), (1, 3))
+VECTOR_COLS = 640
 FIRST = 128
-WARM = 6
 
 
 def tile_picked_sae8_relu_p_kernel(
@@ -59,7 +58,7 @@ def tile_picked_sae8_relu_p_kernel(
         nc.sync.dma_start(w2_raw[:], w2.rearrange("(p j) c -> p j c", j=PACK))
         nc.sync.dma_start(b2_t[:], b2.rearrange("(p t) o -> p (t o)", t=PACK))
 
-        early = [sb.tile([P, U], F32, name="early%d" % h) for h in range(2)]
+        early = [sb.tile([P, U], F32, name="early%d" % h, align_bytes=64) for h in range(2)]
         late = [sb.tile([P, 2 * U], F32, name="late%d" % h) for h in range(2)]
         for h in range(2):
             nc.vector.memset(early[h][:], 0.0)
@@ -108,39 +107,24 @@ def tile_picked_sae8_relu_p_kernel(
 
         for h, lo, hi in ((0, 0, FIRST), (1, 0, HALF), (0, FIRST, S), (1, HALF, S)):
             scatter(early[h], encode(2 * h + 1, lo, hi), lo, hi)
-        y_0 = encode(0, 0, S)
-        y_2 = encode(2, 0, HALF)
+        y_late = [encode(2 * h, 0, S) for h in range(2)]
 
         w2_by_pair = w2_raw[:].rearrange("p j (m g e) -> p g m j e", g=2, e=2)
         w2_bf = [sb.tile([P, 2 * N], BF16, name="w2_bf%d" % g, align_bytes=64) for g in range(2)]
-        w2_q = [sb.tile([P, N // 2], U32, name="w2_q%d" % g, align_bytes=64) for g in range(2)]
-        w2_s = [sb.tile([P, N // 2], U8, name="w2_s%d" % g, align_bytes=64) for g in range(2)]
-
-        def quantise_w2(g):
+        for g in range(2):
             nc.scalar.activation(
                 w2_bf[g][:].rearrange("p (e m j) -> p m j e", e=2, j=PACK), w2_by_pair[:, g], ACT.Copy
             )
-            nc.vector.quantize_mx(out=w2_q[g][:].bitcast(FP8X4), scales=w2_s[g][:], in_=w2_bf[g][:])
-
-        quantise_w2(0)
+            nc.scalar.copy(late[g][:, U : 2 * U], early[g][:])
         for h in range(2):
-            nc.scalar.copy(late[h][:, U : 2 * U], early[h][:])
-        scatter(late[0], y_0, 0, S)
-        scatter(late[1], y_2, 0, HALF)
-        quantise_w2(1)
-        scatter(late[1], encode(2, HALF, S), HALF, S)
+            scatter(late[h], y_late[h], 0, S)
 
-        warm = psum.tile([P, 512], F32, name="acc")
-        for i in range(WARM):
-            nc.tensor.matmul_mx(
-                out=warm[:, 0:HALF],
-                lhsT=w2_q[1][:, 0:P].bitcast(FP8X4),
-                lhsT_scale=w2_s[1][:, 0:P],
-                rhs=w2_q[1][:].bitcast(FP8X4),
-                rhs_scale=w2_s[1][:],
-                start=(i == 0),
-                stop=(i == WARM - 1),
-            )
+        w2_q = sb.tile([P, N], U32, name="w2_q", tag="early1", align_bytes=64)
+        w2_s = sb.tile([P, N], U8, name="w2_s", align_bytes=64)
+
+        def quantise_w2(g):
+            cols = slice(g * N // 2, (g + 1) * N // 2)
+            nc.vector.quantize_mx(out=w2_q[:, cols].bitcast(FP8X4), scales=w2_s[:, cols], in_=w2_bf[g][:])
 
         starts = [sum(CHUNKS[:c]) for c in range(len(CHUNKS))]
         pairs = [late[h][:].rearrange("p (e w) -> p w e", e=2) for h in range(2)]
@@ -150,10 +134,19 @@ def tile_picked_sae8_relu_p_kernel(
             nc.scalar.activation(zb[:, :, 0:2], pairs[0][:, starts[c] : starts[c] + width, :], ACT.Copy)
             z_bf.append(zb)
 
-        nc.scalar.activation(z_bf[-1][:, CAST_COLS:, 2:4], pairs[1][:, U - CAST_COLS : U, :], ACT.Copy)
+        for c, width in enumerate(CHUNKS):
+            lo = max(VECTOR_COLS - starts[c], 0)
+            if lo < width:
+                nc.scalar.activation(
+                    z_bf[c][:, lo:, 2:4], pairs[1][:, starts[c] + lo : starts[c] + width, :], ACT.Copy
+                )
 
-        def cast(c, lo, hi):
-            nc.vector.tensor_copy(z_bf[c][:, lo:hi, 2:4], pairs[1][:, starts[c] + lo : starts[c] + hi, :])
+        def cast(c):
+            hi = min(VECTOR_COLS - starts[c], CHUNKS[c])
+            if hi > 0:
+                nc.vector.tensor_copy(z_bf[c][:, 0:hi, 2:4], pairs[1][:, starts[c] : starts[c] + hi, :])
+
+        z_mx = []
 
         def quantise(c):
             z_q = sb.tile([P, CHUNKS[c]], U32, name="z_q%d" % c, align_bytes=64)
@@ -161,12 +154,17 @@ def tile_picked_sae8_relu_p_kernel(
             nc.vector.quantize_mx(
                 out=z_q[:].bitcast(FP8X4), scales=z_s[:], in_=z_bf[c][:].rearrange("p w t -> p (w t)")
             )
-            return z_q, z_s
+            z_mx.append((z_q, z_s))
 
-        z_mx = []
-        for c, width in enumerate(CHUNKS):
-            cast(c, 0, min(width, CAST_COLS))
-            z_mx.append(quantise(c))
+        quantise_w2(0)
+        cast(0)
+        quantise_w2(1)
+        quantise(0)
+        cast(1)
+        for c in range(1, len(CHUNKS)):
+            if c + 1 < len(CHUNKS):
+                cast(c + 1)
+            quantise(c)
 
         out_rows = out.rearrange("(p t) w -> p t w", t=PACK)
         for c, width in enumerate(CHUNKS):
@@ -177,11 +175,11 @@ def tile_picked_sae8_relu_p_kernel(
                 for e in range(rows):
                     t = t0 + e
                     acc = psum.tile([P, 512], F32, name="acc")
-                    cols = slice(t % 2 * P, (t % 2 + 1) * P)
+                    cols = slice(t * P, (t + 1) * P)
                     nc.tensor.matmul_mx(
                         out=acc[:, 0:width],
-                        lhsT=w2_q[t // 2][:, cols].bitcast(FP8X4),
-                        lhsT_scale=w2_s[t // 2][:, cols],
+                        lhsT=w2_q[:, cols].bitcast(FP8X4),
+                        lhsT_scale=w2_s[:, cols],
                         rhs=z_q[:].bitcast(FP8X4),
                         rhs_scale=z_s[:],
                         start=True,

@@ -17,11 +17,20 @@ ACT = mybir.ActivationFunctionType
 P = 128
 PACK = 4
 HALF = S // 2
-CHUNKS = (128, 128, 128, 128, 256, 256)
-STORE_ROWS = ((2, 2), (4,), (4,), (4,), (4,), (4,))
-VECTOR_ROWS = ((), (), (), (1, 3), (1, 3), (1, 3))
+CHUNKS = (128, 128, 256, 256, 256)
+STORES = (
+    (False, 0, 2, ((0, 128),)),
+    (False, 2, 2, ((0, 256),)),
+    (False, 0, 1, ((128, 256, 512),)),
+    (False, 1, 1, ((128, 256, 512),)),
+    (True, 2, 1, ((256, 768), (768, 1024))),
+    (False, 0, 1, ((512, 1024),)),
+    (True, 3, 1, ((256, 768), (768, 1024))),
+    (False, 1, 1, ((512, 1024),)),
+)
 VECTOR_COLS = 640
 FIRST = 128
+WARM = 6
 
 
 def tile_picked_sae8_relu_p_kernel(
@@ -107,7 +116,8 @@ def tile_picked_sae8_relu_p_kernel(
 
         for h, lo, hi in ((0, 0, FIRST), (1, 0, HALF), (0, FIRST, S), (1, HALF, S)):
             scatter(early[h], encode(2 * h + 1, lo, hi), lo, hi)
-        y_late = [encode(2 * h, 0, S) for h in range(2)]
+        y_0 = encode(0, 0, S)
+        y_2 = [encode(2, h * HALF, (h + 1) * HALF) for h in range(2)]
 
         w2_by_pair = w2_raw[:].rearrange("p j (m g e) -> p g m j e", g=2, e=2)
         w2_bf = [sb.tile([P, 2 * N], BF16, name="w2_bf%d" % g, align_bytes=64) for g in range(2)]
@@ -116,8 +126,6 @@ def tile_picked_sae8_relu_p_kernel(
                 w2_bf[g][:].rearrange("p (e m j) -> p m j e", e=2, j=PACK), w2_by_pair[:, g], ACT.Copy
             )
             nc.scalar.copy(late[g][:, U : 2 * U], early[g][:])
-        for h in range(2):
-            scatter(late[h], y_late[h], 0, S)
 
         w2_q = sb.tile([P, N], U32, name="w2_q", tag="early1", align_bytes=64)
         w2_s = sb.tile([P, N], U8, name="w2_s", align_bytes=64)
@@ -125,6 +133,24 @@ def tile_picked_sae8_relu_p_kernel(
         def quantise_w2(g):
             cols = slice(g * N // 2, (g + 1) * N // 2)
             nc.vector.quantize_mx(out=w2_q[:, cols].bitcast(FP8X4), scales=w2_s[:, cols], in_=w2_bf[g][:])
+
+        scatter(late[0], y_0, 0, S)
+        scatter(late[1], y_2[0], 0, HALF)
+        quantise_w2(0)
+        scatter(late[1], y_2[1], HALF, S)
+        quantise_w2(1)
+
+        warm = psum.tile([P, 512], F32, name="acc")
+        for i in range(WARM):
+            nc.tensor.matmul_mx(
+                out=warm[:, 0:HALF],
+                lhsT=w2_q[:, 0:P].bitcast(FP8X4),
+                lhsT_scale=w2_s[:, 0:P],
+                rhs=w2_q[:, 0:HALF].bitcast(FP8X4),
+                rhs_scale=w2_s[:, 0:HALF],
+                start=(i == 0),
+                stop=(i == WARM - 1),
+            )
 
         starts = [sum(CHUNKS[:c]) for c in range(len(CHUNKS))]
         pairs = [late[h][:].rearrange("p (e w) -> p w e", e=2) for h in range(2)]
@@ -146,47 +172,45 @@ def tile_picked_sae8_relu_p_kernel(
             if hi > 0:
                 nc.vector.tensor_copy(z_bf[c][:, 0:hi, 2:4], pairs[1][:, starts[c] : starts[c] + hi, :])
 
-        z_mx = []
+        z_q = sb.tile([P, U], U32, name="z_q", align_bytes=64)
+        z_s = sb.tile([P, U], U8, name="z_s", align_bytes=64)
 
         def quantise(c):
-            z_q = sb.tile([P, CHUNKS[c]], U32, name="z_q%d" % c, align_bytes=64)
-            z_s = sb.tile([P, CHUNKS[c]], U8, name="z_s%d" % c, align_bytes=64)
+            cols = slice(starts[c], starts[c] + CHUNKS[c])
             nc.vector.quantize_mx(
-                out=z_q[:].bitcast(FP8X4), scales=z_s[:], in_=z_bf[c][:].rearrange("p w t -> p (w t)")
+                out=z_q[:, cols].bitcast(FP8X4), scales=z_s[:, cols], in_=z_bf[c][:].rearrange("p w t -> p (w t)")
             )
-            z_mx.append((z_q, z_s))
 
-        quantise_w2(0)
         cast(0)
-        quantise_w2(1)
-        quantise(0)
-        cast(1)
-        for c in range(1, len(CHUNKS)):
+        for c in range(len(CHUNKS)):
             if c + 1 < len(CHUNKS):
                 cast(c + 1)
             quantise(c)
 
         out_rows = out.rearrange("(p t) w -> p t w", t=PACK)
-        for c, width in enumerate(CHUNKS):
-            z_q, z_s = z_mx[c]
-            for g, rows in enumerate(STORE_ROWS[c]):
-                t0 = sum(STORE_ROWS[c][:g])
-                res = sb.tile([P, rows, width], F32, name="res%d_%d" % (c, g))
-                for e in range(rows):
-                    t = t0 + e
-                    acc = psum.tile([P, 512], F32, name="acc")
-                    cols = slice(t * P, (t + 1) * P)
-                    nc.tensor.matmul_mx(
-                        out=acc[:, 0:width],
-                        lhsT=w2_q[:, cols].bitcast(FP8X4),
-                        lhsT_scale=w2_s[:, cols],
-                        rhs=z_q[:].bitcast(FP8X4),
-                        rhs_scale=z_s[:],
-                        start=True,
-                        stop=True,
-                    )
-                    if t in VECTOR_ROWS[c]:
-                        nc.vector.tensor_scalar_add(res[:, e, :], acc[:, 0:width], b2_t[:, t : t + 1])
-                    else:
-                        nc.scalar.activation(res[:, e, :], acc[:, 0:width], ACT.Identity, bias=b2_t[:, t : t + 1])
-                nc.sync.dma_start(out_rows[:, t0 : t0 + rows, starts[c] : starts[c] + width], res[:])
+
+        def decode(on_vector, res, t, cuts):
+            acc = psum.tile([P, 512], F32, name="acc")
+            for a, b in zip(cuts[:-1], cuts[1:]):
+                nc.tensor.matmul_mx(
+                    out=acc[:, a - cuts[0] : b - cuts[0]],
+                    lhsT=w2_q[:, t * P : (t + 1) * P].bitcast(FP8X4),
+                    lhsT_scale=w2_s[:, t * P : (t + 1) * P],
+                    rhs=z_q[:, a:b].bitcast(FP8X4),
+                    rhs_scale=z_s[:, a:b],
+                    start=True,
+                    stop=True,
+                )
+            width = cuts[-1] - cuts[0]
+            if on_vector:
+                nc.vector.tensor_scalar_add(res, acc[:, 0:width], b2_t[:, t : t + 1])
+            else:
+                nc.scalar.activation(res, acc[:, 0:width], ACT.Identity, bias=b2_t[:, t : t + 1])
+
+        for i, (on_vector, t0, rows, banks) in enumerate(STORES):
+            lo, hi = banks[0][0], banks[-1][-1]
+            res = sb.tile([P, rows, hi - lo], F32, name="res%d" % i)
+            for e in range(rows):
+                for cuts in banks:
+                    decode(on_vector, res[:, e, cuts[0] - lo : cuts[-1] - lo], t0 + e, cuts)
+            nc.sync.dma_start(out_rows[:, t0 : t0 + rows, lo:hi], res[:])

@@ -17,10 +17,12 @@ ACT = mybir.ActivationFunctionType
 P = 128
 PACK = 4
 HALF = S // 2
-CHUNKS = (128, 128, 256, 256, 256)
+CHUNKS = (128, 128, 128, 128, 256, 256)
 STORES = (
-    (False, 0, 2, ((0, 128),)),
-    (False, 2, 2, ((0, 256),)),
+    (False, 0, 1, ((0, 128),)),
+    (False, 1, 1, ((0, 128),)),
+    (False, 2, 1, ((0, 256),)),
+    (False, 3, 1, ((0, 256),)),
     (False, 0, 1, ((128, 256, 512),)),
     (False, 1, 1, ((128, 256, 512),)),
     (True, 2, 1, ((256, 768), (768, 1024))),
@@ -81,10 +83,9 @@ def tile_picked_sae8_relu_p_kernel(
         nc.scalar.activation(w1_dealt[0], w1_by_parity[:, 0], ACT.Copy)
         xs_g = sb.tile([P, S], U8, name="xs_g", align_bytes=64)
         nc.vector.tensor_copy(xs_g[:], xs[:].indirect(offs_t[:]))
-        w1_q = [sb.tile([P, H // 2], U32, name="w1_q%d" % v, align_bytes=64) for v in range(2)]
+        w1_q = {1: sb.tile([P, H // 2], U32, name="w1_q1", align_bytes=64)}
         w1_s = [sb.tile([P, H // 2], U8, name="w1_s%d" % v, align_bytes=64) for v in range(2)]
-        for v in (1, 0):
-            nc.vector.quantize_mx(out=w1_q[v][:].bitcast(FP8X4), scales=w1_s[v][:], in_=w1_bf[v][:])
+        nc.vector.quantize_mx(out=w1_q[1][:].bitcast(FP8X4), scales=w1_s[1][:], in_=w1_bf[1][:])
 
         xw_g = sb.tile([P, S], U32, name="xw_g", tag="w1_bf1", align_bytes=64)
         for h in range(2):
@@ -92,6 +93,8 @@ def tile_picked_sae8_relu_p_kernel(
                 xw_g[:, h * HALF : (h + 1) * HALF],
                 xw[:].bitcast(U32).indirect(offs_t[:, h * 16 : (h + 1) * 16]),
             )
+        w1_q[0] = sb.tile([P, H // 2], U32, name="w1_q0", tag="xw", align_bytes=64)
+        nc.vector.quantize_mx(out=w1_q[0][:].bitcast(FP8X4), scales=w1_s[0][:], in_=w1_bf[0][:])
 
         def encode(t, lo, hi):
             acc = psum.tile([P, 512], F32, name="acc")

@@ -61,7 +61,7 @@ def tile_picked_sae8_relu_p_kernel(
         nc.sync.dma_start(offs_t[:], offs)
         for q in range(4):
             nc.sync.dma_start(
-                xs[32 * q : 32 * q + 4, :].bitcast(I32), x_scales[0, 4 * q : 4 * q + 4, :].bitcast(I32)
+                xs[q:P:32, :].bitcast(I32), x_scales[0, q:16:4, :].bitcast(I32)
             )
         nc.sync.dma_start(xw[:], x_words[0].rearrange("p n r -> p (n r)").bitcast(I32))
         nc.sync.dma_start(b1_t[:], b1.rearrange("(p t) o -> p (t o)", t=PACK))

@@ -22,12 +22,12 @@ STORES = (
     (False, 0, 1, ((0, 128),)),
     (False, 1, 1, ((0, 128),)),
     (False, 2, 1, ((0, 256),)),
-    (False, 3, 1, ((0, 256),)),
-    (False, 0, 1, ((128, 256, 512),)),
-    (False, 1, 1, ((128, 256, 512),)),
+    (False, 3, 1, ((0, 256, 384),)),
+    (False, 0, 1, ((128, 384, 512),)),
+    (False, 1, 1, ((128, 384, 512),)),
     (True, 2, 1, ((256, 768), (768, 1024))),
     (False, 0, 1, ((512, 1024),)),
-    (True, 3, 1, ((256, 768), (768, 1024))),
+    (True, 3, 1, ((384, 512), (512, 1024))),
     (False, 1, 1, ((512, 1024),)),
 )
 VECTOR_COLS = 640
@@ -42,6 +42,7 @@ def tile_picked_sae8_relu_p_kernel(
     with ExitStack() as ctx:
         lists = ctx.enter_context(tc.tile_pool(name="lists", bufs=1))
         sb = ctx.enter_context(tc.tile_pool(name="sb", bufs=1))
+        shared = ctx.enter_context(tc.tile_pool(name="shared", bufs=1))
         psum = ctx.enter_context(tc.psum_pool(name="psum", bufs=8))
 
         offs_t = lists.tile([P, S // 16], U16, name="offs_t")
@@ -53,7 +54,8 @@ def tile_picked_sae8_relu_p_kernel(
         w1_rows = w1.rearrange("(p j) c -> p j c", j=PACK)
         w1_raw = sb.tile([P, PACK, H], F32, name="w1_raw")
         xw = sb.tile([P, T], I32, name="xw", align_bytes=64)
-        w2_raw = sb.tile([P, PACK, N], F32, name="w2_raw")
+        w2_room = shared.tile([P, 7, N], F32, name="w2_room", align_bytes=64, offset=0)
+        w2_raw = w2_room[:, 0:PACK, :]
         b1_t = sb.tile([P, PACK], F32, name="b1_t")
         b2_t = sb.tile([P, PACK], F32, name="b2_t")
 
@@ -66,11 +68,11 @@ def tile_picked_sae8_relu_p_kernel(
         nc.sync.dma_start(xw[:], x_words[0].rearrange("p n r -> p (n r)").bitcast(I32))
         nc.sync.dma_start(b1_t[:], b1.rearrange("(p t) o -> p (t o)", t=PACK))
         nc.sync.dma_start(held_t[:], held)
-        nc.sync.dma_start(w2_raw[:], w2.rearrange("(p j) c -> p j c", j=PACK))
+        nc.sync.dma_start(w2_raw, w2.rearrange("(p j) c -> p j c", j=PACK))
         nc.sync.dma_start(b2_t[:], b2.rearrange("(p t) o -> p (t o)", t=PACK))
 
         early = [sb.tile([P, U], F32, name="early%d" % h, align_bytes=64) for h in range(2)]
-        late = [sb.tile([P, 2 * U], F32, name="late%d" % h) for h in range(2)]
+        late = [sb.tile([P, (h + 1) * U], F32, name="late%d" % h) for h in range(2)]
         for h in range(2):
             nc.vector.memset(early[h][:], 0.0)
         for h in range(2):
@@ -96,10 +98,10 @@ def tile_picked_sae8_relu_p_kernel(
         w1_q[0] = sb.tile([P, H // 2], U32, name="w1_q0", tag="xw", align_bytes=64)
         nc.vector.quantize_mx(out=w1_q[0][:].bitcast(FP8X4), scales=w1_s[0][:], in_=w1_bf[0][:])
 
-        def encode(t, lo, hi):
+        def encode(t, lo, hi, at=None):
             acc = psum.tile([P, 512], F32, name="acc")
             cols = slice(t // 2 * P, (t // 2 + 1) * P)
-            cuts = [lo, hi] if lo % HALF == 0 else [lo, HALF, hi]
+            cuts = [lo, HALF, hi] if 0 < lo < HALF < hi else [lo, hi]
             for a, b in zip(cuts[:-1], cuts[1:]):
                 nc.tensor.matmul_mx(
                     out=acc[:, a - lo : b - lo],
@@ -110,25 +112,41 @@ def tile_picked_sae8_relu_p_kernel(
                     start=True,
                     stop=True,
                 )
-            y = sb.tile([P, hi - lo], F32, name="y%d_%d" % (t, lo))
+            if at is None:
+                y = sb.tile([P, hi - lo], F32, name="y%d_%d" % (t, lo))
+            else:
+                y = shared.tile([P, hi - lo], F32, name="y%d_%d" % (t, lo), align_bytes=64, offset=at)
             nc.scalar.activation(y[:], acc[:, 0 : hi - lo], ACT.Relu, bias=b1_t[:, t : t + 1])
             return y
 
         def scatter(window, y, lo, hi):
             nc.vector.tensor_copy(window[:].indirect(held_t[:, lo // 16 : hi // 16]), y[:])
 
-        for h, lo, hi in ((0, 0, FIRST), (1, 0, HALF), (0, FIRST, S), (1, HALF, S)):
+        for h, lo, hi in ((0, 0, FIRST), (1, 0, FIRST), (0, FIRST, S)):
             scatter(early[h], encode(2 * h + 1, lo, hi), lo, hi)
-        y_0 = encode(0, 0, S)
-        y_2 = [encode(2, h * HALF, (h + 1) * HALF) for h in range(2)]
 
-        w2_by_pair = w2_raw[:].rearrange("p j (m g e) -> p g m j e", g=2, e=2)
+        w2_by_pair = w2_raw.rearrange("p j (m g e) -> p g m j e", g=2, e=2)
         w2_bf = [sb.tile([P, 2 * N], BF16, name="w2_bf%d" % g, align_bytes=64) for g in range(2)]
         for g in range(2):
             nc.scalar.activation(
                 w2_bf[g][:].rearrange("p (e m j) -> p m j e", e=2, j=PACK), w2_by_pair[:, g], ACT.Copy
             )
-            nc.scalar.copy(late[g][:, U : 2 * U], early[g][:])
+        scatter(early[1], encode(3, FIRST, S, 8192), FIRST, S)
+        y_0 = encode(0, 0, S, 9728)
+        y_2 = [encode(2, h * HALF, (h + 1) * HALF, 11776 + 1024 * h) for h in range(2)]
+
+        starts = [sum(CHUNKS[:c]) for c in range(len(CHUNKS))]
+        z_bf = [
+            shared.tile([P, width, PACK], BF16, name="z_bf%d" % c, align_bytes=64, offset=2 * PACK * starts[c])
+            for c, width in enumerate(CHUNKS)
+        ]
+
+        def round_plane(t, window, c):
+            nc.scalar.activation(z_bf[c][:, :, t], window[:, starts[c] : starts[c] + CHUNKS[c]], ACT.Copy)
+
+        for c in range(len(CHUNKS)):
+            round_plane(1, early[0], c)
+        nc.scalar.copy(late[1][:, U : 2 * U], early[1][:])
 
         w2_q = sb.tile([P, N], U32, name="w2_q", tag="early1", align_bytes=64)
         w2_s = sb.tile([P, N], U8, name="w2_s", align_bytes=64)
@@ -155,25 +173,21 @@ def tile_picked_sae8_relu_p_kernel(
                 stop=(i == WARM - 1),
             )
 
-        starts = [sum(CHUNKS[:c]) for c in range(len(CHUNKS))]
-        pairs = [late[h][:].rearrange("p (e w) -> p w e", e=2) for h in range(2)]
-        z_bf = []
-        for c, width in enumerate(CHUNKS):
-            zb = sb.tile([P, width, PACK], BF16, name="z_bf%d" % c, align_bytes=64)
-            nc.scalar.activation(zb[:, :, 0:2], pairs[0][:, starts[c] : starts[c] + width, :], ACT.Copy)
-            z_bf.append(zb)
+        pair = late[1][:].rearrange("p (e w) -> p w e", e=2)
+        for c in range(len(CHUNKS)):
+            round_plane(0, late[0], c)
 
         for c, width in enumerate(CHUNKS):
             lo = max(VECTOR_COLS - starts[c], 0)
             if lo < width:
                 nc.scalar.activation(
-                    z_bf[c][:, lo:, 2:4], pairs[1][:, starts[c] + lo : starts[c] + width, :], ACT.Copy
+                    z_bf[c][:, lo:, 2:4], pair[:, starts[c] + lo : starts[c] + width, :], ACT.Copy
                 )
 
         def cast(c):
             hi = min(VECTOR_COLS - starts[c], CHUNKS[c])
             if hi > 0:
-                nc.vector.tensor_copy(z_bf[c][:, 0:hi, 2:4], pairs[1][:, starts[c] : starts[c] + hi, :])
+                nc.vector.tensor_copy(z_bf[c][:, 0:hi, 2:4], pair[:, starts[c] : starts[c] + hi, :])
 
         z_q = sb.tile([P, U], U32, name="z_q", align_bytes=64)
         z_s = sb.tile([P, U], U8, name="z_s", align_bytes=64)

@@ -16,23 +16,25 @@ ACT = mybir.ActivationFunctionType
 
 P = 128
 PACK = 4
+LIST_ROWS = 16
+BANK = 512
 HALF = S // 2
+SHORT = 128
 CHUNKS = (128, 128, 128, 128, 256, 256)
-STORES = (
-    (False, 0, 1, ((0, 128),)),
-    (False, 1, 1, ((0, 128),)),
-    (False, 2, 1, ((0, 256),)),
-    (False, 3, 1, ((0, 256, 384),)),
-    (False, 0, 1, ((128, 384, 512),)),
-    (False, 1, 1, ((128, 384, 512),)),
-    (True, 2, 1, ((256, 768), (768, 1024))),
-    (False, 0, 1, ((512, 1024),)),
-    (True, 3, 1, ((384, 512), (512, 1024))),
-    (False, 1, 1, ((512, 1024),)),
-)
 VECTOR_COLS = 640
-FIRST = 128
-WARM = 6
+FIRST_STORE = (128, 128, 256, 384)
+WARM_PASSES = 2
+
+
+def bank_cuts(lo, hi):
+    banks = []
+    while lo < hi:
+        cuts, end = [lo], min(lo + BANK, hi)
+        while cuts[-1] < end:
+            cuts.append(cuts[-1] + max(n for n in (512, 256, 128) if n <= end - cuts[-1]))
+        banks.append(cuts)
+        lo = end
+    return banks
 
 
 def tile_picked_sae8_relu_p_kernel(
@@ -42,41 +44,45 @@ def tile_picked_sae8_relu_p_kernel(
     with ExitStack() as ctx:
         lists = ctx.enter_context(tc.tile_pool(name="lists", bufs=1))
         sb = ctx.enter_context(tc.tile_pool(name="sb", bufs=1))
-        shared = ctx.enter_context(tc.tile_pool(name="shared", bufs=1))
+        reused = ctx.enter_context(tc.tile_pool(name="reused", bufs=1))
         psum = ctx.enter_context(tc.psum_pool(name="psum", bufs=8))
 
-        offs_t = lists.tile([P, S // 16], U16, name="offs_t")
-        held_t = lists.tile([P, S // 16], U16, name="held_t")
+        offs_t = lists.tile([P, S // LIST_ROWS], U16, name="offs_t")
+        held_t = lists.tile([P, S // LIST_ROWS], U16, name="held_t")
+
+        def entries(list_t, lo, hi):
+            return list_t[:, lo // LIST_ROWS : hi // LIST_ROWS]
 
         xs = sb.tile([P, T], U8, name="xs", align_bytes=64)
         nc.vector.memset(xs[:].bitcast(I32), 0)
 
-        w1_rows = w1.rearrange("(p j) c -> p j c", j=PACK)
+        z_bytes = 2 * PACK * U
+        late_y_bytes = 4 * ((S - SHORT) + S + S)
+        w2_room = reused.tile([P, (z_bytes + late_y_bytes) // 4], F32, name="w2_room", align_bytes=64, offset=0)
+        w2_raw = w2_room[:, 0 : PACK * N].rearrange("p (j c) -> p j c", j=PACK)
+
         w1_raw = sb.tile([P, PACK, H], F32, name="w1_raw")
         xw = sb.tile([P, T], I32, name="xw", align_bytes=64)
-        w2_room = shared.tile([P, 7, N], F32, name="w2_room", align_bytes=64, offset=0)
-        w2_raw = w2_room[:, 0:PACK, :]
         b1_t = sb.tile([P, PACK], F32, name="b1_t")
         b2_t = sb.tile([P, PACK], F32, name="b2_t")
 
-        nc.sync.dma_start(w1_raw[:], w1_rows)
+        nc.sync.dma_start(w1_raw[:], w1.rearrange("(p j) c -> p j c", j=PACK))
         nc.sync.dma_start(offs_t[:], offs)
-        for q in range(4):
-            nc.sync.dma_start(
-                xs[q:P:32, :].bitcast(I32), x_scales[0, q:16:4, :].bitcast(I32)
-            )
+        for i in range(4):
+            nc.sync.dma_start(xs[i:P:32, :].bitcast(I32), x_scales[0, i:16:4, :].bitcast(I32))
         nc.sync.dma_start(xw[:], x_words[0].rearrange("p n r -> p (n r)").bitcast(I32))
         nc.sync.dma_start(b1_t[:], b1.rearrange("(p t) o -> p (t o)", t=PACK))
         nc.sync.dma_start(held_t[:], held)
         nc.sync.dma_start(w2_raw, w2.rearrange("(p j) c -> p j c", j=PACK))
         nc.sync.dma_start(b2_t[:], b2.rearrange("(p t) o -> p (t o)", t=PACK))
 
-        early = [sb.tile([P, U], F32, name="early%d" % h, align_bytes=64) for h in range(2)]
-        late = [sb.tile([P, (h + 1) * U], F32, name="late%d" % h) for h in range(2)]
-        for h in range(2):
-            nc.vector.memset(early[h][:], 0.0)
-        for h in range(2):
-            nc.scalar.copy(late[h][:, 0:U], early[0][:])
+        window = {t: sb.tile([P, U], F32, name="window%d" % t, align_bytes=64) for t in (1, 3)}
+        window[0] = sb.tile([P, U], F32, name="window0")
+        window[2] = sb.tile([P, 2 * U], F32, name="window2")
+        for t in (1, 3):
+            nc.vector.memset(window[t][:], 0.0)
+        for t in (0, 2):
+            nc.scalar.copy(window[t][:, 0:U], window[1][:])
 
         w1_by_parity = w1_raw[:].rearrange("p j (m u v) -> p v m j u", u=2, v=2)
         w1_bf = [sb.tile([P, 2 * H], BF16, name="w1_bf%d" % v, align_bytes=64) for v in range(2)]
@@ -90,18 +96,15 @@ def tile_picked_sae8_relu_p_kernel(
         nc.vector.quantize_mx(out=w1_q[1][:].bitcast(FP8X4), scales=w1_s[1][:], in_=w1_bf[1][:])
 
         xw_g = sb.tile([P, S], U32, name="xw_g", tag="w1_bf1", align_bytes=64)
-        for h in range(2):
-            nc.vector.tensor_copy(
-                xw_g[:, h * HALF : (h + 1) * HALF],
-                xw[:].bitcast(U32).indirect(offs_t[:, h * 16 : (h + 1) * 16]),
-            )
+        for lo in (0, HALF):
+            nc.vector.tensor_copy(xw_g[:, lo : lo + HALF], xw[:].bitcast(U32).indirect(entries(offs_t, lo, lo + HALF)))
         w1_q[0] = sb.tile([P, H // 2], U32, name="w1_q0", tag="xw", align_bytes=64)
         nc.vector.quantize_mx(out=w1_q[0][:].bitcast(FP8X4), scales=w1_s[0][:], in_=w1_bf[0][:])
 
         def encode(t, lo, hi, at=None):
-            acc = psum.tile([P, 512], F32, name="acc")
+            acc = psum.tile([P, BANK], F32, name="acc")
             cols = slice(t // 2 * P, (t // 2 + 1) * P)
-            cuts = [lo, HALF, hi] if 0 < lo < HALF < hi else [lo, hi]
+            cuts = [lo, hi] if hi - lo in (SHORT, S) else [lo, HALF, hi]
             for a, b in zip(cuts[:-1], cuts[1:]):
                 nc.tensor.matmul_mx(
                     out=acc[:, a - lo : b - lo],
@@ -115,15 +118,15 @@ def tile_picked_sae8_relu_p_kernel(
             if at is None:
                 y = sb.tile([P, hi - lo], F32, name="y%d_%d" % (t, lo))
             else:
-                y = shared.tile([P, hi - lo], F32, name="y%d_%d" % (t, lo), align_bytes=64, offset=at)
+                y = reused.tile([P, hi - lo], F32, name="y%d_%d" % (t, lo), align_bytes=64, offset=at)
             nc.scalar.activation(y[:], acc[:, 0 : hi - lo], ACT.Relu, bias=b1_t[:, t : t + 1])
             return y
 
-        def scatter(window, y, lo, hi):
-            nc.vector.tensor_copy(window[:].indirect(held_t[:, lo // 16 : hi // 16]), y[:])
+        def scatter(t, y, lo, hi):
+            nc.vector.tensor_copy(window[t][:].indirect(entries(held_t, lo, hi)), y[:])
 
-        for h, lo, hi in ((0, 0, FIRST), (1, 0, FIRST), (0, FIRST, S)):
-            scatter(early[h], encode(2 * h + 1, lo, hi), lo, hi)
+        for t, lo, hi in ((1, 0, SHORT), (3, 0, SHORT), (1, SHORT, S)):
+            scatter(t, encode(t, lo, hi), lo, hi)
 
         w2_by_pair = w2_raw.rearrange("p j (m g e) -> p g m j e", g=2, e=2)
         w2_bf = [sb.tile([P, 2 * N], BF16, name="w2_bf%d" % g, align_bytes=64) for g in range(2)]
@@ -131,60 +134,61 @@ def tile_picked_sae8_relu_p_kernel(
             nc.scalar.activation(
                 w2_bf[g][:].rearrange("p (e m j) -> p m j e", e=2, j=PACK), w2_by_pair[:, g], ACT.Copy
             )
-        scatter(early[1], encode(3, FIRST, S, 8192), FIRST, S)
-        y_0 = encode(0, 0, S, 9728)
-        y_2 = [encode(2, h * HALF, (h + 1) * HALF, 11776 + 1024 * h) for h in range(2)]
+
+        y_at = z_bytes
+        scatter(3, encode(3, SHORT, S, y_at), SHORT, S)
+        y_at = y_at + 4 * (S - SHORT)
+        y_0 = encode(0, 0, S, y_at)
+        y_at = y_at + 4 * S
+        y_2 = [encode(2, 0, S - SHORT, y_at), encode(2, S - SHORT, S, y_at + 4 * (S - SHORT))]
 
         starts = [sum(CHUNKS[:c]) for c in range(len(CHUNKS))]
         z_bf = [
-            shared.tile([P, width, PACK], BF16, name="z_bf%d" % c, align_bytes=64, offset=2 * PACK * starts[c])
+            reused.tile([P, width, PACK], BF16, name="z_bf%d" % c, align_bytes=64, offset=2 * PACK * starts[c])
             for c, width in enumerate(CHUNKS)
         ]
 
-        def round_plane(t, window, c):
-            nc.scalar.activation(z_bf[c][:, :, t], window[:, starts[c] : starts[c] + CHUNKS[c]], ACT.Copy)
+        def round_plane(t):
+            for c, width in enumerate(CHUNKS):
+                nc.scalar.activation(z_bf[c][:, :, t], window[t][:, starts[c] : starts[c] + width], ACT.Copy)
 
-        for c in range(len(CHUNKS)):
-            round_plane(1, early[0], c)
-        nc.scalar.copy(late[1][:, U : 2 * U], early[1][:])
+        round_plane(1)
+        nc.scalar.copy(window[2][:, U : 2 * U], window[3][:])
 
-        w2_q = sb.tile([P, N], U32, name="w2_q", tag="early1", align_bytes=64)
+        w2_q = sb.tile([P, N], U32, name="w2_q", tag="window3", align_bytes=64)
         w2_s = sb.tile([P, N], U8, name="w2_s", align_bytes=64)
 
         def quantise_w2(g):
             cols = slice(g * N // 2, (g + 1) * N // 2)
             nc.vector.quantize_mx(out=w2_q[:, cols].bitcast(FP8X4), scales=w2_s[:, cols], in_=w2_bf[g][:])
 
-        scatter(late[0], y_0, 0, S)
-        scatter(late[1], y_2[0], 0, HALF)
+        scatter(0, y_0, 0, S)
+        scatter(2, y_2[0], 0, S - SHORT)
         quantise_w2(0)
-        scatter(late[1], y_2[1], HALF, S)
+        scatter(2, y_2[1], S - SHORT, S)
         quantise_w2(1)
 
-        warm = psum.tile([P, 512], F32, name="acc")
-        for i in range(WARM):
+        warm = psum.tile([P, BANK], F32, name="acc")
+        for i in range(WARM_PASSES):
             nc.tensor.matmul_mx(
-                out=warm[:, 0:HALF],
+                out=warm[:],
                 lhsT=w2_q[:, 0:P].bitcast(FP8X4),
                 lhsT_scale=w2_s[:, 0:P],
-                rhs=w2_q[:, 0:HALF].bitcast(FP8X4),
-                rhs_scale=w2_s[:, 0:HALF],
+                rhs=xw_g[:].bitcast(FP8X4),
+                rhs_scale=xs_g[:],
                 start=(i == 0),
-                stop=(i == WARM - 1),
+                stop=(i == WARM_PASSES - 1),
             )
 
-        pair = late[1][:].rearrange("p (e w) -> p w e", e=2)
-        for c in range(len(CHUNKS)):
-            round_plane(0, late[0], c)
+        round_plane(0)
 
+        pair = window[2][:].rearrange("p (e w) -> p w e", e=2)
         for c, width in enumerate(CHUNKS):
             lo = max(VECTOR_COLS - starts[c], 0)
             if lo < width:
-                nc.scalar.activation(
-                    z_bf[c][:, lo:, 2:4], pair[:, starts[c] + lo : starts[c] + width, :], ACT.Copy
-                )
+                nc.scalar.activation(z_bf[c][:, lo:, 2:4], pair[:, starts[c] + lo : starts[c] + width, :], ACT.Copy)
 
-        def cast(c):
+        def round_pair_on_vector(c):
             hi = min(VECTOR_COLS - starts[c], CHUNKS[c])
             if hi > 0:
                 nc.vector.tensor_copy(z_bf[c][:, 0:hi, 2:4], pair[:, starts[c] : starts[c] + hi, :])
@@ -192,42 +196,42 @@ def tile_picked_sae8_relu_p_kernel(
         z_q = sb.tile([P, U], U32, name="z_q", align_bytes=64)
         z_s = sb.tile([P, U], U8, name="z_s", align_bytes=64)
 
-        def quantise(c):
-            cols = slice(starts[c], starts[c] + CHUNKS[c])
+        round_pair_on_vector(0)
+        for c, width in enumerate(CHUNKS):
+            if c + 1 < len(CHUNKS):
+                round_pair_on_vector(c + 1)
+            cols = slice(starts[c], starts[c] + width)
             nc.vector.quantize_mx(
                 out=z_q[:, cols].bitcast(FP8X4), scales=z_s[:, cols], in_=z_bf[c][:].rearrange("p w t -> p (w t)")
             )
 
-        cast(0)
-        for c in range(len(CHUNKS)):
-            if c + 1 < len(CHUNKS):
-                cast(c + 1)
-            quantise(c)
+        out_planes = out.rearrange("(p t) w -> p t w", t=PACK)
 
-        out_rows = out.rearrange("(p t) w -> p t w", t=PACK)
+        def decode(t, lo, hi, on_vector):
+            res = sb.tile([P, hi - lo], F32, name="res%d_%d" % (t, lo))
+            for cuts in bank_cuts(lo, hi):
+                acc = psum.tile([P, BANK], F32, name="acc")
+                for a, b in zip(cuts[:-1], cuts[1:]):
+                    nc.tensor.matmul_mx(
+                        out=acc[:, a - cuts[0] : b - cuts[0]],
+                        lhsT=w2_q[:, t * P : (t + 1) * P].bitcast(FP8X4),
+                        lhsT_scale=w2_s[:, t * P : (t + 1) * P],
+                        rhs=z_q[:, a:b].bitcast(FP8X4),
+                        rhs_scale=z_s[:, a:b],
+                        start=True,
+                        stop=True,
+                    )
+                sums, part = acc[:, 0 : cuts[-1] - cuts[0]], res[:, cuts[0] - lo : cuts[-1] - lo]
+                if on_vector:
+                    nc.vector.tensor_scalar_add(part, sums, b2_t[:, t : t + 1])
+                else:
+                    nc.scalar.activation(part, sums, ACT.Identity, bias=b2_t[:, t : t + 1])
+            nc.sync.dma_start(out_planes[:, t, lo:hi], res[:])
 
-        def decode(on_vector, res, t, cuts):
-            acc = psum.tile([P, 512], F32, name="acc")
-            for a, b in zip(cuts[:-1], cuts[1:]):
-                nc.tensor.matmul_mx(
-                    out=acc[:, a - cuts[0] : b - cuts[0]],
-                    lhsT=w2_q[:, t * P : (t + 1) * P].bitcast(FP8X4),
-                    lhsT_scale=w2_s[:, t * P : (t + 1) * P],
-                    rhs=z_q[:, a:b].bitcast(FP8X4),
-                    rhs_scale=z_s[:, a:b],
-                    start=True,
-                    stop=True,
-                )
-            width = cuts[-1] - cuts[0]
-            if on_vector:
-                nc.vector.tensor_scalar_add(res, acc[:, 0:width], b2_t[:, t : t + 1])
-            else:
-                nc.scalar.activation(res, acc[:, 0:width], ACT.Identity, bias=b2_t[:, t : t + 1])
-
-        for i, (on_vector, t0, rows, banks) in enumerate(STORES):
-            lo, hi = banks[0][0], banks[-1][-1]
-            res = sb.tile([P, rows, hi - lo], F32, name="res%d" % i)
-            for e in range(rows):
-                for cuts in banks:
-                    decode(on_vector, res[:, e, cuts[0] - lo : cuts[-1] - lo], t0 + e, cuts)
-            nc.sync.dma_start(out_rows[:, t0 : t0 + rows, lo:hi], res[:])
+        for t in range(PACK):
+            decode(t, 0, FIRST_STORE[t], False)
+        for t in (0, 1):
+            decode(t, FIRST_STORE[t], U // 2, False)
+        for t in (0, 1):
+            decode(t + 2, FIRST_STORE[t + 2], U, True)
+            decode(t, U // 2, U, False)

@@ -20,8 +20,9 @@ LIST_ROWS = 16
 BANK = 512
 HALF = S // 2
 SHORT = 128
+THIRD_FIRST = 192
 CHUNKS = (128, 128, 128, 128, 256, 256)
-VECTOR_COLS = 640
+VECTOR_COLS = 576
 FIRST_STORE = (128, 128, 256, 384)
 WARM_PASSES = 2
 
@@ -31,7 +32,7 @@ def bank_cuts(lo, hi):
     while lo < hi:
         cuts, end = [lo], min(lo + BANK, hi)
         while cuts[-1] < end:
-            cuts.append(cuts[-1] + max(n for n in (512, 256, 128) if n <= end - cuts[-1]))
+            cuts.append(cuts[-1] + max(n for n in (512, 256, 128, 64) if n <= end - cuts[-1]))
         banks.append(cuts)
         lo = end
     return banks
@@ -57,14 +58,15 @@ def tile_picked_sae8_relu_p_kernel(
         nc.vector.memset(xs[:].bitcast(I32), 0)
 
         z_bytes = 2 * PACK * U
-        late_y_bytes = 4 * ((S - SHORT) + S + S)
+        late_y_bytes = 4 * ((S - THIRD_FIRST) + S + S)
         w2_room = reused.tile([P, (z_bytes + late_y_bytes) // 4], F32, name="w2_room", align_bytes=64, offset=0)
-        w2_raw = w2_room[:, 0 : PACK * N].rearrange("p (j c) -> p j c", j=PACK)
+        w2_first = sb.tile([P, PACK * N // 2], F32, name="w2_first")
+        w2_raw = [half[:, 0 : PACK * N // 2].rearrange("p (j c) -> p j c", j=PACK) for half in (w2_first, w2_room)]
 
         w1_raw = sb.tile([P, PACK, H], F32, name="w1_raw")
         xw = sb.tile([P, T], I32, name="xw", align_bytes=64)
         b1_t = sb.tile([P, PACK], F32, name="b1_t")
-        b2_t = sb.tile([P, PACK], F32, name="b2_t")
+        b2_t = sb.tile([P, 2, 2], F32, name="b2_t")
 
         nc.sync.dma_start(w1_raw[:], w1.rearrange("(p j) c -> p j c", j=PACK))
         nc.sync.dma_start(offs_t[:], offs)
@@ -73,8 +75,10 @@ def tile_picked_sae8_relu_p_kernel(
         nc.sync.dma_start(xw[:], x_words[0].rearrange("p n r -> p (n r)").bitcast(I32))
         nc.sync.dma_start(b1_t[:], b1.rearrange("(p t) o -> p (t o)", t=PACK))
         nc.sync.dma_start(held_t[:], held)
-        nc.sync.dma_start(w2_raw, w2.rearrange("(p j) c -> p j c", j=PACK))
-        nc.sync.dma_start(b2_t[:], b2.rearrange("(p t) o -> p (t o)", t=PACK))
+        w2_rows = w2.rearrange("(p j) c -> p j c", j=PACK)
+        for g in range(2):
+            nc.sync.dma_start(w2_raw[g], w2_rows[:, :, g * N // 2 : (g + 1) * N // 2])
+        nc.sync.dma_start(b2_t[:], b2.rearrange("(g p e) o -> p g (e o)", g=2, e=2))
 
         window = {t: sb.tile([P, U], F32, name="window%d" % t, align_bytes=64) for t in (1, 3)}
         window[0] = sb.tile([P, U], F32, name="window0")
@@ -104,7 +108,7 @@ def tile_picked_sae8_relu_p_kernel(
         def encode(t, lo, hi, at=None):
             acc = psum.tile([P, BANK], F32, name="acc")
             cols = slice(t // 2 * P, (t // 2 + 1) * P)
-            cuts = [lo, hi] if hi - lo in (SHORT, S) else [lo, HALF, hi]
+            cuts = bank_cuts(lo, hi)[0]
             for a, b in zip(cuts[:-1], cuts[1:]):
                 nc.tensor.matmul_mx(
                     out=acc[:, a - lo : b - lo],
@@ -125,19 +129,20 @@ def tile_picked_sae8_relu_p_kernel(
         def scatter(t, y, lo, hi):
             nc.vector.tensor_copy(window[t][:].indirect(entries(held_t, lo, hi)), y[:])
 
-        for t, lo, hi in ((1, 0, SHORT), (3, 0, SHORT), (1, SHORT, S)):
+        for t, lo, hi in ((1, 0, SHORT), (3, 0, THIRD_FIRST), (1, SHORT, S)):
             scatter(t, encode(t, lo, hi), lo, hi)
 
-        w2_by_pair = w2_raw.rearrange("p j (m g e) -> p g m j e", g=2, e=2)
         w2_bf = [sb.tile([P, 2 * N], BF16, name="w2_bf%d" % g, align_bytes=64) for g in range(2)]
         for g in range(2):
             nc.scalar.activation(
-                w2_bf[g][:].rearrange("p (e m j) -> p m j e", e=2, j=PACK), w2_by_pair[:, g], ACT.Copy
+                w2_bf[g][:].rearrange("p (e m j) -> p m j e", e=2, j=PACK),
+                w2_raw[g].rearrange("p j (m e) -> p m j e", e=2),
+                ACT.Copy,
             )
 
         y_at = z_bytes
-        scatter(3, encode(3, SHORT, S, y_at), SHORT, S)
-        y_at = y_at + 4 * (S - SHORT)
+        scatter(3, encode(3, THIRD_FIRST, S, y_at), THIRD_FIRST, S)
+        y_at = y_at + 4 * (S - THIRD_FIRST)
         y_0 = encode(0, 0, S, y_at)
         y_at = y_at + 4 * S
         y_2 = [encode(2, 0, S - SHORT, y_at), encode(2, S - SHORT, S, y_at + 4 * (S - SHORT))]
@@ -205,9 +210,10 @@ def tile_picked_sae8_relu_p_kernel(
                 out=z_q[:, cols].bitcast(FP8X4), scales=z_s[:, cols], in_=z_bf[c][:].rearrange("p w t -> p (w t)")
             )
 
-        out_planes = out.rearrange("(p t) w -> p t w", t=PACK)
+        out_planes = out.rearrange("(g p e) w -> p g e w", g=2, e=2)
 
         def decode(t, lo, hi, on_vector):
+            bias = b2_t[:, t // 2, t % 2 : t % 2 + 1]
             res = sb.tile([P, hi - lo], F32, name="res%d_%d" % (t, lo))
             for cuts in bank_cuts(lo, hi):
                 acc = psum.tile([P, BANK], F32, name="acc")
@@ -223,10 +229,10 @@ def tile_picked_sae8_relu_p_kernel(
                     )
                 sums, part = acc[:, 0 : cuts[-1] - cuts[0]], res[:, cuts[0] - lo : cuts[-1] - lo]
                 if on_vector:
-                    nc.vector.tensor_scalar_add(part, sums, b2_t[:, t : t + 1])
+                    nc.vector.tensor_scalar_add(part, sums, bias)
                 else:
-                    nc.scalar.activation(part, sums, ACT.Identity, bias=b2_t[:, t : t + 1])
-            nc.sync.dma_start(out_planes[:, t, lo:hi], res[:])
+                    nc.scalar.activation(part, sums, ACT.Identity, bias=bias)
+            nc.sync.dma_start(out_planes[:, t // 2, t % 2, lo:hi], res[:])
 
         for t in range(PACK):
             decode(t, 0, FIRST_STORE[t], False)

@@ -18,13 +18,15 @@ P = 128
 PACK = 4
 LIST_ROWS = 16
 BANK = 512
+BANKS = 8
 HALF = S // 2
 SHORT = 128
 THIRD_FIRST = 192
 CHUNKS = (128, 128, 128, 128, 256, 256)
-VECTOR_COLS = 576
+VECTOR_COLS = 768
 FIRST_STORE = (128, 128, 256, 384)
 WARM_PASSES = 2
+ROUND_FIRST = 2
 
 
 def bank_cuts(lo, hi):
@@ -46,7 +48,13 @@ def tile_picked_sae8_relu_p_kernel(
         lists = ctx.enter_context(tc.tile_pool(name="lists", bufs=1))
         sb = ctx.enter_context(tc.tile_pool(name="sb", bufs=1))
         reused = ctx.enter_context(tc.tile_pool(name="reused", bufs=1))
-        psum = ctx.enter_context(tc.psum_pool(name="psum", bufs=8))
+        psum = ctx.enter_context(tc.psum_pool(name="psum", bufs=1))
+        taken = []
+
+        def next_bank():
+            taken.append(len(taken) % BANKS)
+            return psum.tile([P, BANK], F32, name="bank%d" % taken[-1])
+
 
         offs_t = lists.tile([P, S // LIST_ROWS], U16, name="offs_t")
         held_t = lists.tile([P, S // LIST_ROWS], U16, name="held_t")
@@ -58,14 +66,14 @@ def tile_picked_sae8_relu_p_kernel(
         nc.vector.memset(xs[:].bitcast(I32), 0)
 
         z_bytes = 2 * PACK * U
-        late_y_bytes = 4 * ((S - THIRD_FIRST) + S + S)
+        late_y_bytes = 4 * ((S - THIRD_FIRST) + S + S - SHORT)
         w2_room = reused.tile([P, (z_bytes + late_y_bytes) // 4], F32, name="w2_room", align_bytes=64, offset=0)
         w2_first = sb.tile([P, PACK * N // 2], F32, name="w2_first")
         w2_raw = [half[:, 0 : PACK * N // 2].rearrange("p (j c) -> p j c", j=PACK) for half in (w2_first, w2_room)]
 
         w1_raw = sb.tile([P, PACK, H], F32, name="w1_raw")
         xw = sb.tile([P, T], I32, name="xw", align_bytes=64)
-        b1_t = sb.tile([P, PACK], F32, name="b1_t")
+        b1_t = sb.tile([P, PACK], F32, name="b1_t", align_bytes=64)
         b2_t = sb.tile([P, 2, 2], F32, name="b2_t")
 
         nc.sync.dma_start(w1_raw[:], w1.rearrange("(p j) c -> p j c", j=PACK))
@@ -106,7 +114,7 @@ def tile_picked_sae8_relu_p_kernel(
         nc.vector.quantize_mx(out=w1_q[0][:].bitcast(FP8X4), scales=w1_s[0][:], in_=w1_bf[0][:])
 
         def encode(t, lo, hi, at=None):
-            acc = psum.tile([P, BANK], F32, name="acc")
+            acc = next_bank()
             cols = slice(t // 2 * P, (t // 2 + 1) * P)
             cuts = bank_cuts(lo, hi)[0]
             for a, b in zip(cuts[:-1], cuts[1:]):
@@ -119,7 +127,9 @@ def tile_picked_sae8_relu_p_kernel(
                     start=True,
                     stop=True,
                 )
-            if at is None:
+            if hi == S and t == 2:
+                y = sb.tile([P, hi - lo], F32, name="y_last", tag="window1", align_bytes=64)
+            elif at is None:
                 y = sb.tile([P, hi - lo], F32, name="y%d_%d" % (t, lo))
             else:
                 y = reused.tile([P, hi - lo], F32, name="y%d_%d" % (t, lo), align_bytes=64, offset=at)
@@ -129,8 +139,10 @@ def tile_picked_sae8_relu_p_kernel(
         def scatter(t, y, lo, hi):
             nc.vector.tensor_copy(window[t][:].indirect(entries(held_t, lo, hi)), y[:])
 
-        for t, lo, hi in ((1, 0, SHORT), (3, 0, THIRD_FIRST), (1, SHORT, S)):
+        for t, lo, hi in ((3, 0, SHORT), (1, 0, THIRD_FIRST), (3, SHORT, S)):
             scatter(t, encode(t, lo, hi), lo, hi)
+
+        nc.sync.dma_start(window[2][:, U : 2 * U], window[3][:])
 
         w2_bf = [sb.tile([P, 2 * N], BF16, name="w2_bf%d" % g, align_bytes=64) for g in range(2)]
         for g in range(2):
@@ -141,11 +153,11 @@ def tile_picked_sae8_relu_p_kernel(
             )
 
         y_at = z_bytes
-        scatter(3, encode(3, THIRD_FIRST, S, y_at), THIRD_FIRST, S)
+        scatter(1, encode(1, THIRD_FIRST, S, y_at), THIRD_FIRST, S)
         y_at = y_at + 4 * (S - THIRD_FIRST)
         y_0 = encode(0, 0, S, y_at)
         y_at = y_at + 4 * S
-        y_2 = [encode(2, 0, S - SHORT, y_at), encode(2, S - SHORT, S, y_at + 4 * (S - SHORT))]
+        y_2 = encode(2, 0, S - SHORT, y_at)
 
         starts = [sum(CHUNKS[:c]) for c in range(len(CHUNKS))]
         z_bf = [
@@ -153,31 +165,37 @@ def tile_picked_sae8_relu_p_kernel(
             for c, width in enumerate(CHUNKS)
         ]
 
-        def round_plane(t):
-            for c, width in enumerate(CHUNKS):
-                nc.scalar.activation(z_bf[c][:, :, t], window[t][:, starts[c] : starts[c] + width], ACT.Copy)
+        def round_plane(t, chunks):
+            for c in chunks:
+                nc.scalar.activation(z_bf[c][:, :, t], window[t][:, starts[c] : starts[c] + CHUNKS[c]], ACT.Copy)
 
-        round_plane(1)
-        nc.scalar.copy(window[2][:, U : 2 * U], window[3][:])
+        round_plane(1, range(len(CHUNKS)))
 
-        w2_q = sb.tile([P, N], U32, name="w2_q", tag="window3", align_bytes=64)
+        w2_q = {}
         w2_s = sb.tile([P, N], U8, name="w2_s", align_bytes=64)
 
-        def quantise_w2(g):
-            cols = slice(g * N // 2, (g + 1) * N // 2)
-            nc.vector.quantize_mx(out=w2_q[:, cols].bitcast(FP8X4), scales=w2_s[:, cols], in_=w2_bf[g][:])
+        def quantise_w2(lo, hi):
+            g = lo // 2
+            nc.vector.quantize_mx(
+                out=w2_q[g][:, (lo - 2 * g) * P : (hi - 2 * g) * P].bitcast(FP8X4),
+                scales=w2_s[:, lo * P : hi * P],
+                in_=w2_bf[g][:, (lo - 2 * g) * P * PACK : (hi - 2 * g) * P * PACK],
+            )
 
         scatter(0, y_0, 0, S)
-        scatter(2, y_2[0], 0, S - SHORT)
-        quantise_w2(0)
-        scatter(2, y_2[1], S - SHORT, S)
-        quantise_w2(1)
+        scatter(2, y_2, 0, S - SHORT)
+        round_plane(0, range(ROUND_FIRST))
+        y_last = encode(2, S - SHORT, S)
+        w2_q[0] = sb.tile([P, N // 2], U32, name="w2_q0", tag="b1_t", align_bytes=64)
+        quantise_w2(0, 2)
+        scatter(2, y_last, S - SHORT, S)
+        w2_q[1] = sb.tile([P, N // 2], U32, name="w2_q1", tag="window1", align_bytes=64)
 
-        warm = psum.tile([P, BANK], F32, name="acc")
+        warm = next_bank()
         for i in range(WARM_PASSES):
             nc.tensor.matmul_mx(
                 out=warm[:],
-                lhsT=w2_q[:, 0:P].bitcast(FP8X4),
+                lhsT=w2_q[0][:, 0:P].bitcast(FP8X4),
                 lhsT_scale=w2_s[:, 0:P],
                 rhs=xw_g[:].bitcast(FP8X4),
                 rhs_scale=xs_g[:],
@@ -185,7 +203,7 @@ def tile_picked_sae8_relu_p_kernel(
                 stop=(i == WARM_PASSES - 1),
             )
 
-        round_plane(0)
+        round_plane(0, range(ROUND_FIRST, len(CHUNKS)))
 
         pair = window[2][:].rearrange("p (e w) -> p w e", e=2)
         for c, width in enumerate(CHUNKS):
@@ -201,43 +219,83 @@ def tile_picked_sae8_relu_p_kernel(
         z_q = sb.tile([P, U], U32, name="z_q", align_bytes=64)
         z_s = sb.tile([P, U], U8, name="z_s", align_bytes=64)
 
-        round_pair_on_vector(0)
-        for c, width in enumerate(CHUNKS):
-            if c + 1 < len(CHUNKS):
-                round_pair_on_vector(c + 1)
-            cols = slice(starts[c], starts[c] + width)
+        def quantise_z(c):
+            cols = slice(starts[c], starts[c] + CHUNKS[c])
             nc.vector.quantize_mx(
                 out=z_q[:, cols].bitcast(FP8X4), scales=z_s[:, cols], in_=z_bf[c][:].rearrange("p w t -> p (w t)")
             )
 
+        for c in (0, 2):
+            round_pair_on_vector(c)
+            round_pair_on_vector(c + 1)
+            quantise_w2(2 + c // 2, 3 + c // 2)
+            quantise_z(c)
+            quantise_z(c + 1)
+        round_pair_on_vector(4)
+        quantise_z(5)
+        quantise_z(4)
+
         out_planes = out.rearrange("(g p e) w -> p g e w", g=2, e=2)
 
-        def decode(t, lo, hi, on_vector):
-            bias = b2_t[:, t // 2, t % 2 : t % 2 + 1]
-            res = sb.tile([P, hi - lo], F32, name="res%d_%d" % (t, lo))
-            for cuts in bank_cuts(lo, hi):
-                acc = psum.tile([P, BANK], F32, name="acc")
-                for a, b in zip(cuts[:-1], cuts[1:]):
-                    nc.tensor.matmul_mx(
-                        out=acc[:, a - cuts[0] : b - cuts[0]],
-                        lhsT=w2_q[:, t * P : (t + 1) * P].bitcast(FP8X4),
-                        lhsT_scale=w2_s[:, t * P : (t + 1) * P],
-                        rhs=z_q[:, a:b].bitcast(FP8X4),
-                        rhs_scale=z_s[:, a:b],
-                        start=True,
-                        stop=True,
-                    )
-                sums, part = acc[:, 0 : cuts[-1] - cuts[0]], res[:, cuts[0] - lo : cuts[-1] - lo]
-                if on_vector:
-                    nc.vector.tensor_scalar_add(part, sums, bias)
-                else:
-                    nc.scalar.activation(part, sums, ACT.Identity, bias=bias)
-            nc.sync.dma_start(out_planes[:, t // 2, t % 2, lo:hi], res[:])
+        stores = ((0, 128, 512, U), (0, 256, 512, U), (0, 256, U), (0, 256, U))
+        res = {
+            (t, lo): sb.tile([P, hi - lo], F32, name="res%d_%d" % (t, lo))
+            for t in range(PACK)
+            for lo, hi in zip(stores[t][:-1], stores[t][1:])
+        }
+        left = {(t, lo): hi - lo for t in range(PACK) for lo, hi in zip(stores[t][:-1], stores[t][1:])}
+        sums = {}
 
-        for t in range(PACK):
-            decode(t, 0, FIRST_STORE[t], False)
-        for t in (0, 1):
-            decode(t, FIRST_STORE[t], U // 2, False)
-        for t in (0, 1):
-            decode(t + 2, FIRST_STORE[t + 2], U, True)
-            decode(t, U // 2, U, False)
+        def multiply(t, lo, hi):
+            sums[t, lo] = next_bank()
+            cuts = bank_cuts(lo, hi)[0]
+            for a, b in zip(cuts[:-1], cuts[1:]):
+                nc.tensor.matmul_mx(
+                    out=sums[t, lo][:, a - lo : b - lo],
+                    lhsT=w2_q[t // 2][:, t % 2 * P : (t % 2 + 1) * P].bitcast(FP8X4),
+                    lhsT_scale=w2_s[:, t * P : (t + 1) * P],
+                    rhs=z_q[:, a:b].bitcast(FP8X4),
+                    rhs_scale=z_s[:, a:b],
+                    start=True,
+                    stop=True,
+                )
+
+        def leave(t, lo, hi, on_vector):
+            bias = b2_t[:, t // 2, t % 2 : t % 2 + 1]
+            first = max(cut for cut in stores[t] if cut <= lo)
+            part = res[t, first][:, lo - first : hi - first]
+            if on_vector:
+                nc.vector.tensor_scalar_add(part, sums[t, lo][:, 0 : hi - lo], bias)
+            else:
+                nc.scalar.activation(part, sums[t, lo][:, 0 : hi - lo], ACT.Identity, bias=bias)
+            left[t, first] = left[t, first] - (hi - lo)
+            if left[t, first] == 0:
+                last = min(cut for cut in stores[t] if cut > first)
+                nc.sync.dma_start(out_planes[:, t // 2, t % 2, first:last], res[t, first][:])
+
+        multiply(0, 0, 128)
+        leave(0, 0, 128, False)
+        multiply(1, 0, 256)
+        leave(1, 0, 256, False)
+        multiply(2, 0, 256)
+        leave(2, 0, 256, False)
+        multiply(3, 0, 256)
+        leave(3, 0, 256, False)
+        multiply(0, 128, 512)
+        leave(0, 128, 512, False)
+        multiply(1, 256, 512)
+        leave(1, 256, 512, False)
+        multiply(2, 256, 512)
+        multiply(3, 256, 512)
+        multiply(2, 768, 1024)
+        leave(2, 256, 512, False)
+        leave(2, 768, 1024, True)
+        multiply(2, 512, 768)
+        multiply(3, 512, 1024)
+        multiply(0, 512, 1024)
+        multiply(1, 512, 1024)
+        leave(3, 256, 512, False)
+        leave(2, 512, 768, True)
+        leave(3, 512, 1024, False)
+        leave(0, 512, 1024, True)
+        leave(1, 512, 1024, False)

@@ -22,8 +22,8 @@ BANKS = 8
 HALF = S // 2
 SHORT = 128
 THIRD_FIRST = 192
-CHUNKS = (128, 128, 128, 128, 256, 256)
-VECTOR_COLS = 768
+CHUNKS = (128, 128, 128, 256, 128, 256)
+SCALAR_CHUNKS = (2, 3)
 FIRST_STORE = (128, 128, 256, 384)
 WARM_PASSES = 2
 ROUND_FIRST = 2
@@ -142,7 +142,8 @@ def tile_picked_sae8_relu_p_kernel(
         for t, lo, hi in ((3, 0, SHORT), (1, 0, THIRD_FIRST), (3, SHORT, S)):
             scatter(t, encode(t, lo, hi), lo, hi)
 
-        nc.sync.dma_start(window[2][:, U : 2 * U], window[3][:])
+        for lo, hi in ((0, 256), (640, U)):
+            nc.sync.dma_start(window[2][:, U + lo : U + hi], window[3][:, lo:hi])
 
         w2_bf = [sb.tile([P, 2 * N], BF16, name="w2_bf%d" % g, align_bytes=64) for g in range(2)]
         for g in range(2):
@@ -169,6 +170,7 @@ def tile_picked_sae8_relu_p_kernel(
             for c in chunks:
                 nc.scalar.activation(z_bf[c][:, :, t], window[t][:, starts[c] : starts[c] + CHUNKS[c]], ACT.Copy)
 
+        round_plane(3, SCALAR_CHUNKS)
         round_plane(1, range(len(CHUNKS)))
 
         w2_q = {}
@@ -187,8 +189,9 @@ def tile_picked_sae8_relu_p_kernel(
         round_plane(0, range(ROUND_FIRST))
         y_last = encode(2, S - SHORT, S)
         w2_q[0] = sb.tile([P, N // 2], U32, name="w2_q0", tag="b1_t", align_bytes=64)
-        quantise_w2(0, 2)
+        quantise_w2(0, 1)
         scatter(2, y_last, S - SHORT, S)
+        quantise_w2(1, 2)
         w2_q[1] = sb.tile([P, N // 2], U32, name="w2_q1", tag="window1", align_bytes=64)
 
         warm = next_bank()
@@ -206,15 +209,10 @@ def tile_picked_sae8_relu_p_kernel(
         round_plane(0, range(ROUND_FIRST, len(CHUNKS)))
 
         pair = window[2][:].rearrange("p (e w) -> p w e", e=2)
-        for c, width in enumerate(CHUNKS):
-            lo = max(VECTOR_COLS - starts[c], 0)
-            if lo < width:
-                nc.scalar.activation(z_bf[c][:, lo:, 2:4], pair[:, starts[c] + lo : starts[c] + width, :], ACT.Copy)
+        round_plane(2, SCALAR_CHUNKS)
 
         def round_pair_on_vector(c):
-            hi = min(VECTOR_COLS - starts[c], CHUNKS[c])
-            if hi > 0:
-                nc.vector.tensor_copy(z_bf[c][:, 0:hi, 2:4], pair[:, starts[c] : starts[c] + hi, :])
+            nc.vector.tensor_copy(z_bf[c][:, :, 2:4], pair[:, starts[c] : starts[c] + CHUNKS[c], :])
 
         z_q = sb.tile([P, U], U32, name="z_q", align_bytes=64)
         z_s = sb.tile([P, U], U8, name="z_s", align_bytes=64)
@@ -225,19 +223,21 @@ def tile_picked_sae8_relu_p_kernel(
                 out=z_q[:, cols].bitcast(FP8X4), scales=z_s[:, cols], in_=z_bf[c][:].rearrange("p w t -> p (w t)")
             )
 
-        for c in (0, 2):
-            round_pair_on_vector(c)
-            round_pair_on_vector(c + 1)
-            quantise_w2(2 + c // 2, 3 + c // 2)
+        round_pair_on_vector(0)
+        round_pair_on_vector(1)
+        quantise_w2(2, 3)
+        for c in (0, 1, 2):
             quantise_z(c)
-            quantise_z(c + 1)
+        quantise_w2(3, 4)
         round_pair_on_vector(4)
-        quantise_z(5)
+        quantise_z(3)
+        round_pair_on_vector(5)
         quantise_z(4)
+        quantise_z(5)
 
         out_planes = out.rearrange("(g p e) w -> p g e w", g=2, e=2)
 
-        stores = ((0, 128, 512, U), (0, 256, 512, U), (0, 256, U), (0, 256, U))
+        stores = ((0, 128, 640, U), (0, 256, 640, U), (0, 384, 768, U), (0, 384, 768, U))
         res = {
             (t, lo): sb.tile([P, hi - lo], F32, name="res%d_%d" % (t, lo))
             for t in range(PACK)
@@ -277,25 +277,23 @@ def tile_picked_sae8_relu_p_kernel(
         leave(0, 0, 128, False)
         multiply(1, 0, 256)
         leave(1, 0, 256, False)
-        multiply(2, 0, 256)
-        leave(2, 0, 256, False)
-        multiply(3, 0, 256)
-        leave(3, 0, 256, False)
-        multiply(0, 128, 512)
-        leave(0, 128, 512, False)
-        multiply(1, 256, 512)
-        leave(1, 256, 512, False)
-        multiply(2, 256, 512)
-        multiply(3, 256, 512)
+        multiply(2, 0, 384)
+        leave(2, 0, 384, False)
+        multiply(3, 0, 384)
+        leave(3, 0, 384, False)
+        multiply(0, 128, 640)
+        leave(0, 128, 640, False)
+        multiply(1, 256, 640)
+        leave(1, 256, 640, False)
+        multiply(2, 384, 768)
+        multiply(3, 384, 768)
+        leave(2, 384, 768, True)
         multiply(2, 768, 1024)
-        leave(2, 256, 512, False)
+        multiply(3, 768, 1024)
+        multiply(0, 640, 1024)
+        multiply(1, 640, 1024)
+        leave(3, 384, 768, False)
         leave(2, 768, 1024, True)
-        multiply(2, 512, 768)
-        multiply(3, 512, 1024)
-        multiply(0, 512, 1024)
-        multiply(1, 512, 1024)
-        leave(3, 256, 512, False)
-        leave(2, 512, 768, True)
-        leave(3, 512, 1024, False)
-        leave(0, 512, 1024, True)
-        leave(1, 512, 1024, False)
+        leave(3, 768, 1024, False)
+        leave(0, 640, 1024, True)
+        leave(1, 640, 1024, False)

@@ -147,10 +147,9 @@ def tile_picked_sae8_relu_p_kernel(
 
         w2_bf = [sb.tile([P, 2 * N], BF16, name="w2_bf%d" % g, align_bytes=64) for g in range(2)]
         for g in range(2):
-            nc.scalar.activation(
-                w2_bf[g][:].rearrange("p (e m j) -> p m j e", e=2, j=PACK),
-                w2_raw[g].rearrange("p j (m e) -> p m j e", e=2),
-                ACT.Copy,
+            nc.scalar.copy(
+                w2_bf[g][:].rearrange("p (e c m j) -> p c j m e", e=2, m=2, j=PACK),
+                w2_raw[g].rearrange("p j (c m e) -> p c j m e", m=2, e=2),
             )
 
         y_at = z_bytes
@@ -237,7 +236,7 @@ def tile_picked_sae8_relu_p_kernel(
 
         out_planes = out.rearrange("(g p e) w -> p g e w", g=2, e=2)
 
-        stores = ((0, 128, 640, U), (0, 256, 640, U), (0, 384, 768, U), (0, 384, 768, U))
+        stores = ((0, 128, 640, U), (0, 256, U), (0, 384, U), (0, 384, U))
         res = {
             (t, lo): sb.tile([P, hi - lo], F32, name="res%d_%d" % (t, lo))
             for t in range(PACK)
@@ -283,17 +282,17 @@ def tile_picked_sae8_relu_p_kernel(
         leave(3, 0, 384, False)
         multiply(0, 128, 640)
         leave(0, 128, 640, False)
-        multiply(1, 256, 640)
-        leave(1, 256, 640, False)
         multiply(2, 384, 768)
-        multiply(3, 384, 768)
-        leave(2, 384, 768, True)
+        multiply(1, 256, 768)
         multiply(2, 768, 1024)
-        multiply(3, 768, 1024)
-        multiply(0, 640, 1024)
-        multiply(1, 640, 1024)
-        leave(3, 384, 768, False)
+        leave(2, 384, 768, True)
         leave(2, 768, 1024, True)
-        leave(3, 768, 1024, False)
-        leave(0, 640, 1024, True)
-        leave(1, 640, 1024, False)
+        multiply(1, 768, 1024)
+        multiply(3, 384, 896)
+        multiply(3, 896, 1024)
+        multiply(0, 640, 1024)
+        leave(1, 256, 768, False)
+        leave(1, 768, 1024, False)
+        leave(3, 384, 896, True)
+        leave(3, 896, 1024, True)
+        leave(0, 640, 1024, False)

@@ -21,23 +21,18 @@ BANK = 512
 BANKS = 8
 HALF = S // 2
 SHORT = 128
-THIRD_FIRST = 192
+SECOND_SCATTER = 192
 CHUNKS = (128, 128, 128, 256, 128, 256)
 SCALAR_CHUNKS = (2, 3)
-FIRST_STORE = (128, 128, 256, 384)
-WARM_PASSES = 2
-ROUND_FIRST = 2
+ROUNDED_AHEAD = 2
+STORE_CUTS = ((0, 128, 640, U), (0, 256, U), (0, 384, U), (0, 384, U))
 
 
-def bank_cuts(lo, hi):
-    banks = []
-    while lo < hi:
-        cuts, end = [lo], min(lo + BANK, hi)
-        while cuts[-1] < end:
-            cuts.append(cuts[-1] + max(n for n in (512, 256, 128, 64) if n <= end - cuts[-1]))
-        banks.append(cuts)
-        lo = end
-    return banks
+def pass_cuts(lo, hi):
+    cuts = [lo]
+    while cuts[-1] < hi:
+        cuts.append(cuts[-1] + max(n for n in (512, 256, 128, 64) if n <= hi - cuts[-1]))
+    return cuts
 
 
 def tile_picked_sae8_relu_p_kernel(
@@ -55,7 +50,6 @@ def tile_picked_sae8_relu_p_kernel(
             taken.append(len(taken) % BANKS)
             return psum.tile([P, BANK], F32, name="bank%d" % taken[-1])
 
-
         offs_t = lists.tile([P, S // LIST_ROWS], U16, name="offs_t")
         held_t = lists.tile([P, S // LIST_ROWS], U16, name="held_t")
 
@@ -66,7 +60,7 @@ def tile_picked_sae8_relu_p_kernel(
         nc.vector.memset(xs[:].bitcast(I32), 0)
 
         z_bytes = 2 * PACK * U
-        late_y_bytes = 4 * ((S - THIRD_FIRST) + S + S - SHORT)
+        late_y_bytes = 4 * ((S - SECOND_SCATTER) + S + S - SHORT)
         w2_room = reused.tile([P, (z_bytes + late_y_bytes) // 4], F32, name="w2_room", align_bytes=64, offset=0)
         w2_first = sb.tile([P, PACK * N // 2], F32, name="w2_first")
         w2_raw = [half[:, 0 : PACK * N // 2].rearrange("p (j c) -> p j c", j=PACK) for half in (w2_first, w2_room)]
@@ -113,10 +107,10 @@ def tile_picked_sae8_relu_p_kernel(
         w1_q[0] = sb.tile([P, H // 2], U32, name="w1_q0", tag="xw", align_bytes=64)
         nc.vector.quantize_mx(out=w1_q[0][:].bitcast(FP8X4), scales=w1_s[0][:], in_=w1_bf[0][:])
 
-        def encode(t, lo, hi, at=None):
+        def encode(t, lo, hi, y):
             acc = next_bank()
             cols = slice(t // 2 * P, (t // 2 + 1) * P)
-            cuts = bank_cuts(lo, hi)[0]
+            cuts = pass_cuts(lo, hi)
             for a, b in zip(cuts[:-1], cuts[1:]):
                 nc.tensor.matmul_mx(
                     out=acc[:, a - lo : b - lo],
@@ -127,22 +121,21 @@ def tile_picked_sae8_relu_p_kernel(
                     start=True,
                     stop=True,
                 )
-            if hi == S and t == 2:
-                y = sb.tile([P, hi - lo], F32, name="y_last", tag="window1", align_bytes=64)
-            elif at is None:
-                y = sb.tile([P, hi - lo], F32, name="y%d_%d" % (t, lo))
-            else:
-                y = reused.tile([P, hi - lo], F32, name="y%d_%d" % (t, lo), align_bytes=64, offset=at)
             nc.scalar.activation(y[:], acc[:, 0 : hi - lo], ACT.Relu, bias=b1_t[:, t : t + 1])
             return y
+
+        def late_y(t, lo, hi, at):
+            y = reused.tile([P, hi - lo], F32, name="y%d_%d" % (t, lo), align_bytes=64, offset=at)
+            return encode(t, lo, hi, y)
 
         def scatter(t, y, lo, hi):
             nc.vector.tensor_copy(window[t][:].indirect(entries(held_t, lo, hi)), y[:])
 
-        for t, lo, hi in ((3, 0, SHORT), (1, 0, THIRD_FIRST), (3, SHORT, S)):
-            scatter(t, encode(t, lo, hi), lo, hi)
+        for t, lo, hi in ((3, 0, SHORT), (1, 0, SECOND_SCATTER), (3, SHORT, S)):
+            scatter(t, encode(t, lo, hi, sb.tile([P, hi - lo], F32, name="y%d_%d" % (t, lo))), lo, hi)
 
-        for lo, hi in ((0, 256), (640, U)):
+        starts = [sum(CHUNKS[:c]) for c in range(len(CHUNKS) + 1)]
+        for lo, hi in ((0, starts[SCALAR_CHUNKS[0]]), (starts[SCALAR_CHUNKS[-1] + 1], U)):
             nc.sync.dma_start(window[2][:, U + lo : U + hi], window[3][:, lo:hi])
 
         w2_bf = [sb.tile([P, 2 * N], BF16, name="w2_bf%d" % g, align_bytes=64) for g in range(2)]
@@ -153,13 +146,12 @@ def tile_picked_sae8_relu_p_kernel(
             )
 
         y_at = z_bytes
-        scatter(1, encode(1, THIRD_FIRST, S, y_at), THIRD_FIRST, S)
-        y_at = y_at + 4 * (S - THIRD_FIRST)
-        y_0 = encode(0, 0, S, y_at)
+        scatter(1, late_y(1, SECOND_SCATTER, S, y_at), SECOND_SCATTER, S)
+        y_at = y_at + 4 * (S - SECOND_SCATTER)
+        y_0 = late_y(0, 0, S, y_at)
         y_at = y_at + 4 * S
-        y_2 = encode(2, 0, S - SHORT, y_at)
+        y_2 = late_y(2, 0, S - SHORT, y_at)
 
-        starts = [sum(CHUNKS[:c]) for c in range(len(CHUNKS))]
         z_bf = [
             reused.tile([P, width, PACK], BF16, name="z_bf%d" % c, align_bytes=64, offset=2 * PACK * starts[c])
             for c, width in enumerate(CHUNKS)
@@ -175,40 +167,27 @@ def tile_picked_sae8_relu_p_kernel(
         w2_q = {}
         w2_s = sb.tile([P, N], U8, name="w2_s", align_bytes=64)
 
-        def quantise_w2(lo, hi):
-            g = lo // 2
+        def quantise_w2(t):
             nc.vector.quantize_mx(
-                out=w2_q[g][:, (lo - 2 * g) * P : (hi - 2 * g) * P].bitcast(FP8X4),
-                scales=w2_s[:, lo * P : hi * P],
-                in_=w2_bf[g][:, (lo - 2 * g) * P * PACK : (hi - 2 * g) * P * PACK],
+                out=w2_q[t // 2][:, t % 2 * P : (t % 2 + 1) * P].bitcast(FP8X4),
+                scales=w2_s[:, t * P : (t + 1) * P],
+                in_=w2_bf[t // 2][:, t % 2 * P * PACK : (t % 2 + 1) * P * PACK],
             )
 
         scatter(0, y_0, 0, S)
         scatter(2, y_2, 0, S - SHORT)
-        round_plane(0, range(ROUND_FIRST))
-        y_last = encode(2, S - SHORT, S)
+        round_plane(0, range(ROUNDED_AHEAD))
+        y_last = encode(2, S - SHORT, S, sb.tile([P, SHORT], F32, name="y_last", tag="window1", align_bytes=64))
         w2_q[0] = sb.tile([P, N // 2], U32, name="w2_q0", tag="b1_t", align_bytes=64)
-        quantise_w2(0, 1)
+        quantise_w2(0)
         scatter(2, y_last, S - SHORT, S)
-        quantise_w2(1, 2)
+        quantise_w2(1)
         w2_q[1] = sb.tile([P, N // 2], U32, name="w2_q1", tag="window1", align_bytes=64)
 
-        warm = next_bank()
-        for i in range(WARM_PASSES):
-            nc.tensor.matmul_mx(
-                out=warm[:],
-                lhsT=w2_q[0][:, 0:P].bitcast(FP8X4),
-                lhsT_scale=w2_s[:, 0:P],
-                rhs=xw_g[:].bitcast(FP8X4),
-                rhs_scale=xs_g[:],
-                start=(i == 0),
-                stop=(i == WARM_PASSES - 1),
-            )
-
-        round_plane(0, range(ROUND_FIRST, len(CHUNKS)))
+        round_plane(0, range(ROUNDED_AHEAD, len(CHUNKS)))
+        round_plane(2, SCALAR_CHUNKS)
 
         pair = window[2][:].rearrange("p (e w) -> p w e", e=2)
-        round_plane(2, SCALAR_CHUNKS)
 
         def round_pair_on_vector(c):
             nc.vector.tensor_copy(z_bf[c][:, :, 2:4], pair[:, starts[c] : starts[c] + CHUNKS[c], :])
@@ -224,10 +203,10 @@ def tile_picked_sae8_relu_p_kernel(
 
         round_pair_on_vector(0)
         round_pair_on_vector(1)
-        quantise_w2(2, 3)
+        quantise_w2(2)
         for c in (0, 1, 2):
             quantise_z(c)
-        quantise_w2(3, 4)
+        quantise_w2(3)
         round_pair_on_vector(4)
         quantise_z(3)
         round_pair_on_vector(5)
@@ -236,18 +215,16 @@ def tile_picked_sae8_relu_p_kernel(
 
         out_planes = out.rearrange("(g p e) w -> p g e w", g=2, e=2)
 
-        stores = ((0, 128, 640, U), (0, 256, U), (0, 384, U), (0, 384, U))
         res = {
             (t, lo): sb.tile([P, hi - lo], F32, name="res%d_%d" % (t, lo))
             for t in range(PACK)
-            for lo, hi in zip(stores[t][:-1], stores[t][1:])
+            for lo, hi in zip(STORE_CUTS[t][:-1], STORE_CUTS[t][1:])
         }
-        left = {(t, lo): hi - lo for t in range(PACK) for lo, hi in zip(stores[t][:-1], stores[t][1:])}
         sums = {}
 
         def multiply(t, lo, hi):
             sums[t, lo] = next_bank()
-            cuts = bank_cuts(lo, hi)[0]
+            cuts = pass_cuts(lo, hi)
             for a, b in zip(cuts[:-1], cuts[1:]):
                 nc.tensor.matmul_mx(
                     out=sums[t, lo][:, a - lo : b - lo],
@@ -261,38 +238,32 @@ def tile_picked_sae8_relu_p_kernel(
 
         def leave(t, lo, hi, on_vector):
             bias = b2_t[:, t // 2, t % 2 : t % 2 + 1]
-            first = max(cut for cut in stores[t] if cut <= lo)
+            first = max(cut for cut in STORE_CUTS[t] if cut <= lo)
             part = res[t, first][:, lo - first : hi - first]
             if on_vector:
                 nc.vector.tensor_scalar_add(part, sums[t, lo][:, 0 : hi - lo], bias)
             else:
                 nc.scalar.activation(part, sums[t, lo][:, 0 : hi - lo], ACT.Identity, bias=bias)
-            left[t, first] = left[t, first] - (hi - lo)
-            if left[t, first] == 0:
-                last = min(cut for cut in stores[t] if cut > first)
-                nc.sync.dma_start(out_planes[:, t // 2, t % 2, first:last], res[t, first][:])
+            if hi in STORE_CUTS[t]:
+                nc.sync.dma_start(out_planes[:, t // 2, t % 2, first:hi], res[t, first][:])
 
-        multiply(0, 0, 128)
-        leave(0, 0, 128, False)
-        multiply(1, 0, 256)
-        leave(1, 0, 256, False)
-        multiply(2, 0, 384)
-        leave(2, 0, 384, False)
-        multiply(3, 0, 384)
-        leave(3, 0, 384, False)
-        multiply(0, 128, 640)
-        leave(0, 128, 640, False)
-        multiply(2, 384, 768)
-        multiply(1, 256, 768)
-        multiply(2, 768, 1024)
-        leave(2, 384, 768, True)
-        leave(2, 768, 1024, True)
-        multiply(1, 768, 1024)
-        multiply(3, 384, 896)
-        multiply(3, 896, 1024)
-        multiply(0, 640, 1024)
-        leave(1, 256, 768, False)
-        leave(1, 768, 1024, False)
-        leave(3, 384, 896, True)
-        leave(3, 896, 1024, True)
-        leave(0, 640, 1024, False)
+        for t, n in ((0, 0), (1, 0), (2, 0), (3, 0), (0, 1)):
+            multiply(t, STORE_CUTS[t][n], STORE_CUTS[t][n + 1])
+            leave(t, STORE_CUTS[t][n], STORE_CUTS[t][n + 1], False)
+
+        last_chunk = starts[len(CHUNKS) - 1]
+        rest = {t: STORE_CUTS[t][-2] for t in range(PACK)}
+        multiply(2, rest[2], last_chunk)
+        multiply(1, rest[1], last_chunk)
+        multiply(2, last_chunk, U)
+        leave(2, rest[2], last_chunk, True)
+        leave(2, last_chunk, U, True)
+        multiply(1, last_chunk, U)
+        multiply(3, rest[3], rest[3] + BANK)
+        multiply(3, rest[3] + BANK, U)
+        multiply(0, rest[0], U)
+        leave(1, rest[1], last_chunk, False)
+        leave(1, last_chunk, U, False)
+        leave(3, rest[3], rest[3] + BANK, True)
+        leave(3, rest[3] + BANK, U, True)
+        leave(0, rest[0], U, False)

@@ -60,7 +60,7 @@ def tile_picked_sae8_relu_p_kernel(
         nc.vector.memset(xs[:].bitcast(I32), 0)
 
         z_bytes = 2 * PACK * U
-        late_y_bytes = 4 * ((S - SECOND_SCATTER) + S + S - SHORT)
+        late_y_bytes = 4 * (S + S - SHORT)
         w2_room = reused.tile([P, (z_bytes + late_y_bytes) // 4], F32, name="w2_room", align_bytes=64, offset=0)
         w2_first = sb.tile([P, PACK * N // 2], F32, name="w2_first")
         w2_raw = [half[:, 0 : PACK * N // 2].rearrange("p (j c) -> p j c", j=PACK) for half in (w2_first, w2_room)]
@@ -131,7 +131,7 @@ def tile_picked_sae8_relu_p_kernel(
         def scatter(t, y, lo, hi):
             nc.vector.tensor_copy(window[t][:].indirect(entries(held_t, lo, hi)), y[:])
 
-        for t, lo, hi in ((3, 0, SHORT), (1, 0, SECOND_SCATTER), (3, SHORT, S)):
+        for t, lo, hi in ((3, 0, SHORT), (1, 0, SECOND_SCATTER), (3, SHORT, S), (1, SECOND_SCATTER, S)):
             scatter(t, encode(t, lo, hi, sb.tile([P, hi - lo], F32, name="y%d_%d" % (t, lo))), lo, hi)
 
         starts = [sum(CHUNKS[:c]) for c in range(len(CHUNKS) + 1)]
@@ -146,23 +146,22 @@ def tile_picked_sae8_relu_p_kernel(
             )
 
         y_at = z_bytes
-        scatter(1, late_y(1, SECOND_SCATTER, S, y_at), SECOND_SCATTER, S)
-        y_at = y_at + 4 * (S - SECOND_SCATTER)
         y_0 = late_y(0, 0, S, y_at)
         y_at = y_at + 4 * S
         y_2 = late_y(2, 0, S - SHORT, y_at)
 
-        z_bf = [
-            reused.tile([P, width, PACK], BF16, name="z_bf%d" % c, align_bytes=64, offset=2 * PACK * starts[c])
-            for c, width in enumerate(CHUNKS)
-        ]
+        z_all = reused.tile([P, U, PACK], BF16, name="z_all", align_bytes=64, offset=0)
+        z_bf = [z_all[:, starts[c] : starts[c + 1], :] for c in range(len(CHUNKS))]
+
+        def round_columns(t, lo, hi):
+            nc.scalar.activation(z_all[:, lo:hi, t], window[t][:, lo:hi], ACT.Copy)
 
         def round_plane(t, chunks):
             for c in chunks:
                 nc.scalar.activation(z_bf[c][:, :, t], window[t][:, starts[c] : starts[c] + CHUNKS[c]], ACT.Copy)
 
-        round_plane(3, SCALAR_CHUNKS)
-        round_plane(1, range(len(CHUNKS)))
+        round_columns(3, starts[SCALAR_CHUNKS[0]], starts[SCALAR_CHUNKS[-1] + 1])
+        round_columns(1, 0, U)
 
         w2_q = {}
         w2_s = sb.tile([P, N], U8, name="w2_s", align_bytes=64)
@@ -176,7 +175,7 @@ def tile_picked_sae8_relu_p_kernel(
 
         scatter(0, y_0, 0, S)
         scatter(2, y_2, 0, S - SHORT)
-        round_plane(0, range(ROUNDED_AHEAD))
+        round_columns(0, 0, starts[ROUNDED_AHEAD])
         y_last = encode(2, S - SHORT, S, sb.tile([P, SHORT], F32, name="y_last", tag="window1", align_bytes=64))
         w2_q[0] = sb.tile([P, N // 2], U32, name="w2_q0", tag="b1_t", align_bytes=64)
         quantise_w2(0)
@@ -184,7 +183,7 @@ def tile_picked_sae8_relu_p_kernel(
         quantise_w2(1)
         w2_q[1] = sb.tile([P, N // 2], U32, name="w2_q1", tag="window1", align_bytes=64)
 
-        round_plane(0, range(ROUNDED_AHEAD, len(CHUNKS)))
+        round_columns(0, starts[ROUNDED_AHEAD], U)
         round_plane(2, SCALAR_CHUNKS)
 
         pair = window[2][:].rearrange("p (e w) -> p w e", e=2)
@@ -198,7 +197,7 @@ def tile_picked_sae8_relu_p_kernel(
         def quantise_z(c):
             cols = slice(starts[c], starts[c] + CHUNKS[c])
             nc.vector.quantize_mx(
-                out=z_q[:, cols].bitcast(FP8X4), scales=z_s[:, cols], in_=z_bf[c][:].rearrange("p w t -> p (w t)")
+                out=z_q[:, cols].bitcast(FP8X4), scales=z_s[:, cols], in_=z_bf[c].rearrange("p w t -> p (w t)")
             )
 
         round_pair_on_vector(0)

@@ -26,6 +26,7 @@ CHUNKS = (128, 128, 128, 256, 128, 256)
 SCALAR_CHUNKS = (2, 3)
 ROUNDED_AHEAD = 2
 STORE_CUTS = ((0, 128, 640, U), (0, 256, U), (0, 384, U), (0, 384, U))
+DMA_ALIGN = 256
 
 
 def pass_cuts(lo, hi):
@@ -56,7 +57,7 @@ def tile_picked_sae8_relu_p_kernel(
         def entries(list_t, lo, hi):
             return list_t[:, lo // LIST_ROWS : hi // LIST_ROWS]
 
-        xs = sb.tile([P, T], U8, name="xs", align_bytes=64)
+        xs = sb.tile([P, T], U8, name="xs", align_bytes=DMA_ALIGN)
         nc.vector.memset(xs[:].bitcast(I32), 0)
 
         z_bytes = 2 * PACK * U
@@ -65,8 +66,8 @@ def tile_picked_sae8_relu_p_kernel(
         w2_first = sb.tile([P, PACK * N // 2], F32, name="w2_first")
         w2_raw = [half[:, 0 : PACK * N // 2].rearrange("p (j c) -> p j c", j=PACK) for half in (w2_first, w2_room)]
 
-        w1_raw = sb.tile([P, PACK, H], F32, name="w1_raw")
-        xw = sb.tile([P, T], I32, name="xw", align_bytes=64)
+        w1_raw = sb.tile([P, PACK, H], F32, name="w1_raw", align_bytes=DMA_ALIGN)
+        xw = sb.tile([P, T], I32, name="xw", align_bytes=DMA_ALIGN)
         b1_t = sb.tile([P, PACK], F32, name="b1_t", align_bytes=64)
         b2_t = sb.tile([P, 2, 2], F32, name="b2_t")
 
@@ -104,7 +105,7 @@ def tile_picked_sae8_relu_p_kernel(
         xw_g = sb.tile([P, S], U32, name="xw_g", tag="w1_bf1", align_bytes=64)
         for lo in (0, HALF):
             nc.vector.tensor_copy(xw_g[:, lo : lo + HALF], xw[:].bitcast(U32).indirect(entries(offs_t, lo, lo + HALF)))
-        w1_q[0] = sb.tile([P, H // 2], U32, name="w1_q0", tag="xw", align_bytes=64)
+        w1_q[0] = sb.tile([P, H // 2], U32, name="w1_q0", tag="xw", align_bytes=DMA_ALIGN)
         nc.vector.quantize_mx(out=w1_q[0][:].bitcast(FP8X4), scales=w1_s[0][:], in_=w1_bf[0][:])
 
         def encode(t, lo, hi, y):
@@ -145,20 +146,13 @@ def tile_picked_sae8_relu_p_kernel(
                 w2_raw[g].rearrange("p j (c m e) -> p c j m e", m=2, e=2),
             )
 
-        y_at = z_bytes
-        y_0 = late_y(0, 0, S, y_at)
-        y_at = y_at + 4 * S
-        y_2 = late_y(2, 0, S - SHORT, y_at)
+        y_0 = late_y(0, 0, S, z_bytes)
+        y_2 = late_y(2, 0, S - SHORT, z_bytes + 4 * S)
 
-        z_all = reused.tile([P, U, PACK], BF16, name="z_all", align_bytes=64, offset=0)
-        z_bf = [z_all[:, starts[c] : starts[c + 1], :] for c in range(len(CHUNKS))]
+        z_bf = reused.tile([P, U, PACK], BF16, name="z_bf", align_bytes=64, offset=0)
 
         def round_columns(t, lo, hi):
-            nc.scalar.activation(z_all[:, lo:hi, t], window[t][:, lo:hi], ACT.Copy)
-
-        def round_plane(t, chunks):
-            for c in chunks:
-                nc.scalar.activation(z_bf[c][:, :, t], window[t][:, starts[c] : starts[c] + CHUNKS[c]], ACT.Copy)
+            nc.scalar.activation(z_bf[:, lo:hi, t], window[t][:, lo:hi], ACT.Copy)
 
         round_columns(3, starts[SCALAR_CHUNKS[0]], starts[SCALAR_CHUNKS[-1] + 1])
         round_columns(1, 0, U)
@@ -184,20 +178,22 @@ def tile_picked_sae8_relu_p_kernel(
         w2_q[1] = sb.tile([P, N // 2], U32, name="w2_q1", tag="window1", align_bytes=64)
 
         round_columns(0, starts[ROUNDED_AHEAD], U)
-        round_plane(2, SCALAR_CHUNKS)
+        for c in SCALAR_CHUNKS:
+            round_columns(2, starts[c], starts[c + 1])
 
         pair = window[2][:].rearrange("p (e w) -> p w e", e=2)
 
         def round_pair_on_vector(c):
-            nc.vector.tensor_copy(z_bf[c][:, :, 2:4], pair[:, starts[c] : starts[c] + CHUNKS[c], :])
+            cols = slice(starts[c], starts[c + 1])
+            nc.vector.tensor_copy(z_bf[:, cols, 2:4], pair[:, cols, :])
 
         z_q = sb.tile([P, U], U32, name="z_q", align_bytes=64)
         z_s = sb.tile([P, U], U8, name="z_s", align_bytes=64)
 
         def quantise_z(c):
-            cols = slice(starts[c], starts[c] + CHUNKS[c])
+            cols = slice(starts[c], starts[c + 1])
             nc.vector.quantize_mx(
-                out=z_q[:, cols].bitcast(FP8X4), scales=z_s[:, cols], in_=z_bf[c].rearrange("p w t -> p (w t)")
+                out=z_q[:, cols].bitcast(FP8X4), scales=z_s[:, cols], in_=z_bf[:, cols, :].rearrange("p w t -> p (w t)")
             )
 
         round_pair_on_vector(0)
@@ -215,7 +211,7 @@ def tile_picked_sae8_relu_p_kernel(
         out_planes = out.rearrange("(g p e) w -> p g e w", g=2, e=2)
 
         res = {
-            (t, lo): sb.tile([P, hi - lo], F32, name="res%d_%d" % (t, lo))
+            (t, lo): sb.tile([P, hi - lo], F32, name="res%d_%d" % (t, lo), align_bytes=DMA_ALIGN)
             for t in range(PACK)
             for lo, hi in zip(STORE_CUTS[t][:-1], STORE_CUTS[t][1:])
         }

@@ -19,9 +19,9 @@ PACK = 4
 LIST_ROWS = 16
 BANK = 512
 BANKS = 8
-HALF = S // 2
 SHORT = 128
-SECOND_SCATTER = 192
+SECOND_SCATTER = 128
+W1_ON_VECTOR = 80
 CHUNKS = (128, 128, 128, 256, 128, 256)
 SCALAR_CHUNKS = (2, 3)
 ROUNDED_AHEAD = 2
@@ -71,10 +71,12 @@ def tile_picked_sae8_relu_p_kernel(
         b1_t = sb.tile([P, PACK], F32, name="b1_t", align_bytes=64)
         b2_t = sb.tile([P, 2, 2], F32, name="b2_t")
 
-        nc.sync.dma_start(w1_raw[:], w1.rearrange("(p j) c -> p j c", j=PACK))
+        w1_in = w1.rearrange("(p j) c -> p j c", j=PACK)
+        nc.sync.dma_start(w1_raw[:, 0:2], w1_in[:, 0:2])
         nc.sync.dma_start(offs_t[:], offs)
         for i in range(4):
             nc.sync.dma_start(xs[i:P:32, :].bitcast(I32), x_scales[0, i:16:4, :].bitcast(I32))
+        nc.sync.dma_start(w1_raw[:, 2:4], w1_in[:, 2:4])
         nc.sync.dma_start(xw[:], x_words[0].rearrange("p n r -> p (n r)").bitcast(I32))
         nc.sync.dma_start(b1_t[:], b1.rearrange("(p t) o -> p (t o)", t=PACK))
         nc.sync.dma_start(held_t[:], held)
@@ -91,32 +93,31 @@ def tile_picked_sae8_relu_p_kernel(
         for t in (0, 2):
             nc.scalar.copy(window[t][:, 0:U], window[1][:])
 
-        w1_by_parity = w1_raw[:].rearrange("p j (m u v) -> p v m j u", u=2, v=2)
-        w1_bf = [sb.tile([P, 2 * H], BF16, name="w1_bf%d" % v, align_bytes=64) for v in range(2)]
-        w1_dealt = [w1_bf[v][:].rearrange("p (u m j) -> p m j u", u=2, j=PACK) for v in range(2)]
-        nc.vector.tensor_copy(w1_dealt[1], w1_by_parity[:, 1])
-        nc.scalar.activation(w1_dealt[0], w1_by_parity[:, 0], ACT.Copy)
         xs_g = sb.tile([P, S], U8, name="xs_g", align_bytes=64)
         nc.vector.tensor_copy(xs_g[:], xs[:].indirect(offs_t[:]))
-        w1_q = {1: sb.tile([P, H // 2], U32, name="w1_q1", align_bytes=64)}
-        w1_s = [sb.tile([P, H // 2], U8, name="w1_s%d" % v, align_bytes=64) for v in range(2)]
-        nc.vector.quantize_mx(out=w1_q[1][:].bitcast(FP8X4), scales=w1_s[1][:], in_=w1_bf[1][:])
 
-        xw_g = sb.tile([P, S], U32, name="xw_g", tag="w1_bf1", align_bytes=64)
-        for lo in (0, HALF):
-            nc.vector.tensor_copy(xw_g[:, lo : lo + HALF], xw[:].bitcast(U32).indirect(entries(offs_t, lo, lo + HALF)))
-        w1_q[0] = sb.tile([P, H // 2], U32, name="w1_q0", tag="xw", align_bytes=DMA_ALIGN)
-        nc.vector.quantize_mx(out=w1_q[0][:].bitcast(FP8X4), scales=w1_s[0][:], in_=w1_bf[0][:])
+        w1_bf = sb.tile([P, PACK * H], BF16, name="w1_bf", align_bytes=64)
+        w1_rows = w1_raw[:].rearrange("p j (m t) -> p m j t", t=PACK)
+        w1_dealt = w1_bf[:].rearrange("p (t m j) -> p m j t", t=PACK, j=PACK)
+        nc.vector.tensor_copy(w1_dealt[:, 0:W1_ON_VECTOR], w1_rows[:, 0:W1_ON_VECTOR])
+        nc.scalar.copy(w1_dealt[:, W1_ON_VECTOR:P], w1_rows[:, W1_ON_VECTOR:P])
+        w1_q = sb.tile([P, H], U32, name="w1_q", align_bytes=64)
+        w1_s = sb.tile([P, H], U8, name="w1_s", align_bytes=64)
+        nc.vector.quantize_mx(out=w1_q[:].bitcast(FP8X4), scales=w1_s[:], in_=w1_bf[:])
+
+        xw_g = sb.tile([P, S], U32, name="xw_g", tag="w1_bf", align_bytes=64)
+        for lo, hi in ((0, SHORT), (SHORT, S)):
+            nc.vector.tensor_copy(xw_g[:, lo:hi], xw[:].bitcast(U32).indirect(entries(offs_t, lo, hi)))
 
         def encode(t, lo, hi, y):
             acc = next_bank()
-            cols = slice(t // 2 * P, (t // 2 + 1) * P)
+            cols = slice(t * P, (t + 1) * P)
             cuts = pass_cuts(lo, hi)
             for a, b in zip(cuts[:-1], cuts[1:]):
                 nc.tensor.matmul_mx(
                     out=acc[:, a - lo : b - lo],
-                    lhsT=w1_q[t % 2][:, cols].bitcast(FP8X4),
-                    lhsT_scale=w1_s[t % 2][:, cols],
+                    lhsT=w1_q[:, cols].bitcast(FP8X4),
+                    lhsT_scale=w1_s[:, cols],
                     rhs=xw_g[:, a:b].bitcast(FP8X4),
                     rhs_scale=xs_g[:, a:b],
                     start=True,

@@ -25,6 +25,8 @@ W1_ON_VECTOR = 80
 CHUNKS = (128, 128, 128, 256, 128, 256)
 SCALAR_CHUNKS = (2, 3)
 ROUNDED_AHEAD = 2
+LATE_Y = 64
+AHEAD_OF_LATE_Y = 640
 STORE_CUTS = ((0, 128, 640, U), (0, 256, U), (0, 384, U), (0, 384, U))
 DMA_ALIGN = 256
 
@@ -61,7 +63,7 @@ def tile_picked_sae8_relu_p_kernel(
         nc.vector.memset(xs[:].bitcast(I32), 0)
 
         z_bytes = 2 * PACK * U
-        late_y_bytes = 4 * (S + S - SHORT)
+        late_y_bytes = 4 * 2 * S
         w2_room = reused.tile([P, (z_bytes + late_y_bytes) // 4], F32, name="w2_room", align_bytes=64, offset=0)
         w2_first = sb.tile([P, PACK * N // 2], F32, name="w2_first")
         w2_raw = [half[:, 0 : PACK * N // 2].rearrange("p (j c) -> p j c", j=PACK) for half in (w2_first, w2_room)]
@@ -123,18 +125,15 @@ def tile_picked_sae8_relu_p_kernel(
                     start=True,
                     stop=True,
                 )
-            nc.scalar.activation(y[:], acc[:, 0 : hi - lo], ACT.Relu, bias=b1_t[:, t : t + 1])
-            return y
-
-        def late_y(t, lo, hi, at):
-            y = reused.tile([P, hi - lo], F32, name="y%d_%d" % (t, lo), align_bytes=64, offset=at)
-            return encode(t, lo, hi, y)
+            nc.scalar.activation(y, acc[:, 0 : hi - lo], ACT.Relu, bias=b1_t[:, t : t + 1])
 
         def scatter(t, y, lo, hi):
             nc.vector.tensor_copy(window[t][:].indirect(entries(held_t, lo, hi)), y[:])
 
         for t, lo, hi in ((3, 0, SHORT), (1, 0, SECOND_SCATTER), (3, SHORT, S), (1, SECOND_SCATTER, S)):
-            scatter(t, encode(t, lo, hi, sb.tile([P, hi - lo], F32, name="y%d_%d" % (t, lo))), lo, hi)
+            y = sb.tile([P, hi - lo], F32, name="y%d_%d" % (t, lo))
+            encode(t, lo, hi, y[:])
+            scatter(t, y, lo, hi)
 
         starts = [sum(CHUNKS[:c]) for c in range(len(CHUNKS) + 1)]
         for lo, hi in ((0, starts[SCALAR_CHUNKS[0]]), (starts[SCALAR_CHUNKS[-1] + 1], U)):
@@ -147,8 +146,10 @@ def tile_picked_sae8_relu_p_kernel(
                 w2_raw[g].rearrange("p j (c m e) -> p c j m e", m=2, e=2),
             )
 
-        y_0 = late_y(0, 0, S, z_bytes)
-        y_2 = late_y(2, 0, S - SHORT, z_bytes + 4 * S)
+        y_0 = reused.tile([P, S], F32, name="y_0", align_bytes=64, offset=z_bytes)
+        y_2 = reused.tile([P, S], F32, name="y_2", align_bytes=64, offset=z_bytes + 4 * S)
+        encode(0, 0, S, y_0[:])
+        encode(2, 0, S - LATE_Y, y_2[:, 0 : S - LATE_Y])
 
         z_bf = reused.tile([P, U, PACK], BF16, name="z_bf", align_bytes=64, offset=0)
 
@@ -156,27 +157,26 @@ def tile_picked_sae8_relu_p_kernel(
             nc.scalar.activation(z_bf[:, lo:hi, t], window[t][:, lo:hi], ACT.Copy)
 
         round_columns(3, starts[SCALAR_CHUNKS[0]], starts[SCALAR_CHUNKS[-1] + 1])
-        round_columns(1, 0, U)
+        round_columns(1, 0, AHEAD_OF_LATE_Y)
+        encode(2, S - LATE_Y, S, y_2[:, S - LATE_Y : S])
+        round_columns(1, AHEAD_OF_LATE_Y, U)
 
-        w2_q = {}
         w2_s = sb.tile([P, N], U8, name="w2_s", align_bytes=64)
 
-        def quantise_w2(t):
+        scatter(0, y_0, 0, S)
+        scatter(2, y_2, 0, S)
+        round_columns(0, 0, starts[ROUNDED_AHEAD])
+
+        w2_q = reused.tile([P, N], U32, name="w2_q", align_bytes=64, offset=z_bytes + 4 * S)
+
+        def quantise_w2(first, last):
             nc.vector.quantize_mx(
-                out=w2_q[t // 2][:, t % 2 * P : (t % 2 + 1) * P].bitcast(FP8X4),
-                scales=w2_s[:, t * P : (t + 1) * P],
-                in_=w2_bf[t // 2][:, t % 2 * P * PACK : (t % 2 + 1) * P * PACK],
+                out=w2_q[:, first * P : (last + 1) * P].bitcast(FP8X4),
+                scales=w2_s[:, first * P : (last + 1) * P],
+                in_=w2_bf[first // 2][:, first % 2 * P * PACK : (last % 2 + 1) * P * PACK],
             )
 
-        scatter(0, y_0, 0, S)
-        scatter(2, y_2, 0, S - SHORT)
-        round_columns(0, 0, starts[ROUNDED_AHEAD])
-        y_last = encode(2, S - SHORT, S, sb.tile([P, SHORT], F32, name="y_last", tag="window1", align_bytes=64))
-        w2_q[0] = sb.tile([P, N // 2], U32, name="w2_q0", tag="b1_t", align_bytes=64)
-        quantise_w2(0)
-        scatter(2, y_last, S - SHORT, S)
-        quantise_w2(1)
-        w2_q[1] = sb.tile([P, N // 2], U32, name="w2_q1", tag="window1", align_bytes=64)
+        quantise_w2(0, 1)
 
         round_columns(0, starts[ROUNDED_AHEAD], U)
         for c in SCALAR_CHUNKS:
@@ -199,10 +199,10 @@ def tile_picked_sae8_relu_p_kernel(
 
         round_pair_on_vector(0)
         round_pair_on_vector(1)
-        quantise_w2(2)
+        quantise_w2(2, 2)
         for c in (0, 1, 2):
             quantise_z(c)
-        quantise_w2(3)
+        quantise_w2(3, 3)
         round_pair_on_vector(4)
         quantise_z(3)
         round_pair_on_vector(5)
@@ -224,7 +224,7 @@ def tile_picked_sae8_relu_p_kernel(
             for a, b in zip(cuts[:-1], cuts[1:]):
                 nc.tensor.matmul_mx(
                     out=sums[t, lo][:, a - lo : b - lo],
-                    lhsT=w2_q[t // 2][:, t % 2 * P : (t % 2 + 1) * P].bitcast(FP8X4),
+                    lhsT=w2_q[:, t * P : (t + 1) * P].bitcast(FP8X4),
                     lhsT_scale=w2_s[:, t * P : (t + 1) * P],
                     rhs=z_q[:, a:b].bitcast(FP8X4),
                     rhs_scale=z_s[:, a:b],

@@ -59,27 +59,40 @@ def tile_picked_sae8_relu_p_kernel(
         def entries(list_t, lo, hi):
             return list_t[:, lo // LIST_ROWS : hi // LIST_ROWS]
 
-        xs = sb.tile([P, T], U8, name="xs", align_bytes=DMA_ALIGN)
-        nc.vector.memset(xs[:].bitcast(I32), 0)
+        window = {t: sb.tile([P, U], F32, name="window%d" % t, align_bytes=64) for t in (1, 3)}
+        window[0] = sb.tile([P, U], F32, name="window0")
+        window[2] = sb.tile([P, 2 * U], F32, name="window2")
+        nc.vector.memset(window[1][:], 0.0)
+        for t in (3, 0):
+            nc.scalar.copy(window[t][:, 0:U], window[1][:])
+
+        xs = reused.tile([P, T], U8, name="xs", align_bytes=DMA_ALIGN, offset=3072)
+        for lo, hi in ((0, 96), (96, 112)):
+            nc.vector.memset(xs[lo:hi, :].bitcast(I32), 0)
+        xs_m = sb.tile([P, S], U8, name="xs_m", align_bytes=64)
+        nc.vector.memset(xs_m[:].bitcast(I32), 0)
 
         z_bytes = 2 * PACK * U
         late_y_bytes = 4 * 2 * S
-        w2_room = reused.tile([P, (z_bytes + late_y_bytes) // 4], F32, name="w2_room", align_bytes=64, offset=0)
-        w2_first = sb.tile([P, PACK * N // 2], F32, name="w2_first")
+        b2_at = 4 * PACK * N // 2
+        room = b2_at + 64
+        w2_room = reused.tile([P, (z_bytes + late_y_bytes) // 4], F32, name="w2_room", align_bytes=64, offset=room)
+        w2_first = reused.tile([P, PACK * N // 2], F32, name="w2_first", align_bytes=64, offset=0)
         w2_raw = [half[:, 0 : PACK * N // 2].rearrange("p (j c) -> p j c", j=PACK) for half in (w2_first, w2_room)]
 
         w1_raw = sb.tile([P, PACK, H], F32, name="w1_raw", align_bytes=DMA_ALIGN)
         xw = sb.tile([P, T], I32, name="xw", align_bytes=DMA_ALIGN)
         b1_t = sb.tile([P, PACK], F32, name="b1_t", align_bytes=64)
-        b2_t = sb.tile([P, 2, 2], F32, name="b2_t")
+        b2_t = reused.tile([P, 2, 2], F32, name="b2_t", align_bytes=64, offset=b2_at)
 
-        w1_in = w1.rearrange("(p j) c -> p j c", j=PACK)
-        nc.sync.dma_start(w1_raw[:, 0:2], w1_in[:, 0:2])
+        nc.sync.dma_start(xs[112:P, :].bitcast(I32), x_scales[0].bitcast(I32))
         nc.sync.dma_start(offs_t[:], offs)
-        for i in range(4):
-            nc.sync.dma_start(xs[i:P:32, :].bitcast(I32), x_scales[0, i:16:4, :].bitcast(I32))
-        nc.sync.dma_start(w1_raw[:, 2:4], w1_in[:, 2:4])
+        nc.sync.dma_start(w1_raw[:], w1.rearrange("(p j) c -> p j c", j=PACK))
         nc.sync.dma_start(xw[:], x_words[0].rearrange("p n r -> p (n r)").bitcast(I32))
+        xs_g = sb.tile([P, S], U8, name="xs_g", align_bytes=64)
+        nc.vector.tensor_copy(xs_g[:], xs[:].indirect(offs_t[:]))
+        for i in range(4):
+            nc.sync.dma_start(xs_m[i:P:32, :].bitcast(I32), xs_g[112 + i : P : 4, :].bitcast(I32))
         nc.sync.dma_start(b1_t[:], b1.rearrange("(p t) o -> p (t o)", t=PACK))
         nc.sync.dma_start(held_t[:], held)
         w2_rows = w2.rearrange("(p j) c -> p j c", j=PACK)
@@ -87,16 +100,7 @@ def tile_picked_sae8_relu_p_kernel(
             nc.sync.dma_start(w2_raw[g], w2_rows[:, :, g * N // 2 : (g + 1) * N // 2])
         nc.sync.dma_start(b2_t[:], b2.rearrange("(g p e) o -> p g (e o)", g=2, e=2))
 
-        window = {t: sb.tile([P, U], F32, name="window%d" % t, align_bytes=64) for t in (1, 3)}
-        window[0] = sb.tile([P, U], F32, name="window0")
-        window[2] = sb.tile([P, 2 * U], F32, name="window2")
-        for t in (1, 3):
-            nc.vector.memset(window[t][:], 0.0)
-        for t in (0, 2):
-            nc.scalar.copy(window[t][:, 0:U], window[1][:])
-
-        xs_g = sb.tile([P, S], U8, name="xs_g", align_bytes=64)
-        nc.vector.tensor_copy(xs_g[:], xs[:].indirect(offs_t[:]))
+        nc.vector.memset(window[2][:, 0:U], 0.0)
 
         w1_bf = sb.tile([P, PACK * H], BF16, name="w1_bf", align_bytes=64)
         w1_rows = w1_raw[:].rearrange("p j (m t) -> p m j t", t=PACK)
@@ -121,7 +125,7 @@ def tile_picked_sae8_relu_p_kernel(
                     lhsT=w1_q[:, cols].bitcast(FP8X4),
                     lhsT_scale=w1_s[:, cols],
                     rhs=xw_g[:, a:b].bitcast(FP8X4),
-                    rhs_scale=xs_g[:, a:b],
+                    rhs_scale=xs_m[:, a:b],
                     start=True,
                     stop=True,
                 )
@@ -146,12 +150,12 @@ def tile_picked_sae8_relu_p_kernel(
                 w2_raw[g].rearrange("p j (c m e) -> p c j m e", m=2, e=2),
             )
 
-        y_0 = reused.tile([P, S], F32, name="y_0", align_bytes=64, offset=z_bytes)
-        y_2 = reused.tile([P, S], F32, name="y_2", align_bytes=64, offset=z_bytes + 4 * S)
+        y_0 = reused.tile([P, S], F32, name="y_0", align_bytes=64, offset=room + z_bytes)
+        y_2 = reused.tile([P, S], F32, name="y_2", align_bytes=64, offset=room + z_bytes + 4 * S)
         encode(0, 0, S, y_0[:])
         encode(2, 0, S - LATE_Y, y_2[:, 0 : S - LATE_Y])
 
-        z_bf = reused.tile([P, U, PACK], BF16, name="z_bf", align_bytes=64, offset=0)
+        z_bf = reused.tile([P, U, PACK], BF16, name="z_bf", align_bytes=64, offset=room)
 
         def round_columns(t, lo, hi):
             nc.scalar.activation(z_bf[:, lo:hi, t], window[t][:, lo:hi], ACT.Copy)
@@ -167,7 +171,7 @@ def tile_picked_sae8_relu_p_kernel(
         scatter(2, y_2, 0, S)
         round_columns(0, 0, starts[ROUNDED_AHEAD])
 
-        w2_q = reused.tile([P, N], U32, name="w2_q", align_bytes=64, offset=z_bytes + 4 * S)
+        w2_q = reused.tile([P, N], U32, name="w2_q", align_bytes=64, offset=room + z_bytes + 4 * S)
 
         def quantise_w2(first, last):
             nc.vector.quantize_mx(

@@ -75,14 +75,15 @@ def tile_picked_sae8_relu_p_kernel(
         z_bytes = 2 * PACK * U
         late_y_bytes = 4 * 2 * S
         b2_at = 4 * PACK * N // 2
-        room = b2_at + 64
+        b1_at = b2_at + 64
+        room = b1_at + 64
         w2_room = reused.tile([P, (z_bytes + late_y_bytes) // 4], F32, name="w2_room", align_bytes=64, offset=room)
         w2_first = reused.tile([P, PACK * N // 2], F32, name="w2_first", align_bytes=64, offset=0)
         w2_raw = [half[:, 0 : PACK * N // 2].rearrange("p (j c) -> p j c", j=PACK) for half in (w2_first, w2_room)]
 
         w1_raw = sb.tile([P, PACK, H], F32, name="w1_raw", align_bytes=DMA_ALIGN)
         xw = sb.tile([P, T], I32, name="xw", align_bytes=DMA_ALIGN)
-        b1_t = sb.tile([P, PACK], F32, name="b1_t", align_bytes=64)
+        b1_t = reused.tile([P, PACK], F32, name="b1_t", align_bytes=64, offset=b1_at)
         b2_t = reused.tile([P, 2, 2], F32, name="b2_t", align_bytes=64, offset=b2_at)
 
         nc.sync.dma_start(xs[112:P, :].bitcast(I32), x_scales[0].bitcast(I32))
@@ -252,18 +253,12 @@ def tile_picked_sae8_relu_p_kernel(
             leave(t, STORE_CUTS[t][n], STORE_CUTS[t][n + 1], False)
 
         last_chunk = starts[len(CHUNKS) - 1]
-        rest = {t: STORE_CUTS[t][-2] for t in range(PACK)}
-        multiply(2, rest[2], last_chunk)
-        multiply(1, rest[1], last_chunk)
-        multiply(2, last_chunk, U)
-        leave(2, rest[2], last_chunk, True)
-        leave(2, last_chunk, U, True)
-        multiply(1, last_chunk, U)
-        multiply(3, rest[3], rest[3] + BANK)
-        multiply(3, rest[3] + BANK, U)
-        multiply(0, rest[0], U)
-        leave(1, rest[1], last_chunk, False)
-        leave(1, last_chunk, U, False)
-        leave(3, rest[3], rest[3] + BANK, True)
-        leave(3, rest[3] + BANK, U, True)
-        leave(0, rest[0], U, False)
+        rest = [STORE_CUTS[t][-2] for t in range(PACK)]
+        cut = [last_chunk, last_chunk, rest[2] + BANK, rest[3] + BANK]
+        for t, lo, hi in [(t, rest[t], cut[t]) for t in (0, 1)] + [(t, cut[t], U) for t in (0, 1)]:
+            multiply(t, lo, hi)
+            leave(t, lo, hi, t == 0)
+        for t in (2, 3):
+            for lo, hi in ((rest[t], cut[t]), (cut[t], U)):
+                multiply(t, lo, hi)
+                leave(t, lo, hi, t == 2)

@@ -23,7 +23,7 @@ SHORT = 128
 SECOND_SCATTER = 128
 W1_ON_VECTOR = 80
 CHUNKS = (128, 128, 128, 256, 128, 256)
-SCALAR_CHUNKS = (2, 3)
+SCALAR_CHUNKS = (2, 3, 4)
 ROUNDED_AHEAD = 2
 LATE_Y = 64
 AHEAD_OF_LATE_Y = 640
@@ -208,11 +208,9 @@ def tile_picked_sae8_relu_p_kernel(
         for c in (0, 1, 2):
             quantise_z(c)
         quantise_w2(3, 3)
-        round_pair_on_vector(4)
-        quantise_z(3)
         round_pair_on_vector(5)
-        quantise_z(4)
-        quantise_z(5)
+        for c in (3, 4, 5):
+            quantise_z(c)
 
         out_planes = out.rearrange("(g p e) w -> p g e w", g=2, e=2)
 

@@ -20,13 +20,11 @@ LIST_ROWS = 16
 BANK = 512
 BANKS = 8
 SHORT = 128
-SECOND_SCATTER = 128
 W1_ON_VECTOR = 80
 CHUNKS = (128, 128, 128, 256, 128, 256)
-SCALAR_CHUNKS = (2, 3, 4)
+SCALAR_CUTS = (256, 384, 640, 704)
 ROUNDED_AHEAD = 2
 LATE_Y = 64
-AHEAD_OF_LATE_Y = 640
 STORE_CUTS = ((0, 128, 640, U), (0, 256, U), (0, 384, U), (0, 384, U))
 DMA_ALIGN = 256
 
@@ -74,9 +72,9 @@ def tile_picked_sae8_relu_p_kernel(
 
         z_bytes = 2 * PACK * U
         late_y_bytes = 4 * 2 * S
-        b2_at = 4 * PACK * N // 2
-        b1_at = b2_at + 64
-        room = b1_at + 64
+        b1_at = 4 * PACK * N // 2
+        b2_at = b1_at + 64
+        room = b2_at + 64
         w2_room = reused.tile([P, (z_bytes + late_y_bytes) // 4], F32, name="w2_room", align_bytes=64, offset=room)
         w2_first = reused.tile([P, PACK * N // 2], F32, name="w2_first", align_bytes=64, offset=0)
         w2_raw = [half[:, 0 : PACK * N // 2].rearrange("p (j c) -> p j c", j=PACK) for half in (w2_first, w2_room)]
@@ -135,13 +133,13 @@ def tile_picked_sae8_relu_p_kernel(
         def scatter(t, y, lo, hi):
             nc.vector.tensor_copy(window[t][:].indirect(entries(held_t, lo, hi)), y[:])
 
-        for t, lo, hi in ((3, 0, SHORT), (1, 0, SECOND_SCATTER), (3, SHORT, S), (1, SECOND_SCATTER, S)):
+        for t, lo, hi in ((1, 0, SHORT), (3, 0, SHORT), (1, SHORT, S), (3, SHORT, S)):
             y = sb.tile([P, hi - lo], F32, name="y%d_%d" % (t, lo))
             encode(t, lo, hi, y[:])
             scatter(t, y, lo, hi)
 
         starts = [sum(CHUNKS[:c]) for c in range(len(CHUNKS) + 1)]
-        for lo, hi in ((0, starts[SCALAR_CHUNKS[0]]), (starts[SCALAR_CHUNKS[-1] + 1], U)):
+        for lo, hi in ((0, SCALAR_CUTS[0]), (SCALAR_CUTS[-1], U)):
             nc.sync.dma_start(window[2][:, U + lo : U + hi], window[3][:, lo:hi])
 
         w2_bf = [sb.tile([P, 2 * N], BF16, name="w2_bf%d" % g, align_bytes=64) for g in range(2)]
@@ -161,10 +159,9 @@ def tile_picked_sae8_relu_p_kernel(
         def round_columns(t, lo, hi):
             nc.scalar.activation(z_bf[:, lo:hi, t], window[t][:, lo:hi], ACT.Copy)
 
-        round_columns(3, starts[SCALAR_CHUNKS[0]], starts[SCALAR_CHUNKS[-1] + 1])
-        round_columns(1, 0, AHEAD_OF_LATE_Y)
+        round_columns(1, 0, U)
         encode(2, S - LATE_Y, S, y_2[:, S - LATE_Y : S])
-        round_columns(1, AHEAD_OF_LATE_Y, U)
+        round_columns(3, SCALAR_CUTS[0], SCALAR_CUTS[-1])
 
         w2_s = sb.tile([P, N], U8, name="w2_s", align_bytes=64)
 
@@ -172,7 +169,7 @@ def tile_picked_sae8_relu_p_kernel(
         scatter(2, y_2, 0, S)
         round_columns(0, 0, starts[ROUNDED_AHEAD])
 
-        w2_q = reused.tile([P, N], U32, name="w2_q", align_bytes=64, offset=room + z_bytes + 4 * S)
+        w2_q = reused.tile([P, N], U32, name="w2_q", align_bytes=64, offset=b2_at - 4 * N)
 
         def quantise_w2(first, last):
             nc.vector.quantize_mx(
@@ -184,14 +181,13 @@ def tile_picked_sae8_relu_p_kernel(
         quantise_w2(0, 1)
 
         round_columns(0, starts[ROUNDED_AHEAD], U)
-        for c in SCALAR_CHUNKS:
-            round_columns(2, starts[c], starts[c + 1])
+        for lo, hi in zip(SCALAR_CUTS[:-1], SCALAR_CUTS[1:]):
+            round_columns(2, lo, hi)
 
         pair = window[2][:].rearrange("p (e w) -> p w e", e=2)
 
-        def round_pair_on_vector(c):
-            cols = slice(starts[c], starts[c + 1])
-            nc.vector.tensor_copy(z_bf[:, cols, 2:4], pair[:, cols, :])
+        def round_pair_on_vector(lo, hi):
+            nc.vector.tensor_copy(z_bf[:, lo:hi, 2:4], pair[:, lo:hi, :])
 
         z_q = sb.tile([P, U], U32, name="z_q", align_bytes=64)
         z_s = sb.tile([P, U], U8, name="z_s", align_bytes=64)
@@ -202,13 +198,13 @@ def tile_picked_sae8_relu_p_kernel(
                 out=z_q[:, cols].bitcast(FP8X4), scales=z_s[:, cols], in_=z_bf[:, cols, :].rearrange("p w t -> p (w t)")
             )
 
-        round_pair_on_vector(0)
-        round_pair_on_vector(1)
+        round_pair_on_vector(0, starts[1])
+        round_pair_on_vector(starts[1], starts[2])
         quantise_w2(2, 2)
         for c in (0, 1, 2):
             quantise_z(c)
         quantise_w2(3, 3)
-        round_pair_on_vector(5)
+        round_pair_on_vector(SCALAR_CUTS[-1], U)
         for c in (3, 4, 5):
             quantise_z(c)
 

@@ -21,11 +21,11 @@ BANK = 512
 BANKS = 8
 SHORT = 128
 W1_ON_VECTOR = 80
-CHUNKS = (128, 128, 128, 256, 128, 256)
-SCALAR_CUTS = (256, 384, 640, 704)
+CHUNKS = (128,) * 8
+SCALAR_CUTS = (256, 384, 512)
 ROUNDED_AHEAD = 2
 LATE_Y = 64
-STORE_CUTS = ((0, 128, 640, U), (0, 256, U), (0, 384, U), (0, 384, U))
+STORE_CUTS = ((0, 128, 640, U), (0, 256, U), (0, 384, U), (0, 512, U))
 DMA_ALIGN = 256
 
 
@@ -204,9 +204,10 @@ def tile_picked_sae8_relu_p_kernel(
         for c in (0, 1, 2):
             quantise_z(c)
         quantise_w2(3, 3)
-        round_pair_on_vector(SCALAR_CUTS[-1], U)
-        for c in (3, 4, 5):
-            quantise_z(c)
+        for c in range(4, len(CHUNKS)):
+            round_pair_on_vector(starts[c], starts[c + 1])
+            quantise_z(c - 1)
+        quantise_z(len(CHUNKS) - 1)
 
         out_planes = out.rearrange("(g p e) w -> p g e w", g=2, e=2)
 
@@ -219,7 +220,7 @@ def tile_picked_sae8_relu_p_kernel(
 
         def multiply(t, lo, hi):
             sums[t, lo] = next_bank()
-            cuts = pass_cuts(lo, hi)
+            cuts = {(0, 512): [0, 256, 384, 512], (128, 640): [128, 384, 512, 640]}.get((lo, hi), pass_cuts(lo, hi))
             for a, b in zip(cuts[:-1], cuts[1:]):
                 nc.tensor.matmul_mx(
                     out=sums[t, lo][:, a - lo : b - lo],
@@ -239,20 +240,21 @@ def tile_picked_sae8_relu_p_kernel(
                 nc.vector.tensor_scalar_add(part, sums[t, lo][:, 0 : hi - lo], bias)
             else:
                 nc.scalar.activation(part, sums[t, lo][:, 0 : hi - lo], ACT.Identity, bias=bias)
-            if hi in STORE_CUTS[t]:
-                nc.sync.dma_start(out_planes[:, t // 2, t % 2, first:hi], res[t, first][:])
-
-        for t, n in ((0, 0), (1, 0), (2, 0), (3, 0), (0, 1)):
-            multiply(t, STORE_CUTS[t][n], STORE_CUTS[t][n + 1])
-            leave(t, STORE_CUTS[t][n], STORE_CUTS[t][n + 1], False)
 
         last_chunk = starts[len(CHUNKS) - 1]
-        rest = [STORE_CUTS[t][-2] for t in range(PACK)]
-        cut = [last_chunk, last_chunk, rest[2] + BANK, rest[3] + BANK]
-        for t, lo, hi in [(t, rest[t], cut[t]) for t in (0, 1)] + [(t, cut[t], U) for t in (0, 1)]:
-            multiply(t, lo, hi)
-            leave(t, lo, hi, t == 0)
-        for t in (2, 3):
-            for lo, hi in ((rest[t], cut[t]), (cut[t], U)):
+        for t, parts in (
+            (0, ((0, 128, False),)),
+            (1, ((0, 256, False),)),
+            (2, ((0, 384, False),)),
+            (3, ((0, 512, False),)),
+            (0, ((128, 640, False),)),
+            (0, ((640, last_chunk, True), (last_chunk, U, True))),
+            (1, ((256, 768, False), (768, U, False))),
+            (2, ((512, U, True), (384, 512, True))),
+            (3, ((512, U, False),)),
+        ):
+            for lo, hi, on_vector in parts:
                 multiply(t, lo, hi)
-                leave(t, lo, hi, t == 2)
+                leave(t, lo, hi, on_vector)
+            first, end = min(part[0] for part in parts), max(part[1] for part in parts)
+            nc.sync.dma_start(out_planes[:, t // 2, t % 2, first:end], res[t, first][:])

@@ -15,17 +15,20 @@ FP8X4 = mybir.dt.float8_e4m3fn_x4
 ACT = mybir.ActivationFunctionType
 
 P = 128
+QUADRANT = 32
 PACK = 4
 LIST_ROWS = 16
+SCALE_ROWS = K // 32
 BANK = 512
 BANKS = 8
 SHORT = 128
 W1_ON_VECTOR = 80
-CHUNKS = (128,) * 8
-SCALAR_CUTS = (256, 384, 512)
-ROUNDED_AHEAD = 2
 LATE_Y = 64
+CHUNK = 128
+CHUNKS = U // CHUNK
+SCALAR_CHUNKS = (2, 3)
 STORE_CUTS = ((0, 128, 640, U), (0, 256, U), (0, 384, U), (0, 512, U))
+PART = 256
 DMA_ALIGN = 256
 
 
@@ -57,6 +60,13 @@ def tile_picked_sae8_relu_p_kernel(
         def entries(list_t, lo, hi):
             return list_t[:, lo // LIST_ROWS : hi // LIST_ROWS]
 
+        w2_half_bytes = 4 * PACK * N // 2
+        z_bytes = 2 * PACK * U
+        y_bytes = 4 * S
+        b1_at = w2_half_bytes
+        b2_at = b1_at + 64
+        room_at = b2_at + 64
+
         window = {t: sb.tile([P, U], F32, name="window%d" % t, align_bytes=64) for t in (1, 3)}
         window[0] = sb.tile([P, U], F32, name="window0")
         window[2] = sb.tile([P, 2 * U], F32, name="window2")
@@ -64,18 +74,14 @@ def tile_picked_sae8_relu_p_kernel(
         for t in (3, 0):
             nc.scalar.copy(window[t][:, 0:U], window[1][:])
 
-        xs = reused.tile([P, T], U8, name="xs", align_bytes=DMA_ALIGN, offset=3072)
-        for lo, hi in ((0, 96), (96, 112)):
+        first_row = P - SCALE_ROWS
+        xs = reused.tile([P, T], U8, name="xs", align_bytes=DMA_ALIGN, offset=b1_at - T // 2)
+        for lo, hi in ((0, P - QUADRANT), (P - QUADRANT, first_row)):
             nc.vector.memset(xs[lo:hi, :].bitcast(I32), 0)
-        xs_m = sb.tile([P, S], U8, name="xs_m", align_bytes=64)
-        nc.vector.memset(xs_m[:].bitcast(I32), 0)
+        xs_moved = sb.tile([P, S], U8, name="xs_moved", align_bytes=64)
+        nc.vector.memset(xs_moved[:].bitcast(I32), 0)
 
-        z_bytes = 2 * PACK * U
-        late_y_bytes = 4 * 2 * S
-        b1_at = 4 * PACK * N // 2
-        b2_at = b1_at + 64
-        room = b2_at + 64
-        w2_room = reused.tile([P, (z_bytes + late_y_bytes) // 4], F32, name="w2_room", align_bytes=64, offset=room)
+        w2_room = reused.tile([P, (z_bytes + 2 * y_bytes) // 4], F32, name="w2_room", align_bytes=64, offset=room_at)
         w2_first = reused.tile([P, PACK * N // 2], F32, name="w2_first", align_bytes=64, offset=0)
         w2_raw = [half[:, 0 : PACK * N // 2].rearrange("p (j c) -> p j c", j=PACK) for half in (w2_first, w2_room)]
 
@@ -84,14 +90,14 @@ def tile_picked_sae8_relu_p_kernel(
         b1_t = reused.tile([P, PACK], F32, name="b1_t", align_bytes=64, offset=b1_at)
         b2_t = reused.tile([P, 2, 2], F32, name="b2_t", align_bytes=64, offset=b2_at)
 
-        nc.sync.dma_start(xs[112:P, :].bitcast(I32), x_scales[0].bitcast(I32))
+        nc.scalar.dma_start(xs[first_row:P, :].bitcast(I32), x_scales[0].bitcast(I32))
         nc.sync.dma_start(offs_t[:], offs)
         nc.sync.dma_start(w1_raw[:], w1.rearrange("(p j) c -> p j c", j=PACK))
         nc.sync.dma_start(xw[:], x_words[0].rearrange("p n r -> p (n r)").bitcast(I32))
-        xs_g = sb.tile([P, S], U8, name="xs_g", align_bytes=64)
-        nc.vector.tensor_copy(xs_g[:], xs[:].indirect(offs_t[:]))
+        xs_picked = sb.tile([P, S], U8, name="xs_picked", align_bytes=64)
+        nc.vector.tensor_copy(xs_picked[:], xs[:].indirect(offs_t[:]))
         for i in range(4):
-            nc.sync.dma_start(xs_m[i:P:32, :].bitcast(I32), xs_g[112 + i : P : 4, :].bitcast(I32))
+            nc.sync.dma_start(xs_moved[i:P:QUADRANT, :].bitcast(I32), xs_picked[first_row + i : P : 4, :].bitcast(I32))
         nc.sync.dma_start(b1_t[:], b1.rearrange("(p t) o -> p (t o)", t=PACK))
         nc.sync.dma_start(held_t[:], held)
         w2_rows = w2.rearrange("(p j) c -> p j c", j=PACK)
@@ -110,9 +116,9 @@ def tile_picked_sae8_relu_p_kernel(
         w1_s = sb.tile([P, H], U8, name="w1_s", align_bytes=64)
         nc.vector.quantize_mx(out=w1_q[:].bitcast(FP8X4), scales=w1_s[:], in_=w1_bf[:])
 
-        xw_g = sb.tile([P, S], U32, name="xw_g", tag="w1_bf", align_bytes=64)
+        xw_picked = sb.tile([P, S], U32, name="xw_picked", align_bytes=64)
         for lo, hi in ((0, SHORT), (SHORT, S)):
-            nc.vector.tensor_copy(xw_g[:, lo:hi], xw[:].bitcast(U32).indirect(entries(offs_t, lo, hi)))
+            nc.vector.tensor_copy(xw_picked[:, lo:hi], xw[:].bitcast(U32).indirect(entries(offs_t, lo, hi)))
 
         def encode(t, lo, hi, y):
             acc = next_bank()
@@ -123,8 +129,8 @@ def tile_picked_sae8_relu_p_kernel(
                     out=acc[:, a - lo : b - lo],
                     lhsT=w1_q[:, cols].bitcast(FP8X4),
                     lhsT_scale=w1_s[:, cols],
-                    rhs=xw_g[:, a:b].bitcast(FP8X4),
-                    rhs_scale=xs_m[:, a:b],
+                    rhs=xw_picked[:, a:b].bitcast(FP8X4),
+                    rhs_scale=xs_moved[:, a:b],
                     start=True,
                     stop=True,
                 )
@@ -138,8 +144,8 @@ def tile_picked_sae8_relu_p_kernel(
             encode(t, lo, hi, y[:])
             scatter(t, y, lo, hi)
 
-        starts = [sum(CHUNKS[:c]) for c in range(len(CHUNKS) + 1)]
-        for lo, hi in ((0, SCALAR_CUTS[0]), (SCALAR_CUTS[-1], U)):
+        scalar_lo, scalar_hi = SCALAR_CHUNKS[0] * CHUNK, (SCALAR_CHUNKS[-1] + 1) * CHUNK
+        for lo, hi in ((0, scalar_lo), (scalar_hi, U)):
             nc.sync.dma_start(window[2][:, U + lo : U + hi], window[3][:, lo:hi])
 
         w2_bf = [sb.tile([P, 2 * N], BF16, name="w2_bf%d" % g, align_bytes=64) for g in range(2)]
@@ -149,25 +155,25 @@ def tile_picked_sae8_relu_p_kernel(
                 w2_raw[g].rearrange("p j (c m e) -> p c j m e", m=2, e=2),
             )
 
-        y_0 = reused.tile([P, S], F32, name="y_0", align_bytes=64, offset=room + z_bytes)
-        y_2 = reused.tile([P, S], F32, name="y_2", align_bytes=64, offset=room + z_bytes + 4 * S)
+        y_0 = reused.tile([P, S], F32, name="y_0", align_bytes=64, offset=room_at + z_bytes)
+        y_2 = reused.tile([P, S], F32, name="y_2", align_bytes=64, offset=room_at + z_bytes + y_bytes)
         encode(0, 0, S, y_0[:])
         encode(2, 0, S - LATE_Y, y_2[:, 0 : S - LATE_Y])
 
-        z_bf = reused.tile([P, U, PACK], BF16, name="z_bf", align_bytes=64, offset=room)
+        z_bf = reused.tile([P, U, PACK], BF16, name="z_bf", align_bytes=64, offset=room_at)
 
-        def round_columns(t, lo, hi):
+        def round_on_scalar(t, lo, hi):
             nc.scalar.activation(z_bf[:, lo:hi, t], window[t][:, lo:hi], ACT.Copy)
 
-        round_columns(1, 0, U)
+        round_on_scalar(1, 0, U)
         encode(2, S - LATE_Y, S, y_2[:, S - LATE_Y : S])
-        round_columns(3, SCALAR_CUTS[0], SCALAR_CUTS[-1])
+        round_on_scalar(3, scalar_lo, scalar_hi)
 
         w2_s = sb.tile([P, N], U8, name="w2_s", align_bytes=64)
 
         scatter(0, y_0, 0, S)
         scatter(2, y_2, 0, S)
-        round_columns(0, 0, starts[ROUNDED_AHEAD])
+        round_on_scalar(0, 0, scalar_lo)
 
         w2_q = reused.tile([P, N], U32, name="w2_q", align_bytes=64, offset=b2_at - 4 * N)
 
@@ -180,34 +186,35 @@ def tile_picked_sae8_relu_p_kernel(
 
         quantise_w2(0, 1)
 
-        round_columns(0, starts[ROUNDED_AHEAD], U)
-        for lo, hi in zip(SCALAR_CUTS[:-1], SCALAR_CUTS[1:]):
-            round_columns(2, lo, hi)
+        round_on_scalar(0, scalar_lo, U)
+        for c in SCALAR_CHUNKS:
+            round_on_scalar(2, c * CHUNK, (c + 1) * CHUNK)
 
         pair = window[2][:].rearrange("p (e w) -> p w e", e=2)
 
-        def round_pair_on_vector(lo, hi):
-            nc.vector.tensor_copy(z_bf[:, lo:hi, 2:4], pair[:, lo:hi, :])
+        def round_pair_on_vector(c):
+            cols = slice(c * CHUNK, (c + 1) * CHUNK)
+            nc.vector.tensor_copy(z_bf[:, cols, 2:4], pair[:, cols, :])
 
         z_q = sb.tile([P, U], U32, name="z_q", align_bytes=64)
         z_s = sb.tile([P, U], U8, name="z_s", align_bytes=64)
 
         def quantise_z(c):
-            cols = slice(starts[c], starts[c + 1])
+            cols = slice(c * CHUNK, (c + 1) * CHUNK)
             nc.vector.quantize_mx(
                 out=z_q[:, cols].bitcast(FP8X4), scales=z_s[:, cols], in_=z_bf[:, cols, :].rearrange("p w t -> p (w t)")
             )
 
-        round_pair_on_vector(0, starts[1])
-        round_pair_on_vector(starts[1], starts[2])
+        round_pair_on_vector(0)
+        round_pair_on_vector(1)
         quantise_w2(2, 2)
         for c in (0, 1, 2):
             quantise_z(c)
         quantise_w2(3, 3)
-        for c in range(4, len(CHUNKS)):
-            round_pair_on_vector(starts[c], starts[c + 1])
+        for c in range(SCALAR_CHUNKS[-1] + 1, CHUNKS):
+            round_pair_on_vector(c)
             quantise_z(c - 1)
-        quantise_z(len(CHUNKS) - 1)
+        quantise_z(CHUNKS - 1)
 
         out_planes = out.rearrange("(g p e) w -> p g e w", g=2, e=2)
 
@@ -216,14 +223,13 @@ def tile_picked_sae8_relu_p_kernel(
             for t in range(PACK)
             for lo, hi in zip(STORE_CUTS[t][:-1], STORE_CUTS[t][1:])
         }
-        sums = {}
 
-        def multiply(t, lo, hi):
-            sums[t, lo] = next_bank()
-            cuts = {(0, 512): [0, 256, 384, 512], (128, 640): [128, 384, 512, 640]}.get((lo, hi), pass_cuts(lo, hi))
+        def decode(t, cuts, into, on_vector):
+            acc = next_bank()
+            lo, hi = cuts[0], cuts[-1]
             for a, b in zip(cuts[:-1], cuts[1:]):
                 nc.tensor.matmul_mx(
-                    out=sums[t, lo][:, a - lo : b - lo],
+                    out=acc[:, a - lo : b - lo],
                     lhsT=w2_q[:, t * P : (t + 1) * P].bitcast(FP8X4),
                     lhsT_scale=w2_s[:, t * P : (t + 1) * P],
                     rhs=z_q[:, a:b].bitcast(FP8X4),
@@ -231,30 +237,24 @@ def tile_picked_sae8_relu_p_kernel(
                     start=True,
                     stop=True,
                 )
-
-        def leave(t, lo, hi, on_vector):
             bias = b2_t[:, t // 2, t % 2 : t % 2 + 1]
-            first = max(cut for cut in STORE_CUTS[t] if cut <= lo)
-            part = res[t, first][:, lo - first : hi - first]
             if on_vector:
-                nc.vector.tensor_scalar_add(part, sums[t, lo][:, 0 : hi - lo], bias)
+                nc.vector.tensor_scalar_add(into, acc[:, 0 : hi - lo], bias)
             else:
-                nc.scalar.activation(part, sums[t, lo][:, 0 : hi - lo], ACT.Identity, bias=bias)
+                nc.scalar.activation(into, acc[:, 0 : hi - lo], ACT.Identity, bias=bias)
 
-        last_chunk = starts[len(CHUNKS) - 1]
-        for t, parts in (
-            (0, ((0, 128, False),)),
-            (1, ((0, 256, False),)),
-            (2, ((0, 384, False),)),
-            (3, ((0, 512, False),)),
-            (0, ((128, 640, False),)),
-            (0, ((640, last_chunk, True), (last_chunk, U, True))),
-            (1, ((256, 768, False), (768, U, False))),
-            (2, ((512, U, True), (384, 512, True))),
-            (3, ((512, U, False),)),
-        ):
-            for lo, hi, on_vector in parts:
-                multiply(t, lo, hi)
-                leave(t, lo, hi, on_vector)
-            first, end = min(part[0] for part in parts), max(part[1] for part in parts)
+        def store(t, n, parts):
+            first, end = STORE_CUTS[t][n], STORE_CUTS[t][n + 1]
+            for cuts, on_vector in parts:
+                decode(t, cuts, res[t, first][:, cuts[0] - first : cuts[-1] - first], on_vector)
             nc.sync.dma_start(out_planes[:, t // 2, t % 2, first:end], res[t, first][:])
+
+        store(0, 0, [((0, 128), False)])
+        store(1, 0, [((0, 256), False)])
+        store(2, 0, [((0, 256, 384), False)])
+        store(3, 0, [((0, 256, 384, 512), False)])
+        store(0, 1, [((128, 384, 512, 640), False)])
+        store(0, 2, [((640, 896), True), ((896, U), True)])
+        store(1, 1, [((256, 768), False), ((768, U), False)])
+        store(2, 1, [((512, U), True), ((384, 512), True)])
+        store(3, 1, [((512, U), False)])

@@ -27,8 +27,7 @@ LATE_Y = 64
 CHUNK = 128
 CHUNKS = U // CHUNK
 SCALAR_CHUNKS = (2, 3)
-STORE_CUTS = ((0, 128, 640, U), (0, 256, U), (0, 384, U), (0, 512, U))
-PART = 256
+STORE_CUTS = ((0, 128, 512, U), (0, 256, U), (0, 384, U), (0, 384, U))
 DMA_ALIGN = 256
 
 
@@ -243,18 +242,27 @@ def tile_picked_sae8_relu_p_kernel(
             else:
                 nc.scalar.activation(into, acc[:, 0 : hi - lo], ACT.Identity, bias=bias)
 
-        def store(t, n, parts):
+        def part(t, n, cuts, on_vector):
+            first = STORE_CUTS[t][n]
+            decode(t, cuts, res[t, first][:, cuts[0] - first : cuts[-1] - first], on_vector)
+
+        def store(t, n):
             first, end = STORE_CUTS[t][n], STORE_CUTS[t][n + 1]
-            for cuts, on_vector in parts:
-                decode(t, cuts, res[t, first][:, cuts[0] - first : cuts[-1] - first], on_vector)
             nc.sync.dma_start(out_planes[:, t // 2, t % 2, first:end], res[t, first][:])
 
-        store(0, 0, [((0, 128), False)])
-        store(1, 0, [((0, 256), False)])
-        store(2, 0, [((0, 256, 384), False)])
-        store(3, 0, [((0, 256, 384, 512), False)])
-        store(0, 1, [((128, 384, 512, 640), False)])
-        store(0, 2, [((640, 896), True), ((896, U), True)])
-        store(1, 1, [((256, 768), False), ((768, U), False)])
-        store(2, 1, [((512, U), True), ((384, 512), True)])
-        store(3, 1, [((512, U), False)])
+        for t, n, cuts in ((0, 0, (0, 128)), (1, 0, (0, 128, 256)), (2, 0, (0, 256, 384)), (3, 0, (0, 256, 384)), (0, 1, (128, 384, 512))):
+            part(t, n, cuts, False)
+            store(t, n)
+        part(0, 2, (512, 768), False)
+        part(2, 1, (384, 640), False)
+        part(0, 2, (768, 896), True)
+        part(0, 2, (896, U), True)
+        store(0, 2)
+        part(2, 1, (640, 896, U), True)
+        store(2, 1)
+        part(3, 1, (512, U), False)
+        part(3, 1, (384, 512), False)
+        store(3, 1)
+        part(1, 1, (256, 768), True)
+        part(1, 1, (768, U), False)
+        store(1, 1)

@@ -27,7 +27,7 @@ LATE_Y = 64
 CHUNK = 128
 CHUNKS = U // CHUNK
 SCALAR_CHUNKS = (2, 3)
-STORE_CUTS = ((0, 128, 512, U), (0, 256, U), (0, 384, U), (0, 384, U))
+STORE_CUTS = ((0, 256, 512, U), (0, 256, 512, U), (0, 512, U), (0, U))
 DMA_ALIGN = 256
 
 
@@ -49,8 +49,8 @@ def tile_picked_sae8_relu_p_kernel(
         psum = ctx.enter_context(tc.psum_pool(name="psum", bufs=1))
         taken = []
 
-        def next_bank():
-            taken.append(len(taken) % BANKS)
+        def next_bank(behind=BANKS):
+            taken.append(len(taken) if len(taken) < BANKS else taken[-behind])
             return psum.tile([P, BANK], F32, name="bank%d" % taken[-1])
 
         offs_t = lists.tile([P, S // LIST_ROWS], U16, name="offs_t")
@@ -223,8 +223,8 @@ def tile_picked_sae8_relu_p_kernel(
             for lo, hi in zip(STORE_CUTS[t][:-1], STORE_CUTS[t][1:])
         }
 
-        def decode(t, cuts, into, on_vector):
-            acc = next_bank()
+        def decode(t, cuts, into, on_vector, behind):
+            acc = next_bank(behind)
             lo, hi = cuts[0], cuts[-1]
             for a, b in zip(cuts[:-1], cuts[1:]):
                 nc.tensor.matmul_mx(
@@ -242,27 +242,29 @@ def tile_picked_sae8_relu_p_kernel(
             else:
                 nc.scalar.activation(into, acc[:, 0 : hi - lo], ACT.Identity, bias=bias)
 
-        def part(t, n, cuts, on_vector):
+        def part(t, n, cuts, on_vector, behind=BANKS):
             first = STORE_CUTS[t][n]
-            decode(t, cuts, res[t, first][:, cuts[0] - first : cuts[-1] - first], on_vector)
+            decode(t, cuts, res[t, first][:, cuts[0] - first : cuts[-1] - first], on_vector, behind)
 
         def store(t, n):
             first, end = STORE_CUTS[t][n], STORE_CUTS[t][n + 1]
             nc.sync.dma_start(out_planes[:, t // 2, t % 2, first:end], res[t, first][:])
 
-        for t, n, cuts in ((0, 0, (0, 128)), (1, 0, (0, 128, 256)), (2, 0, (0, 256, 384)), (3, 0, (0, 256, 384)), (0, 1, (128, 384, 512))):
+        for t, n, cuts in ((0, 0, (0, 128, 256)), (1, 0, (0, 256)), (0, 1, (256, 384, 512)), (1, 1, (256, 512))):
             part(t, n, cuts, False)
             store(t, n)
+        part(2, 0, (0, 256), False)
+        part(2, 0, (256, 512), False)
+        store(2, 0)
         part(0, 2, (512, 768), False)
-        part(2, 1, (384, 640), False)
         part(0, 2, (768, 896), True)
         part(0, 2, (896, U), True)
         store(0, 2)
-        part(2, 1, (640, 896, U), True)
+        part(1, 2, (512, U), True)
+        store(1, 2)
+        part(2, 1, (512, U), False)
         store(2, 1)
-        part(3, 1, (512, U), False)
-        part(3, 1, (384, 512), False)
-        store(3, 1)
-        part(1, 1, (256, 768), True)
-        part(1, 1, (768, U), False)
-        store(1, 1)
+        part(3, 0, (0, 512), True, 4)
+        part(3, 0, (512, 768), False, 4)
+        part(3, 0, (768, U), True)
+        store(3, 0)

@@ -190,6 +190,7 @@ def tile_picked_sae8_relu_p_kernel(
             round_on_scalar(2, c * CHUNK, (c + 1) * CHUNK)
 
         pair = window[2][:].rearrange("p (e w) -> p w e", e=2)
+        nc.scalar.copy(z_bf[:, U - CHUNK : U, 2:4], pair[:, U - CHUNK : U, :])
 
         def round_pair_on_vector(c):
             cols = slice(c * CHUNK, (c + 1) * CHUNK)
@@ -209,11 +210,12 @@ def tile_picked_sae8_relu_p_kernel(
         quantise_w2(2, 2)
         for c in (0, 1, 2):
             quantise_z(c)
-        quantise_w2(3, 3)
-        for c in range(SCALAR_CHUNKS[-1] + 1, CHUNKS):
+        for c in range(SCALAR_CHUNKS[-1] + 1, CHUNKS - 1):
             round_pair_on_vector(c)
             quantise_z(c - 1)
         quantise_z(CHUNKS - 1)
+        quantise_z(CHUNKS - 2)
+        quantise_w2(3, 3)
 
         out_planes = out.rearrange("(g p e) w -> p g e w", g=2, e=2)
 
@@ -257,8 +259,8 @@ def tile_picked_sae8_relu_p_kernel(
         part(2, 0, (256, 512), False)
         store(2, 0)
         part(0, 2, (512, 768), False)
-        part(0, 2, (768, 896), True)
         part(0, 2, (896, U), True)
+        part(0, 2, (768, 896), True)
         store(0, 2)
         part(1, 2, (512, U), True)
         store(1, 2)

@@ -208,9 +208,10 @@ def tile_picked_sae8_relu_p_kernel(
         round_pair_on_vector(0)
         round_pair_on_vector(1)
         quantise_w2(2, 2)
-        for c in (0, 1, 2):
+        for c in (0, 1, 2, 3):
             quantise_z(c)
-        for c in range(SCALAR_CHUNKS[-1] + 1, CHUNKS - 1):
+        round_pair_on_vector(4)
+        for c in (5, 6):
             round_pair_on_vector(c)
             quantise_z(c - 1)
         quantise_z(CHUNKS - 1)
@@ -252,21 +253,22 @@ def tile_picked_sae8_relu_p_kernel(
             first, end = STORE_CUTS[t][n], STORE_CUTS[t][n + 1]
             nc.sync.dma_start(out_planes[:, t // 2, t % 2, first:end], res[t, first][:])
 
-        for t, n, cuts in ((0, 0, (0, 128, 256)), (1, 0, (0, 256)), (0, 1, (256, 384, 512)), (1, 1, (256, 512))):
+        part(0, 0, (0, 128), False)
+        for t, n, cuts in ((0, 0, (128, 256)), (1, 0, (0, 256)), (0, 1, (256, 384, 512)), (1, 1, (256, 512))):
             part(t, n, cuts, False)
             store(t, n)
         part(2, 0, (0, 256), False)
-        part(2, 0, (256, 512), False)
+        part(2, 0, (256, 512), True)
         store(2, 0)
-        part(0, 2, (512, 768), False)
+        part(0, 2, (512, 640, 768), False)
         part(0, 2, (896, U), True)
         part(0, 2, (768, 896), True)
         store(0, 2)
-        part(1, 2, (512, U), True)
+        part(1, 2, (512, U), False)
         store(1, 2)
-        part(2, 1, (512, U), False)
+        part(2, 1, (512, U), True)
         store(2, 1)
-        part(3, 0, (0, 512), True, 4)
-        part(3, 0, (512, 768), False, 4)
-        part(3, 0, (768, U), True)
+        part(3, 0, (0, 512), False, 4)
+        part(3, 0, (512, 768), True, 4)
+        part(3, 0, (768, U), False)
         store(3, 0)

@@ -13,6 +13,7 @@ U16 = mybir.dt.uint16
 U8 = mybir.dt.uint8
 FP8X4 = mybir.dt.float8_e4m3fn_x4
 ACT = mybir.ActivationFunctionType
+ALU = mybir.AluOpType
 
 P = 128
 QUADRANT = 32
@@ -23,11 +24,10 @@ BANK = 512
 BANKS = 8
 SHORT = 128
 W1_ON_VECTOR = 80
-LATE_Y = 64
 CHUNK = 128
 CHUNKS = U // CHUNK
-SCALAR_CHUNKS = (2, 3)
-STORE_CUTS = ((0, 256, 512, U), (0, 256, 512, U), (0, 512, U), (0, U))
+EARLY = 768
+STORE_CUTS = ((0, 256, 512, U), (0, 256, 512, U), (0, 512, U), (0, 512, U))
 DMA_ALIGN = 256
 
 
@@ -50,7 +50,7 @@ def tile_picked_sae8_relu_p_kernel(
         taken = []
 
         def next_bank(behind=BANKS):
-            taken.append(len(taken) if len(taken) < BANKS else taken[-behind])
+            taken.append(len(taken) % BANKS)
             return psum.tile([P, BANK], F32, name="bank%d" % taken[-1])
 
         offs_t = lists.tile([P, S // LIST_ROWS], U16, name="offs_t")
@@ -60,29 +60,26 @@ def tile_picked_sae8_relu_p_kernel(
             return list_t[:, lo // LIST_ROWS : hi // LIST_ROWS]
 
         w2_half_bytes = 4 * PACK * N // 2
-        z_bytes = 2 * PACK * U
-        y_bytes = 4 * S
-        b1_at = w2_half_bytes
-        b2_at = b1_at + 64
-        room_at = b2_at + 64
+        staged_at = (3 * w2_half_bytes, 4 * w2_half_bytes, 6 * w2_half_bytes)
+        b2_at = w2_half_bytes
+        b1_at = b2_at + 64
+        first_at = b2_at + 5 * DMA_ALIGN
 
-        window = {t: sb.tile([P, U], F32, name="window%d" % t, align_bytes=64) for t in (1, 3)}
-        window[0] = sb.tile([P, U], F32, name="window0")
-        window[2] = sb.tile([P, 2 * U], F32, name="window2")
-        nc.vector.memset(window[1][:], 0.0)
-        for t in (3, 0):
-            nc.scalar.copy(window[t][:, 0:U], window[1][:])
+        window = [sb.tile([P, U], F32, name="window%d" % t, align_bytes=DMA_ALIGN) for t in range(PACK)]
+        nc.vector.memset(window[0][:], 0.0)
+        for t in (1, 3):
+            nc.scalar.copy(window[t][:], window[0][:])
 
         first_row = P - SCALE_ROWS
-        xs = reused.tile([P, T], U8, name="xs", align_bytes=DMA_ALIGN, offset=b1_at - T // 2)
+        xs = reused.tile([P, T], U8, name="xs", align_bytes=DMA_ALIGN, offset=b2_at - 2 * DMA_ALIGN)
         for lo, hi in ((0, P - QUADRANT), (P - QUADRANT, first_row)):
             nc.vector.memset(xs[lo:hi, :].bitcast(I32), 0)
         xs_moved = sb.tile([P, S], U8, name="xs_moved", align_bytes=64)
         nc.vector.memset(xs_moved[:].bitcast(I32), 0)
 
-        w2_room = reused.tile([P, (z_bytes + 2 * y_bytes) // 4], F32, name="w2_room", align_bytes=64, offset=room_at)
-        w2_first = reused.tile([P, PACK * N // 2], F32, name="w2_first", align_bytes=64, offset=0)
-        w2_raw = [half[:, 0 : PACK * N // 2].rearrange("p (j c) -> p j c", j=PACK) for half in (w2_first, w2_room)]
+        w2_first = reused.tile([P, PACK * N // 2], F32, name="w2_first", align_bytes=DMA_ALIGN, offset=first_at)
+        w2_room = reused.tile([P, U], F32, name="w2_room", align_bytes=DMA_ALIGN, offset=0)
+        w2_raw = [half.rearrange("p (j c) -> p j c", j=PACK) for half in (w2_first[:], w2_room[:])]
 
         w1_raw = sb.tile([P, PACK, H], F32, name="w1_raw", align_bytes=DMA_ALIGN)
         xw = sb.tile([P, T], I32, name="xw", align_bytes=DMA_ALIGN)
@@ -104,7 +101,7 @@ def tile_picked_sae8_relu_p_kernel(
             nc.sync.dma_start(w2_raw[g], w2_rows[:, :, g * N // 2 : (g + 1) * N // 2])
         nc.sync.dma_start(b2_t[:], b2.rearrange("(g p e) o -> p g (e o)", g=2, e=2))
 
-        nc.vector.memset(window[2][:, 0:U], 0.0)
+        nc.vector.memset(window[2][:], 0.0)
 
         w1_bf = sb.tile([P, PACK * H], BF16, name="w1_bf", align_bytes=64)
         w1_rows = w1_raw[:].rearrange("p j (m t) -> p m j t", t=PACK)
@@ -119,7 +116,7 @@ def tile_picked_sae8_relu_p_kernel(
         for lo, hi in ((0, SHORT), (SHORT, S)):
             nc.vector.tensor_copy(xw_picked[:, lo:hi], xw[:].bitcast(U32).indirect(entries(offs_t, lo, hi)))
 
-        def encode(t, lo, hi, y):
+        def encode(t, lo, hi, y, on_vector):
             acc = next_bank()
             cols = slice(t * P, (t + 1) * P)
             cuts = pass_cuts(lo, hi)
@@ -133,90 +130,114 @@ def tile_picked_sae8_relu_p_kernel(
                     start=True,
                     stop=True,
                 )
-            nc.scalar.activation(y, acc[:, 0 : hi - lo], ACT.Relu, bias=b1_t[:, t : t + 1])
+            bias = b1_t[:, t : t + 1]
+            if on_vector:
+                nc.vector.tensor_scalar(y, acc[:, 0 : hi - lo], bias, 0.0, ALU.add, ALU.max)
+            else:
+                nc.scalar.activation(y, acc[:, 0 : hi - lo], ACT.Relu, bias=bias)
 
-        def scatter(t, y, lo, hi):
-            nc.vector.tensor_copy(window[t][:].indirect(entries(held_t, lo, hi)), y[:])
+        def scatter(t, y, lo, hi, on_vector):
+            target = window[t][:].indirect(entries(held_t, lo, hi))
+            if on_vector:
+                nc.vector.tensor_copy(target, y)
+            else:
+                nc.scalar.activation(target, y, ACT.Copy)
 
-        for t, lo, hi in ((1, 0, SHORT), (3, 0, SHORT), (1, SHORT, S), (3, SHORT, S)):
-            y = sb.tile([P, hi - lo], F32, name="y%d_%d" % (t, lo))
-            encode(t, lo, hi, y[:])
-            scatter(t, y, lo, hi)
+        STAGES = ((0, 256), (256, EARLY), (EARLY, U))
+        staged = [
+            reused.tile(
+                [P, PACK, hi - lo], F32, name="staged%d" % lo, align_bytes=DMA_ALIGN, offset=at
+            )
+            for (lo, hi), at in zip(STAGES, staged_at)
+        ]
 
-        scalar_lo, scalar_hi = SCALAR_CHUNKS[0] * CHUNK, (SCALAR_CHUNKS[-1] + 1) * CHUNK
-        for lo, hi in ((0, scalar_lo), (scalar_hi, U)):
-            nc.sync.dma_start(window[2][:, U + lo : U + hi], window[3][:, lo:hi])
+        def stage_by_dma(t, h):
+            nc.sync.dma_start(staged[h][:, t, :], window[t][:, STAGES[h][0] : STAGES[h][1]])
 
+        y = {
+            (t, lo): sb.tile([P, hi - lo], F32, name="y%d_%d" % (t, lo))
+            for t in range(PACK)
+            for lo, hi in ((0, SHORT), (SHORT, S))
+        }
+
+        for t in range(PACK):
+            encode(t, 0, SHORT, y[t, 0][:], t == 1)
+        for t in range(PACK):
+            scatter(t, y[t, 0][:], 0, SHORT, t != 1)
         w2_bf = [sb.tile([P, 2 * N], BF16, name="w2_bf%d" % g, align_bytes=64) for g in range(2)]
-        for g in range(2):
-            nc.scalar.copy(
-                w2_bf[g][:].rearrange("p (e c m j) -> p c j m e", e=2, m=2, j=PACK),
-                w2_raw[g].rearrange("p j (c m e) -> p c j m e", m=2, e=2),
+        for g, e in ((0, 0), (0, 1), (1, 0), (1, 1)):
+            nc.gpsimd.tensor_scalar(
+                w2_bf[g][:].rearrange("p (e n j) -> p e n j", e=2, j=PACK)[:, e],
+                w2_raw[g].rearrange("p j (n e) -> p e n j", e=2)[:, e],
+                1.0,
+                0.0,
+                ALU.mult,
+                ALU.add,
             )
 
-        y_0 = reused.tile([P, S], F32, name="y_0", align_bytes=64, offset=room_at + z_bytes)
-        y_2 = reused.tile([P, S], F32, name="y_2", align_bytes=64, offset=room_at + z_bytes + y_bytes)
-        encode(0, 0, S, y_0[:])
-        encode(2, 0, S - LATE_Y, y_2[:, 0 : S - LATE_Y])
-
-        z_bf = reused.tile([P, U, PACK], BF16, name="z_bf", align_bytes=64, offset=room_at)
-
-        def round_on_scalar(t, lo, hi):
-            nc.scalar.activation(z_bf[:, lo:hi, t], window[t][:, lo:hi], ACT.Copy)
-
-        round_on_scalar(1, 0, U)
-        encode(2, S - LATE_Y, S, y_2[:, S - LATE_Y : S])
-        round_on_scalar(3, scalar_lo, scalar_hi)
+        for t in range(PACK):
+            encode(t, SHORT, S, y[t, SHORT][:], False)
+        for t in (0, 1):
+            scatter(t, y[t, SHORT][:], SHORT, S, t == 0)
+            for h in range(3):
+                stage_by_dma(t, h)
+        for t in (2, 3):
+            scatter(t, y[t, SHORT][:], SHORT, S, t == 2)
 
         w2_s = sb.tile([P, N], U8, name="w2_s", align_bytes=64)
+        w2_q = [
+            reused.tile([P, N // 2], U32, name="w2_q0", align_bytes=64, offset=b1_at),
+            reused.tile([P, N // 2], U32, name="w2_q1", align_bytes=64, offset=staged_at[0]),
+        ]
 
-        scatter(0, y_0, 0, S)
-        scatter(2, y_2, 0, S)
-        round_on_scalar(0, 0, scalar_lo)
-
-        w2_q = reused.tile([P, N], U32, name="w2_q", align_bytes=64, offset=b2_at - 4 * N)
-
-        def quantise_w2(first, last):
+        def quantise_w2(g):
             nc.vector.quantize_mx(
-                out=w2_q[:, first * P : (last + 1) * P].bitcast(FP8X4),
-                scales=w2_s[:, first * P : (last + 1) * P],
-                in_=w2_bf[first // 2][:, first % 2 * P * PACK : (last % 2 + 1) * P * PACK],
+                out=w2_q[g][:].bitcast(FP8X4), scales=w2_s[:, g * N // 2 : (g + 1) * N // 2], in_=w2_bf[g][:]
             )
 
-        quantise_w2(0, 1)
+        quantise_w2(0)
 
-        round_on_scalar(0, scalar_lo, U)
-        for c in SCALAR_CHUNKS:
-            round_on_scalar(2, c * CHUNK, (c + 1) * CHUNK)
+        for t in (3, 2):
+            stage_by_dma(t, 2)
+        for h in range(2):
+            lo, hi = STAGES[h]
+            nc.vector.tensor_copy(staged[h][:, 2, :], window[2][:, lo:hi])
+            nc.scalar.copy(staged[h][:, 3, :], window[3][:, lo:hi])
 
-        pair = window[2][:].rearrange("p (e w) -> p w e", e=2)
-        nc.scalar.copy(z_bf[:, U - CHUNK : U, 2:4], pair[:, U - CHUNK : U, :])
-
-        def round_pair_on_vector(c):
-            cols = slice(c * CHUNK, (c + 1) * CHUNK)
-            nc.vector.tensor_copy(z_bf[:, cols, 2:4], pair[:, cols, :])
-
+        z_bf = sb.tile([P, U, PACK], BF16, name="z_bf", align_bytes=64)
         z_q = sb.tile([P, U], U32, name="z_q", align_bytes=64)
         z_s = sb.tile([P, U], U8, name="z_s", align_bytes=64)
 
-        def quantise_z(c):
-            cols = slice(c * CHUNK, (c + 1) * CHUNK)
+        def round_z(lo, hi, on_vector):
+            h = max(n for n in range(3) if STAGES[n][0] <= lo)
+            first = STAGES[h][0]
+            src = staged[h][:, :, lo - first : hi - first].rearrange("p t (c i) -> p c t i", i=4)
+            dst = z_bf[:, lo:hi, :].rearrange("p (c i) t -> p c t i", i=4)
+            if on_vector:
+                nc.vector.tensor_copy(dst, src)
+            else:
+                nc.scalar.copy(dst, src)
+
+        def quantise_z(lo, hi):
             nc.vector.quantize_mx(
-                out=z_q[:, cols].bitcast(FP8X4), scales=z_s[:, cols], in_=z_bf[:, cols, :].rearrange("p w t -> p (w t)")
+                out=z_q[:, lo:hi].bitcast(FP8X4),
+                scales=z_s[:, lo:hi],
+                in_=z_bf[:, lo:hi, :].rearrange("p w t -> p (w t)"),
             )
 
-        round_pair_on_vector(0)
-        round_pair_on_vector(1)
-        quantise_w2(2, 2)
-        for c in (0, 1, 2, 3):
-            quantise_z(c)
-        round_pair_on_vector(4)
-        for c in (5, 6):
-            round_pair_on_vector(c)
-            quantise_z(c - 1)
-        quantise_z(CHUNKS - 1)
-        quantise_z(CHUNKS - 2)
-        quantise_w2(3, 3)
+        round_z(0, 128, True)
+        round_z(128, 256, True)
+        quantise_z(0, 128)
+        round_z(256, 384, True)
+        round_z(384, 512, False)
+        round_z(512, 640, False)
+        quantise_z(128, 256)
+        quantise_w2(1)
+        quantise_z(256, 512)
+        round_z(640, 768, True)
+        round_z(768, U, True)
+        quantise_z(512, 768)
+        quantise_z(768, U)
 
         out_planes = out.rearrange("(g p e) w -> p g e w", g=2, e=2)
 
@@ -232,7 +253,7 @@ def tile_picked_sae8_relu_p_kernel(
             for a, b in zip(cuts[:-1], cuts[1:]):
                 nc.tensor.matmul_mx(
                     out=acc[:, a - lo : b - lo],
-                    lhsT=w2_q[:, t * P : (t + 1) * P].bitcast(FP8X4),
+                    lhsT=w2_q[t // 2][:, t % 2 * P : (t % 2 + 1) * P].bitcast(FP8X4),
                     lhsT_scale=w2_s[:, t * P : (t + 1) * P],
                     rhs=z_q[:, a:b].bitcast(FP8X4),
                     rhs_scale=z_s[:, a:b],
@@ -254,21 +275,17 @@ def tile_picked_sae8_relu_p_kernel(
             nc.sync.dma_start(out_planes[:, t // 2, t % 2, first:end], res[t, first][:])
 
         part(0, 0, (0, 128), False)
-        for t, n, cuts in ((0, 0, (128, 256)), (1, 0, (0, 256)), (0, 1, (256, 384, 512)), (1, 1, (256, 512))):
+        for t, n, cuts in ((0, 0, (128, 256)), (1, 0, (0, 256))):
             part(t, n, cuts, False)
             store(t, n)
         part(2, 0, (0, 256), False)
-        part(2, 0, (256, 512), True)
+        for t in (0, 1):
+            part(t, 1, (256, 512), False)
+            store(t, 1)
+        part(2, 0, (256, 512), False)
         store(2, 0)
-        part(0, 2, (512, 640, 768), False)
-        part(0, 2, (896, U), True)
-        part(0, 2, (768, 896), True)
-        store(0, 2)
-        part(1, 2, (512, U), False)
-        store(1, 2)
-        part(2, 1, (512, U), True)
-        store(2, 1)
-        part(3, 0, (0, 512), False, 4)
-        part(3, 0, (512, 768), True, 4)
-        part(3, 0, (768, U), False)
+        part(3, 0, (0, 512), False)
         store(3, 0)
+        for t, n in ((0, 2), (1, 2), (2, 1), (3, 1)):
+            part(t, n, (512, 768, U), t % 2 == 0)
+            store(t, n)

@@ -27,7 +27,7 @@ W1_ON_VECTOR = 80
 CHUNK = 128
 CHUNKS = U // CHUNK
 EARLY = 768
-STORE_CUTS = ((0, 256, 512, U), (0, 256, 512, U), (0, 512, U), (0, 512, U))
+STORE_CUTS = ((0, 256, 512, U), (0, 256, U), (0, 512, U), (0, 512, U))
 DMA_ALIGN = 256
 
 
@@ -156,13 +156,14 @@ def tile_picked_sae8_relu_p_kernel(
 
         y = {
             (t, lo): sb.tile([P, hi - lo], F32, name="y%d_%d" % (t, lo))
-            for t in range(PACK)
+            for t in range(3)
             for lo, hi in ((0, SHORT), (SHORT, S))
         }
+        y_3 = sb.tile([P, S], F32, name="y_3")
 
-        for t in range(PACK):
+        for t in range(3):
             encode(t, 0, SHORT, y[t, 0][:], t == 1)
-        for t in range(PACK):
+        for t in range(3):
             scatter(t, y[t, 0][:], 0, SHORT, t != 1)
         w2_bf = [sb.tile([P, 2 * N], BF16, name="w2_bf%d" % g, align_bytes=64) for g in range(2)]
         for g, e in ((0, 0), (0, 1), (1, 0), (1, 1)):
@@ -175,19 +176,22 @@ def tile_picked_sae8_relu_p_kernel(
                 ALU.add,
             )
 
-        for t in range(PACK):
+        encode(0, SHORT, S, y[0, SHORT][:], False)
+        encode(3, 0, S, y_3[:], False)
+        for t in (1, 2):
             encode(t, SHORT, S, y[t, SHORT][:], False)
         for t in (0, 1):
             scatter(t, y[t, SHORT][:], SHORT, S, t == 0)
             for h in range(3):
                 stage_by_dma(t, h)
-        for t in (2, 3):
-            scatter(t, y[t, SHORT][:], SHORT, S, t == 2)
+        scatter(3, y_3[:, 0:SHORT], 0, SHORT, True)
+        scatter(2, y[2, SHORT][:], SHORT, S, True)
+        scatter(3, y_3[:, SHORT:S], SHORT, S, False)
 
         w2_s = sb.tile([P, N], U8, name="w2_s", align_bytes=64)
         w2_q = [
             reused.tile([P, N // 2], U32, name="w2_q0", align_bytes=64, offset=b1_at),
-            reused.tile([P, N // 2], U32, name="w2_q1", align_bytes=64, offset=staged_at[0]),
+            sb.tile([P, N // 2], U32, name="w2_q1", align_bytes=64),
         ]
 
         def quantise_w2(g):
@@ -202,7 +206,9 @@ def tile_picked_sae8_relu_p_kernel(
         for h in range(2):
             lo, hi = STAGES[h]
             nc.vector.tensor_copy(staged[h][:, 2, :], window[2][:, lo:hi])
-            nc.scalar.copy(staged[h][:, 3, :], window[3][:, lo:hi])
+            for a, b in ((0, 128), (128, 256)) if h == 0 else ((0, hi - lo),):
+                nc.scalar.copy(staged[h][:, 3, a:b], window[3][:, lo + a : lo + b])
+        quantise_w2(1)
 
         z_bf = sb.tile([P, U, PACK], BF16, name="z_bf", align_bytes=64)
         z_q = sb.tile([P, U], U32, name="z_q", align_bytes=64)
@@ -228,11 +234,10 @@ def tile_picked_sae8_relu_p_kernel(
         round_z(0, 128, True)
         round_z(128, 256, True)
         quantise_z(0, 128)
+        quantise_z(128, 256)
         round_z(256, 384, True)
         round_z(384, 512, False)
-        round_z(512, 640, False)
-        quantise_z(128, 256)
-        quantise_w2(1)
+        round_z(512, 640, True)
         quantise_z(256, 512)
         round_z(640, 768, True)
         round_z(768, U, True)
@@ -279,13 +284,18 @@ def tile_picked_sae8_relu_p_kernel(
             part(t, n, cuts, False)
             store(t, n)
         part(2, 0, (0, 256), False)
-        for t in (0, 1):
-            part(t, 1, (256, 512), False)
-            store(t, 1)
         part(2, 0, (256, 512), False)
         store(2, 0)
-        part(3, 0, (0, 512), False)
+        part(3, 0, (0, 256, 512), False)
         store(3, 0)
-        for t, n in ((0, 2), (1, 2), (2, 1), (3, 1)):
-            part(t, n, (512, 768, U), t % 2 == 0)
-            store(t, n)
+        part(0, 1, (256, 512), False)
+        store(0, 1)
+        part(0, 2, (512, 768), False)
+        part(0, 2, (768, U), True)
+        store(0, 2)
+        part(1, 1, (256, 512, 768), False)
+        part(1, 1, (768, U), True)
+        store(1, 1)
+        for t in (2, 3):
+            part(t, 1, (512, 768, U), t == 2)
+            store(t, 1)

@@ -201,9 +201,7 @@ def tile_picked_sae8_relu_p_kernel(
 
         quantise_w2(0)
 
-        for t in (3, 2):
-            stage_by_dma(t, 2)
-        for h in range(2):
+        for h in range(3):
             lo, hi = STAGES[h]
             nc.vector.tensor_copy(staged[h][:, 2, :], window[2][:, lo:hi])
             for a, b in ((0, 128), (128, 256)) if h == 0 else ((0, hi - lo),):
@@ -297,5 +295,5 @@ def tile_picked_sae8_relu_p_kernel(
         part(1, 1, (768, U), True)
         store(1, 1)
         for t in (2, 3):
-            part(t, 1, (512, 768, U), t == 2)
+            part(t, 1, (512, U), t == 2)
             store(t, 1)

@@ -27,7 +27,7 @@ W1_ON_VECTOR = 80
 CHUNK = 128
 CHUNKS = U // CHUNK
 EARLY = 768
-STORE_CUTS = ((0, 256, 512, U), (0, 256, U), (0, 512, U), (0, 512, U))
+STORE_CUTS = ((0, 256, 512, U), (0, 256, 512, U), (0, 512, U), (0, 512, U))
 DMA_ALIGN = 256
 
 
@@ -286,14 +286,12 @@ def tile_picked_sae8_relu_p_kernel(
         store(2, 0)
         part(3, 0, (0, 256, 512), False)
         store(3, 0)
-        part(0, 1, (256, 512), False)
-        store(0, 1)
+        for t in (0, 1):
+            part(t, 1, (256, 512), False)
+            store(t, 1)
         part(0, 2, (512, 768), False)
         part(0, 2, (768, U), True)
         store(0, 2)
-        part(1, 1, (256, 512, 768), False)
-        part(1, 1, (768, U), True)
-        store(1, 1)
-        for t in (2, 3):
-            part(t, 1, (512, U), t == 2)
-            store(t, 1)
+        for t, n in ((1, 2), (2, 1), (3, 1)):
+            part(t, n, (512, U), t != 2)
+            store(t, n)

from contextlib import ExitStack

import concourse.mybir as mybir

K, T, S, N, U, H = 512, 2048, 512, 512, 1024, 512
FLOPS = 2 * K * H * S + 2 * H * N * U

F32 = mybir.dt.float32
BF16 = mybir.dt.bfloat16
I32 = mybir.dt.int32
U32 = mybir.dt.uint32
U16 = mybir.dt.uint16
U8 = mybir.dt.uint8
FP8X4 = mybir.dt.float8_e4m3fn_x4
ACT = mybir.ActivationFunctionType
ALU = mybir.AluOpType

P = 128
QUADRANT = 32
PACK = 4
LIST_ROWS = 16
SCALE_ROWS = K // 32
BANK = 512
BANKS = 8
SHORT = 128
W1_ON_VECTOR = 80
CHUNK = 128
CHUNKS = U // CHUNK
EARLY = 768
STORE_CUTS = ((0, 256, 512, U), (0, 256, 512, U), (0, 512, U), (0, 512, U))
DMA_ALIGN = 256


def pass_cuts(lo, hi):
    cuts = [lo]
    while cuts[-1] < hi:
        cuts.append(cuts[-1] + max(n for n in (512, 256, 128, 64) if n <= hi - cuts[-1]))
    return cuts


def tile_picked_sae8_relu_p_kernel(
    tc, x_words, x_scales, w1, b1, w2, b2, offs, held, out
):
    nc = tc.nc
    with ExitStack() as ctx:
        lists = ctx.enter_context(tc.tile_pool(name="lists", bufs=1))
        sb = ctx.enter_context(tc.tile_pool(name="sb", bufs=1))
        reused = ctx.enter_context(tc.tile_pool(name="reused", bufs=1))
        psum = ctx.enter_context(tc.psum_pool(name="psum", bufs=1))
        taken = []

        def next_bank(behind=BANKS):
            taken.append(len(taken) % BANKS)
            return psum.tile([P, BANK], F32, name="bank%d" % taken[-1])

        offs_t = lists.tile([P, S // LIST_ROWS], U16, name="offs_t")
        held_t = lists.tile([P, S // LIST_ROWS], U16, name="held_t")

        def entries(list_t, lo, hi):
            return list_t[:, lo // LIST_ROWS : hi // LIST_ROWS]

        w2_half_bytes = 4 * PACK * N // 2
        staged_at = (3 * w2_half_bytes, 4 * w2_half_bytes, 6 * w2_half_bytes)
        b2_at = w2_half_bytes
        b1_at = b2_at + 64
        first_at = b2_at + 5 * DMA_ALIGN

        window = [sb.tile([P, U], F32, name="window%d" % t, align_bytes=DMA_ALIGN) for t in range(PACK)]
        nc.vector.memset(window[0][:], 0.0)
        for t in (1, 3):
            nc.scalar.copy(window[t][:], window[0][:])

        first_row = P - SCALE_ROWS
        xs = reused.tile([P, T], U8, name="xs", align_bytes=DMA_ALIGN, offset=b2_at - 2 * DMA_ALIGN)
        for lo, hi in ((0, P - QUADRANT), (P - QUADRANT, first_row)):
            nc.vector.memset(xs[lo:hi, :].bitcast(I32), 0)
        xs_moved = sb.tile([P, S], U8, name="xs_moved", align_bytes=64)
        nc.vector.memset(xs_moved[:].bitcast(I32), 0)

        w2_first = reused.tile([P, PACK * N // 2], F32, name="w2_first", align_bytes=DMA_ALIGN, offset=first_at)
        w2_room = reused.tile([P, U], F32, name="w2_room", align_bytes=DMA_ALIGN, offset=0)
        w2_raw = [half.rearrange("p (j c) -> p j c", j=PACK) for half in (w2_first[:], w2_room[:])]

        w1_raw = sb.tile([P, PACK, H], F32, name="w1_raw", align_bytes=DMA_ALIGN)
        xw = sb.tile([P, T], I32, name="xw", align_bytes=DMA_ALIGN)
        b1_t = reused.tile([P, PACK], F32, name="b1_t", align_bytes=64, offset=b1_at)
        b2_t = reused.tile([P, 2, 2], F32, name="b2_t", align_bytes=64, offset=b2_at)

        nc.scalar.dma_start(xs[first_row:P, :].bitcast(I32), x_scales[0].bitcast(I32))
        nc.sync.dma_start(offs_t[:], offs)
        nc.sync.dma_start(w1_raw[:], w1.rearrange("(p j) c -> p j c", j=PACK))
        nc.sync.dma_start(xw[:], x_words[0].rearrange("p n r -> p (n r)").bitcast(I32))
        xs_picked = sb.tile([P, S], U8, name="xs_picked", align_bytes=64)
        nc.vector.tensor_copy(xs_picked[:], xs[:].indirect(offs_t[:]))
        for i in range(4):
            nc.sync.dma_start(xs_moved[i:P:QUADRANT, :].bitcast(I32), xs_picked[first_row + i : P : 4, :].bitcast(I32))
        nc.sync.dma_start(b1_t[:], b1.rearrange("(p t) o -> p (t o)", t=PACK))
        nc.sync.dma_start(held_t[:], held)
        w2_rows = w2.rearrange("(p j) c -> p j c", j=PACK)
        for g in range(2):
            nc.sync.dma_start(w2_raw[g], w2_rows[:, :, g * N // 2 : (g + 1) * N // 2])
        nc.sync.dma_start(b2_t[:], b2.rearrange("(g p e) o -> p g (e o)", g=2, e=2))

        nc.vector.memset(window[2][:], 0.0)

        w1_bf = sb.tile([P, PACK * H], BF16, name="w1_bf", align_bytes=64)
        w1_rows = w1_raw[:].rearrange("p j (m t) -> p m j t", t=PACK)
        w1_dealt = w1_bf[:].rearrange("p (t m j) -> p m j t", t=PACK, j=PACK)
        nc.vector.tensor_copy(w1_dealt[:, 0:W1_ON_VECTOR], w1_rows[:, 0:W1_ON_VECTOR])
        nc.scalar.copy(w1_dealt[:, W1_ON_VECTOR:P], w1_rows[:, W1_ON_VECTOR:P])
        w1_q = sb.tile([P, H], U32, name="w1_q", align_bytes=64)
        w1_s = sb.tile([P, H], U8, name="w1_s", align_bytes=64)
        nc.vector.quantize_mx(out=w1_q[:].bitcast(FP8X4), scales=w1_s[:], in_=w1_bf[:])

        xw_picked = sb.tile([P, S], U32, name="xw_picked", align_bytes=64)
        for lo, hi in ((0, SHORT), (SHORT, S)):
            nc.vector.tensor_copy(xw_picked[:, lo:hi], xw[:].bitcast(U32).indirect(entries(offs_t, lo, hi)))

        def encode(t, lo, hi, y, on_vector):
            acc = next_bank()
            cols = slice(t * P, (t + 1) * P)
            cuts = pass_cuts(lo, hi)
            for a, b in zip(cuts[:-1], cuts[1:]):
                nc.tensor.matmul_mx(
                    out=acc[:, a - lo : b - lo],
                    lhsT=w1_q[:, cols].bitcast(FP8X4),
                    lhsT_scale=w1_s[:, cols],
                    rhs=xw_picked[:, a:b].bitcast(FP8X4),
                    rhs_scale=xs_moved[:, a:b],
                    start=True,
                    stop=True,
                )
            bias = b1_t[:, t : t + 1]
            if on_vector:
                nc.vector.tensor_scalar(y, acc[:, 0 : hi - lo], bias, 0.0, ALU.add, ALU.max)
            else:
                nc.scalar.activation(y, acc[:, 0 : hi - lo], ACT.Relu, bias=bias)

        def scatter(t, y, lo, hi, on_vector):
            target = window[t][:].indirect(entries(held_t, lo, hi))
            if on_vector:
                nc.vector.tensor_copy(target, y)
            else:
                nc.scalar.activation(target, y, ACT.Copy)

        STAGES = ((0, 256), (256, EARLY), (EARLY, U))
        staged = [
            reused.tile(
                [P, PACK, hi - lo], F32, name="staged%d" % lo, align_bytes=DMA_ALIGN, offset=at
            )
            for (lo, hi), at in zip(STAGES, staged_at)
        ]

        def stage_by_dma(t, h):
            nc.sync.dma_start(staged[h][:, t, :], window[t][:, STAGES[h][0] : STAGES[h][1]])

        y = {
            (t, lo): sb.tile([P, hi - lo], F32, name="y%d_%d" % (t, lo))
            for t in range(3)
            for lo, hi in ((0, SHORT), (SHORT, S))
        }
        y_3 = sb.tile([P, S], F32, name="y_3")

        for t in range(3):
            encode(t, 0, SHORT, y[t, 0][:], t == 1)
        for t in range(3):
            scatter(t, y[t, 0][:], 0, SHORT, t != 1)
        w2_bf = [sb.tile([P, 2 * N], BF16, name="w2_bf%d" % g, align_bytes=64) for g in range(2)]
        for g, e in ((0, 0), (0, 1), (1, 0), (1, 1)):
            nc.gpsimd.tensor_scalar(
                w2_bf[g][:].rearrange("p (e n j) -> p e n j", e=2, j=PACK)[:, e],
                w2_raw[g].rearrange("p j (n e) -> p e n j", e=2)[:, e],
                1.0,
                0.0,
                ALU.mult,
                ALU.add,
            )

        encode(0, SHORT, S, y[0, SHORT][:], False)
        encode(3, 0, S, y_3[:], False)
        for t in (1, 2):
            encode(t, SHORT, S, y[t, SHORT][:], False)
        for t in (0, 1):
            scatter(t, y[t, SHORT][:], SHORT, S, t == 0)
            for h in range(3):
                stage_by_dma(t, h)
        scatter(3, y_3[:, 0:SHORT], 0, SHORT, True)
        scatter(2, y[2, SHORT][:], SHORT, S, True)
        scatter(3, y_3[:, SHORT:S], SHORT, S, False)

        w2_s = sb.tile([P, N], U8, name="w2_s", align_bytes=64)
        w2_q = [
            reused.tile([P, N // 2], U32, name="w2_q0", align_bytes=64, offset=b1_at),
            sb.tile([P, N // 2], U32, name="w2_q1", align_bytes=64),
        ]

        def quantise_w2(g):
            nc.vector.quantize_mx(
                out=w2_q[g][:].bitcast(FP8X4), scales=w2_s[:, g * N // 2 : (g + 1) * N // 2], in_=w2_bf[g][:]
            )

        quantise_w2(0)

        for h in range(3):
            lo, hi = STAGES[h]
            nc.vector.tensor_copy(staged[h][:, 2, :], window[2][:, lo:hi])
            for a, b in ((0, 128), (128, 256)) if h == 0 else ((0, hi - lo),):
                nc.scalar.copy(staged[h][:, 3, a:b], window[3][:, lo + a : lo + b])
        quantise_w2(1)

        z_bf = sb.tile([P, U, PACK], BF16, name="z_bf", align_bytes=64)
        z_q = sb.tile([P, U], U32, name="z_q", align_bytes=64)
        z_s = sb.tile([P, U], U8, name="z_s", align_bytes=64)

        def round_z(lo, hi, on_vector):
            h = max(n for n in range(3) if STAGES[n][0] <= lo)
            first = STAGES[h][0]
            src = staged[h][:, :, lo - first : hi - first].rearrange("p t (c i) -> p c t i", i=4)
            dst = z_bf[:, lo:hi, :].rearrange("p (c i) t -> p c t i", i=4)
            if on_vector:
                nc.vector.tensor_copy(dst, src)
            else:
                nc.scalar.copy(dst, src)

        def quantise_z(lo, hi):
            nc.vector.quantize_mx(
                out=z_q[:, lo:hi].bitcast(FP8X4),
                scales=z_s[:, lo:hi],
                in_=z_bf[:, lo:hi, :].rearrange("p w t -> p (w t)"),
            )

        round_z(0, 128, True)
        round_z(128, 256, True)
        quantise_z(0, 128)
        quantise_z(128, 256)
        round_z(256, 384, True)
        round_z(384, 512, False)
        round_z(512, 640, True)
        quantise_z(256, 512)
        round_z(640, 768, True)
        round_z(768, U, True)
        quantise_z(512, 768)
        quantise_z(768, U)

        out_planes = out.rearrange("(g p e) w -> p g e w", g=2, e=2)

        res = {
            (t, lo): sb.tile([P, hi - lo], F32, name="res%d_%d" % (t, lo), align_bytes=DMA_ALIGN)
            for t in range(PACK)
            for lo, hi in zip(STORE_CUTS[t][:-1], STORE_CUTS[t][1:])
        }

        def decode(t, cuts, into, on_vector, behind):
            acc = next_bank(behind)
            lo, hi = cuts[0], cuts[-1]
            for a, b in zip(cuts[:-1], cuts[1:]):
                nc.tensor.matmul_mx(
                    out=acc[:, a - lo : b - lo],
                    lhsT=w2_q[t // 2][:, t % 2 * P : (t % 2 + 1) * P].bitcast(FP8X4),
                    lhsT_scale=w2_s[:, t * P : (t + 1) * P],
                    rhs=z_q[:, a:b].bitcast(FP8X4),
                    rhs_scale=z_s[:, a:b],
                    start=True,
                    stop=True,
                )
            bias = b2_t[:, t // 2, t % 2 : t % 2 + 1]
            if on_vector:
                nc.vector.tensor_scalar_add(into, acc[:, 0 : hi - lo], bias)
            else:
                nc.scalar.activation(into, acc[:, 0 : hi - lo], ACT.Identity, bias=bias)

        def part(t, n, cuts, on_vector, behind=BANKS):
            first = STORE_CUTS[t][n]
            decode(t, cuts, res[t, first][:, cuts[0] - first : cuts[-1] - first], on_vector, behind)

        def store(t, n):
            first, end = STORE_CUTS[t][n], STORE_CUTS[t][n + 1]
            nc.sync.dma_start(out_planes[:, t // 2, t % 2, first:end], res[t, first][:])

        part(0, 0, (0, 128), False)
        for t, n, cuts in ((0, 0, (128, 256)), (1, 0, (0, 256))):
            part(t, n, cuts, False)
            store(t, n)
        part(2, 0, (0, 256), False)
        part(2, 0, (256, 512), False)
        store(2, 0)
        part(3, 0, (0, 256, 512), False)
        store(3, 0)
        for t in (0, 1):
            part(t, 1, (256, 512), False)
            store(t, 1)
        part(0, 2, (512, 768), False)
        part(0, 2, (768, U), True)
        store(0, 2)
        for t, n in ((1, 2), (2, 1), (3, 1)):
            part(t, n, (512, U), t != 2)
            store(t, n)
